import numpy as np, ml_dtypes
CORES = [3,11,19,27,35,43,51,59]
N = 8
import mx_ref
BF = ml_dtypes.bfloat16
def gentries(a):
    return np.ascontiguousarray(a.reshape(8, 16, -1).transpose(0, 2, 1)).reshape(8, -1)
def gtable(e):
    e = np.asarray(e); return np.ascontiguousarray(e.reshape(8, -1, 16).transpose(0, 2, 1)).reshape(128, -1).astype(np.int32)
def gcols(t, e):
    v = np.concatenate([t.reshape(8, 16, -1, 4), np.zeros((8, 16, 1, 4), BF)], axis=2)
    return np.ascontiguousarray(np.stack([v[g][:, e[g]] for g in range(8)])).reshape(128, -1)
def tile(rs):
    return np.stack(rs, axis=2).reshape(128, -1).astype(BF)
def pick(q, e):
    c = np.concatenate([q[0].reshape(128, -1, 4), np.zeros((128, 1, 4), np.uint8)], axis=1); s = np.concatenate([q[1], np.ones((16, 1), np.uint8)], axis=1)
    return (np.ascontiguousarray(c[:, e].reshape(128, -1)), np.ascontiguousarray(s[:, e]))
def join(*qs):
    return (np.concatenate([q[0] for q in qs], axis=1), np.concatenate([q[1] for q in qs], axis=1))
def put(q, e, v):
    c, s = q[0].reshape(128, -1, 4).copy(), q[1].copy(); c[:, e] = v[0].reshape(128, -1, 4); s[:, e] = v[1]
    return (c.reshape(128, -1), s)
def pk(c, s):
    return (np.ascontiguousarray(c), mx_ref.live(s))
def emit(q):
    return q[0], q[1]
def packed(v, rng):
    q = [mx_ref.quantize(np.ascontiguousarray(v[r])) for r in range(N)]
    return np.stack([a for a, b in q]), np.stack([mx_ref.plane(b, rng) for a, b in q])
def values_of_codes():
    e, c = np.zeros((128, 128, 4), np.float32), np.zeros((128, 2, 4), np.uint8)
    e[np.arange(128), np.arange(128), 0] = 1
    c[:127, :, 0] = np.arange(256).reshape(2, 128).T[:127]
    return mx_ref.matmul(mx_ref.quantize(e.reshape(128, 512).astype(BF)), (c.reshape(128, 8), np.full((16, 2), 127, np.uint8))).T.reshape(-1).astype(np.float64)
CODE_VALUE, SCALE_VALUE = values_of_codes(), 2.0 ** (np.arange(256) - 127.0)
def decode(q):
    return (CODE_VALUE[q[0]].reshape(16, 8, -1, 4) * SCALE_VALUE[q[1]][:, None, :, None] + 0.0).reshape(128, -1).astype(np.float32)
def f(rng, *shape):
    return mx_ref.flush((rng.standard_normal(shape, dtype=np.float32) * np.exp2(rng.integers(-2, 3, shape[:-1] + (1,)))).astype(BF))
def wide(rng, *shape, cols=0):
    v = rng.standard_normal(shape, dtype=np.float32) * np.exp2(rng.integers(-12, 13, shape)).astype(np.float32)
    if cols: v *= np.repeat(np.exp2(rng.integers(-cols, cols + 1, shape[:-2] + (1, shape[-1] // 4))) * (rng.random(shape[:-2] + (1, shape[-1] // 4)) > 0.0625), 4, axis=-1).astype(np.float32)
    return mx_ref.flush(v.astype(BF))
C = 320
STEP = [1, 2, 4]
def numbers_of(rng):
    return {"x": np.array(f(rng, N, 128, 4 * C)), "u": np.array(f(rng, N, 128, 512)), "v": np.array(f(rng, N, 128, 512))}
def stored(h, t):
    return {"hl": np.stack([gtable(h[r]) for r in range(N)]), "tl": np.stack([gtable(t[r]) for r in range(N)])}
def lists(rng):
    e = np.tile(np.arange(C), (N, 8, 1))
    return stored(rng.permuted(e, axis=2), rng.permuted(e, axis=2))
def layers(rng, still=()):
    w = np.array(f(rng, N, 128, 2048)).reshape(N, 8, 16, 4, 8, 16, 4)
    for i in still:
        w[:, :, i] = 0
        w[:, :, :, :, :, i] = 0
    return w
def weights(rng, w):
    c, s = packed(np.ascontiguousarray(w).reshape(N, 128, 2048), rng)
    return {"wc": c, "ws": s}
def setup_inputs(rng):
    return {**numbers_of(rng), **lists(rng), **weights(rng, layers(rng))}
def setup_inputs_ties(rng):
    d = numbers_of(rng)
    o = rng.permutation(N)
    k = rng.integers(0, 4, (N, 2, 8, C))
    k[o[1]] += 1
    for g in rng.permutation(8)[:4]: k[o[2], :, g] = 1
    x = d["x"].reshape(N, 8, 16, C, 4)
    u = d["u"].reshape(N, 128, 128, 4)
    for i in range(2):
        x[:, :, i] = 0
        x[:, :, i, :, 0] = k[:, i].astype(np.float32).astype(BF)
        u[:, :, i::16] = 0
        for r in range(N):
            for h in range(i, 128, 16): u[r, h, h, 0] = 0.0 if r == o[0] else -1.0 if r == o[1] else 1.0
    a = np.exp2(rng.integers(-3, 4, (8, 1)).astype(np.float32))
    x[:, :, 8:] = 0
    x[:, :, 8, :, 0] = (-1.125 * a).astype(BF)
    x[:, :, 10, :, 0] = (-0.0703125 * a).astype(BF)
    w = layers(rng, [0, 1])
    w[:, :, :, :, :, 8:] = 0
    for g in range(8):
        w[:, g, 8, 0, g, 8, 0] = -28.0
        for b in range(4): w[:, g, 10, b, g, 9, 0] = -2.0 ** (b - 5)
    return {"x": x.reshape(N, 128, 4 * C), "u": u.reshape(N, 128, 512), "v": d["v"], **lists(rng), **weights(rng, w)}
def setup_inputs_near(rng):
    d = numbers_of(rng)
    x = d["x"].astype(np.float32).reshape(N, 8, 16, C, 4)
    x[:, :, 0] = 0
    x[:, :, 8:] = 0
    u = d["u"].reshape(N, 128, 128, 4)
    for i in range(2): u[:, :, i::16] = 0
    w = layers(rng, [0, 8, 9, 10, 11, 12, 13, 14, 15])
    o = rng.permutation(N) % 4
    for r in range(N):
        c = rng.choice([-1.0, 1.0], (8, 1))
        k = 1.0 if o[r] == 0 else 2.0 ** -30
        if o[r] < 2:
            x[r, :, 0, :, 0] = c
            x[r, :, 11, :, 0] = 2.0 ** -10
        x[r, :, 13, :, 0] = rng.integers(0, 2, (8, C)) * (2.0 ** -20 if o[r] < 2 else 2.0 ** -30)
        x[r, :, 15, :, 0] = 2.0 ** -20 if o[r] < 2 else 2.0 ** -29
        for g in range(8):
            w[r, g, 13, 0, g, 12, 0] = 2.0 ** -18 if o[r] < 2 else 2.0 ** -8
            if o[r] < 2: w[r, g, 14, 0, g, 12, 0] = 2.0 ** -6
            w[r, g, 15, 0, g, 15, 0] = 2.0 ** -5 if o[r] < 2 else 16.0
        for i in range(2):
            s = rng.integers(0, 16, (8, C))
            digits = ((s[:, :, None] >> np.arange(4)) & 1) * np.exp2(np.arange(4) - 23.0)
            if o[r] < 2: x[r, :, 8 + i] = digits
            elif o[r] == 2: x[r, :, 8 + i] = digits * rng.choice([-1.0, 1.0], (8, C, 1))
            else:
                x[r, :, 8 + 2 * i, :, 0] = np.where(s < 8, 1.25, 0.0) * 2.0 ** -30 * c
                x[r, :, 9 + 2 * i, :, 0] = np.where(s < 8, 0.0, 1.125) * 2.0 ** -30 * c
                for g in rng.permutation(8)[:4]:
                    e = rng.choice([-1.0, 1.0], C) * 2.0 ** -30
                    x[r, g, 8 + 2 * i, :, 0] = 1.25 * e
                    x[r, g, 9 + 2 * i, :, 0] = -1.125 * e
            for p in range(0, 128, 16):
                u[r, p, p + i, 0] = k if o[r] < 2 else 1.0
                u[r, p + 12, p + i, 0] = k
                if o[r] < 2: u[r, p + 11, p + i, 0] = k
                if o[r] < 3: u[r, p + 8 + i, p + i] = k
                else:
                    u[r, p + 8 + 2 * i, p + i, 0] = k
                    u[r, p + 9 + 2 * i, p + i, 0] = 1.125 * k
        at = [0, C - 1, int(rng.integers(C)), int(rng.integers(C))]
        for g, j in zip(rng.permutation(8)[:4], at): x[r, g, 0, j, 0] = 2.0 ** 29 * rng.choice([-1.0, 1.0])
    return {"x": x.reshape(N, 128, 4 * C).astype(BF), "u": u.reshape(N, 128, 512), "v": d["v"], **lists(rng), **weights(rng, w)}
def setup_inputs_odd(rng):
    d = numbers_of(rng)
    x = (1.0 + (2 * rng.integers(0, 64, (N, 16, 8, C, 4)) + 1) * 2.0 ** -7) * np.exp2(-rng.integers(0, 7, (N, 16, 8, C, 4)).astype(np.float64)) * rng.choice([-1.0, 1.0], (N, 16, 8, C, 4))
    x[:, :, 0, :, 0] = 1.96875 * 2.0 ** 8 * rng.choice([-1.0, 1.0], (N, 16, 1))
    u = d["u"].reshape(N, 128, 128, 4)
    for i in range(2):
        x[:, ::2, 1 + i, :, 0] = (8 + rng.integers(0, 2, (N, 8, C))) * 2.0 ** -8
        u[:, :, i::16] = 0
        for h in range(i, 128, 16): u[:, h + 1, h, 0] = 1.0
    return {"x": x.astype(np.float32).reshape(N, 128, 4 * C).astype(BF), "u": u.reshape(N, 128, 512), "v": d["v"], **lists(rng), **weights(rng, layers(rng, [0, 8]))}
def setup_inputs_ends(rng):
    d = numbers_of(rng)
    x = np.zeros((N, 8, 16, C, 4))
    u = d["u"].astype(np.float32).reshape(N, 128, 128, 4)
    v = d["v"].astype(np.float32)
    w = np.zeros((N, 128, 4, 128, 4), np.float32)
    hh, tt = np.zeros((N, 8, C), np.int64), np.zeros((N, 8, C), np.int64)
    o, e = rng.permutation(N) % 4, rng.permutation(N) % 4
    i, a = np.arange(128), np.arange(C)
    for r in range(N):
        low = -(0.8 + 0.08 * rng.random((8, 16, C, 4))) * 2.0 ** 30
        low[:, 15] = -2.0 ** 30
        tiny = -(1.0 + 0.125 * rng.integers(0, 8, (8, 16, C, 4))) * 2.0 ** -30
        if o[r] == 0: x[r] = low
        if o[r] == 1: x[r] = np.where((rng.random(C) < 0.5)[:, None], -low, low)
        if o[r] == 2: x[r] = tiny
        if o[r] == 3: x[r] = d["x"][r].astype(np.float32).reshape(8, 16, C, 4)[:, :, :1]
        x[r, 0] = tiny[0] * 2.0 ** 20 if o[r] < 2 else tiny[0] if o[r] == 2 else -2.0 ** -30
        for k in range(2):
            h = rng.permutation(8)
            c = np.where(h < 2, 0.0, h % 2 * 2.0 - 1.0)[None, :, None]
            if o[r] < 2: u[r, :, k::16] = c * (0.9 + 0.1 * rng.random((128, 8, 4))) * 2.0 ** 30
            if o[r] == 2: u[r, :, k::16] = c * (1.0 + 0.125 * rng.integers(0, 8, (128, 8, 4))) * 2.0 ** -30
            if o[r] == 3: u[r, :, k::16] *= np.abs(c).astype(np.float32)
        if o[r] < 2: v[r] = rng.choice([-1.0, 1.0], (128, 512)) * (0.9 + 0.1 * rng.random((128, 512))) * 2.0 ** 30
        else: v[r] = rng.choice([-1.0, 1.0], (128, 512)) * (1.0 + 0.125 * rng.integers(0, 8, (128, 512))) * 2.0 ** -30
        k = np.array([0.25, 0.5, 1.0])[rng.permutation(8) % 3] * rng.choice([-1.0, 1.0], 8)
        if o[r] == 2: k[:] = 0.0
        k[0] = 2.0 ** 8 if o[r] > 1 else 2.0 ** -8
        for b in range(4): w[r, i, b, i, b] = np.where((i >= 16) & (i % 16 == 15), 0.0, k[i // 16])
        hh[r] = C - 1 - a if e[r] == 1 else a
        if e[r] == 3: hh[r] = rng.permuted(np.tile(a, (8, 1)), axis=1)
        tt[r] = hh[r] if e[r] < 2 else np.roll(a, 1) if e[r] == 2 else hh[r] ^ 1
    return {"x": x.astype(np.float32).reshape(N, 128, 4 * C).astype(BF), "u": u.reshape(N, 128, 512).astype(BF), "v": v.astype(BF), **stored(hh, tt), **weights(rng, w.astype(BF))}
def setup_inputs_spread(rng):
    d = setup_inputs(rng)
    d["x"] = wide(rng, N, 128, 4 * C, cols=6)
    return d
def check_inputs(d):
    b = []
    for k in ("x", "u", "v"):
        a = np.abs(d[k].astype(np.float32))
        if not (np.isfinite(a).all() and ((a == 0) | (a >= 2.0 ** -30) & (a <= 2.0 ** 30)).all()): b.append("a value of " + k)
    for k in ("hl", "tl"):
        for r in range(N):
            if not (np.sort(gentries(d[k][r]), axis=1) == np.arange(C)).all(): b.append(k + ": every number once in a group")
    none, least, most = [emit(mx_ref.quantize(np.full((128, 16), k, np.float32).astype(BF)))[1][0, 0] for k in (0.0, 2.0 ** -8, 2.0 ** 8)]
    for r in range(N):
        if ((d["wc"][r] == 0x7F) | (d["wc"][r] == 0xFF)).any(): b.append("wc: a code that is no number")
        s = mx_ref.live(d["ws"][r])
        if ((s != none) & ((s < least) | (s > most))).any(): b.append("ws: a scale out of range")
    return b
def ordered(s, a):
    e = np.sort(np.argsort(a, axis=1).reshape(8, -1, 2), axis=2)
    k = np.take_along_axis(s, e.reshape(8, -1), axis=1).reshape(e.shape)
    return np.where((k[:, :, 1] > k[:, :, 0])[:, :, None], e[:, :, ::-1], e).reshape(8, -1)
def transition(s, h, t):
    m = np.zeros((8, C), np.int64)
    np.put_along_axis(m, ordered(s, h), ordered(s, t), axis=1)
    return m
def behind(a, e):
    return np.take_along_axis(a, e, axis=1)
def reference(x, u, v, hl, tl, wc, ws):
    qu = [mx_ref.quantize(u[r]) for r in range(N)]
    lay = [pk(wc[r], ws[r]) for r in range(N)]
    now = [x[r] for r in range(N)]
    head, tail = [gentries(hl[r]) for r in range(N)], [gentries(tl[r]) for r in range(N)]
    for step in STEP:
        way, made = [], []
        for r in range(N):
            s = mx_ref.matmul(qu[r], mx_ref.quantize(now[r])) + np.float32(0.0)
            m0, m1 = transition(s[0::16], head[r], tail[r]), transition(s[1::16], head[r], tail[r])
            way.append(behind(m1, m0))
            z = mx_ref.quantize(((gcols(now[r], m0).astype(np.float32) + gcols(now[r], way[r]).astype(np.float32)) * np.float32(0.5)).astype(BF))
            made.append(mx_ref.quantize(tile([mx_ref.matmul(pick(lay[r], np.arange(128 * b, 128 * b + 128)), z) * np.float32(0.03125) for b in range(4)])))
        for r in range(N):
            p = r ^ step
            far = gcols(decode(made[p]).astype(BF), behind(way[r], way[p]))
            now[r] = (now[r].astype(np.float32) + far.astype(np.float32)).astype(BF)
            head[r], tail[r] = tail[r], behind(head[r], way[p])
    y, tp = np.zeros((N, 128, C), np.float32), np.zeros((N, 8, C), np.float32)
    oc, osc = np.zeros((N, 128, 4 * C), np.uint8), np.zeros((N, 16, C), np.uint8)
    for r in range(N):
        q = mx_ref.quantize(now[r])
        y[r] = mx_ref.matmul(mx_ref.quantize(v[r]), q)
        tp[r] = tail[r]
        oc[r], osc[r] = emit(q)
    return {"y": y, "tp": tp, "oc": oc, "osc": osc}

@@ -1,0 +1,467 @@
+from concourse.mybir import dt, AluOpType, ActivationFunctionType
+
+A = AluOpType
+AF = ActivationFunctionType
+C = 320
+HC = 160
+STEP = [1, 2, 4]
+CODE = "float8_e4m3fn_x4"
+
+SCRATCH = {
+    "cio": ("sbuf", [128, 320], "float32"), "dec": ("sbuf", [128, 320], "float32"),
+    "him": ("sbuf", [128, 320], "int32"), "hia": ("sbuf", [128, 320], "int32"), "mk": ("sbuf", [128, 320], "float32"),
+    "hold": ("sbuf", [128, 320], "float32"), "holdb": ("sbuf", [128, 320], "bfloat16"), "alt": ("sbuf", [128, 320], "bfloat16"),
+    "pmi": ("sbuf", [128, 2], "int32"), "pma": ("sbuf", [128, 2], "int32"), "sub": ("sbuf", [128, 1], "float32"),
+    "cp": ("sbuf", [128, 1], "float32"), "cp2": ("sbuf", [128, 1], "float32"), "cs": ("sbuf", [128, 1], "float32"),
+    "c16": ("sbuf", [128, 20], "float32"), "ciw": ("sbuf", [128, 20], "float32"),
+    "uoi": ("sbuf", [128, 16], "int32"), "uof": ("sbuf", [128, 16], "uint16"),
+    "one": ("sbuf", [128, 512], "bfloat16"), "et": ("sbuf", [128, 2048], "bfloat16"),
+    "qe": ("sbuf", [128, 512], CODE), "se": ("sbuf", [128, 512], "uint8"),
+    "ut": ("sbuf", [128, 512], "bfloat16"), "vt": ("sbuf", [128, 512], "bfloat16"),
+    "qu": ("sbuf", [128, 128], CODE), "su": ("sbuf", [128, 128], "uint8"),
+    "qu2": ("sbuf", [128, 256], CODE), "su2": ("sbuf", [128, 256], "uint8"),
+    "qv": ("sbuf", [128, 128], CODE), "sv": ("sbuf", [128, 128], "uint8"),
+    "qw": ("sbuf", [128, 512], CODE), "sw": ("sbuf", [128, 512], "uint8"),
+    "hlt": ("sbuf", [128, 40], "int32"), "hb": ("sbuf", [128, 40], "int32"), "hv": ("sbuf", [128, 40], "int32"),
+    "hb2": ("sbuf", [128, 40], "int32"), "enci": ("sbuf", [128, 40], "int32"),
+    "xp": ("sbuf", [128, 1280], "bfloat16"), "y32": ("sbuf", [128, 1280], "float32"), "zt": ("sbuf", [128, 1280], "bfloat16"),
+    "ht": ("sbuf", [128, 1280], "bfloat16"), "dd": ("sbuf", [128, 1280], "bfloat16"),
+    "qz": ("sbuf", [128, 320], CODE), "sz": ("sbuf", [128, 320], "uint8"),
+    "qx": ("sbuf", [128, 320], CODE), "sx": ("sbuf", [128, 320], "uint8"),
+    "qo": ("sbuf", [128, 320], CODE), "so": ("sbuf", [128, 320], "uint8"),
+    "yo": ("sbuf", [128, 320], "float32"), "tpr": ("sbuf", [128, 320], "float32"),
+    "ps": ("psum", [128, 4096], "float32"),
+    "fi": ("sbuf", [128, 320], "float32"),
+    "mt": ("sbuf", [128, 40], "float32"), "mf": ("sbuf", [128, 40], "float32"),
+    "g2": ("sbuf", [128, 40], "float32"), "q2": ("sbuf", [128, 40], "float32"),
+    "ga": ("sbuf", [128, 640], "float32"), "bit": ("sbuf", [128, 640], "bfloat16"),
+    "sca": ("sbuf", [128, 320], "float32"), "scb": ("sbuf", [128, 320], "float32"),
+    "m1r": ("sbuf", [128, 320], "float32"), "fr": ("sbuf", [128, 320], "float32"), "lr": ("sbuf", [128, 320], "float32"),
+    "lw": ("sbuf", [128, 20], "uint16"), "ajr": ("sbuf", [128, 320], "float32"),
+    "kjr": ("sbuf", [128, 640], "float32"), "kjs": ("sbuf", [128, 640], "float32"),
+    "ddc": ("sbuf", [128, 20], "float32"), "kd": ("sbuf", [128, 20], "float32"), "kq": ("sbuf", [128, 20], "float32"),
+    "k1": ("sbuf", [128, 20], "float32"), "kx": ("sbuf", [128, 20], "float32"), "kc": ("sbuf", [128, 20], "float32"),
+    "tr": ("sbuf", [128, 320], "float32"), "cvm": ("sbuf", [128, 320], "float32"), "hvr": ("sbuf", [128, 320], "float32"),
+    "raw0": ("sbuf", [128, 320], "float32"), "raw2": ("sbuf", [128, 320], "float32"),
+    "lohi": ("sbuf", [128, 20], "float32"), "rr": ("sbuf", [128, 20], "float32"),
+}
+for _k in (0, 1):
+    SCRATCH["sk%d" % _k] = ("sbuf", [128, 320], "float32")
+    SCRATCH["sum%d" % _k] = ("sbuf", [128, 320], "bfloat16")
+    SCRATCH["nx%d" % _k] = ("sbuf", [128, 320], "bfloat16")
+    SCRATCH["w%d" % _k] = ("sbuf", [128, 320], "bfloat16")
+    SCRATCH["mw%d" % _k] = ("sbuf", [128, 20], "uint16")
+    SCRATCH["xi%d" % _k] = ("sbuf", [128, 1280], "bfloat16")
+    SCRATCH["hvs%d" % _k] = ("sbuf", [128, 20], "uint16")
+    SCRATCH["hv%d" % _k] = ("sbuf", [128, 20], "uint16")
+    SCRATCH["lhr%d" % _k] = ("sbuf", [128, 320], "float32")
+for _n in range(4):
+    if _n < 2:
+        SCRATCH["enc%d" % _n] = ("sbuf", [128, 20], "uint16")
+    SCRATCH["pr%d" % _n] = ("sbuf", [128, 320], "float32")
+    SCRATCH["lhu%d" % _n] = ("sbuf", [128, 20], "uint16")
+for _r in (1, 2, 3):
+    SCRATCH["qh%d" % _r] = ("sbuf", [128, 320], CODE)
+    SCRATCH["sh%d" % _r] = ("sbuf", [128, 320], "uint8")
+    SCRATCH["lc%d" % _r] = ("sbuf", [128, 320], CODE)
+    SCRATCH["ls%d" % _r] = ("sbuf", [128, 320], "uint8")
+    SCRATCH["fw%d" % _r] = ("sbuf", [128, 20], "uint16")
+    SCRATCH["fp%d" % _r] = ("sbuf", [128, 20], "uint16")
+
+SEMAPHORES = ["qv_", "qs_", "qt_", "qg_", "dx", "dl", "du", "dw", "dv", "lsem", "oq", "oy", "ot"] + \
+    ["a%df" % r for r in (1, 2, 3)] + ["a%dc%d" % (r, c) for r in (1, 2, 3) for c in (0, 1)]
+
+
+def rank_program(g, core, T, topo):
+    rank = T.rank_of(core)
+    if rank is None:
+        return
+    Q = {"v": g.vector, "s": g.scalar, "t": g.tensor, "g": g, "y": g.sync}
+    SEM = {"v": "qv_", "s": "qs_", "t": "qt_", "g": "qg_"}
+    cnt = {}
+    known = {q: {} for q in Q}
+    snap = {}
+    wrote, read = {}, {}
+
+    def need(q, sem, val):
+        if known[q].get(sem, 0) >= val:
+            return
+        Q[q].wait_ge(T.sem[sem], val)
+        known[q][sem] = val
+        for k, w in snap.get((sem, val), {}).items():
+            if known[q].get(k, 0) < w:
+                known[q][k] = w
+
+    def order(q, rd, wr):
+        deps = {}
+        for t in rd:
+            for k, w in wrote.get(t, {}).items():
+                deps[k] = max(deps.get(k, 0), w)
+        for t in wr:
+            for d in (wrote.get(t, {}), read.get(t, {})):
+                for k, w in d.items():
+                    deps[k] = max(deps.get(k, 0), w)
+        for k, w in deps.items():
+            need(q, k, w)
+
+    def done(sem, val, rd, wr):
+        for t in rd:
+            d = read.setdefault(t, {})
+            d[sem] = max(d.get(sem, 0), val)
+        for t in wr:
+            wrote[t] = {sem: val}
+            read[t] = {}
+
+    def op(q, rd, wr, f):
+        order(q, rd, wr)
+        sem = SEM[q]
+        f().then_inc(T.sem[sem], 1)
+        cnt[sem] = cnt.get(sem, 0) + 1
+        snap[(sem, cnt[sem])] = dict(known[q])
+        done(sem, cnt[sem], rd, wr)
+
+    def dma(q, sem, out, in_, rd=(), wr=(), total=16):
+        order(q, rd, wr)
+        Q[q].dma_start(out, in_).then_inc(T.sem[sem], 16)
+        cnt[sem] = total
+        done(sem, total, rd, wr)
+
+    V, S, P = g.vector, g.scalar, g.tensor
+
+    def bank(k, n):
+        return T.ps[:, 512 * k:512 * k + n]
+
+    def lst(name, a=0, b=20):
+        return T[name][:, a:b]
+
+    def pick(name, off, a=0, n=C):
+        return T[name][:, a:a + n].indirect(off)
+
+    dma("s", "dl", T.hlt[:, 0:20], T.hl[:], wr=["hlt"], total=32)
+    dma("y", "dl", T.hlt[:, 20:40], T.tl[:], total=32)
+    dma("y", "dx", T.xi0[:], T.x[:], wr=["xi0.%d" % b for b in range(4)])
+    dma("s", "du", T.ut[:], T.u[:], wr=["ut"])
+    dma("y", "dw", T.qw[:].bitcast(dt.uint8), T.wc[:], wr=["qw"], total=32)
+    dma("y", "dw", T.sw[:], T.ws[:], total=32)
+    dma("y", "dv", T.vt[:], T.v[:], wr=["vt"])
+
+    op("g", [], ["pmi"], lambda: g.iota(T.pmi[:], [[0, 2]], 0, 1))
+    op("g", [], ["him"], lambda: g.iota(T.him[:], [[1, 320]], 128, -1))
+    op("g", [], ["c16"], lambda: g.iota(T.c16[:], [[16, 20]], 0, 0, allow_small_or_imprecise_dtypes=True))
+    op("g", [], ["cio"], lambda: g.iota(T.cio[:], [[1, 320]], 0, 0, allow_small_or_imprecise_dtypes=True))
+    op("g", [], ["uoi"], lambda: g.iota(T.uoi[:], [[1, 2], [16, 8]], 0, 0))
+    op("g", [], ["alt"], lambda: g.iota(T.alt[:], [[0, 160], [1, 2]], 0, 0, allow_small_or_imprecise_dtypes=True))
+    op("g", [], ["cvm"], lambda: g.iota(T.cvm[:], [[0, 2], [1, 160]], 0, 0, allow_small_or_imprecise_dtypes=True))
+    op("g", [], ["dec"], lambda: g.iota(T.dec[:], [[1, 2], [2, 160]], 0, 0, allow_small_or_imprecise_dtypes=True))
+    op("v", [], ["one"], lambda: V.memset(T.one[:], 1.0))
+    for b in range(4):
+        op("g", ["one"], ["et%d" % b], lambda: g.affine_select(T.et[:, 512 * b:512 * b + 512], T.one[:], [[-1, 512]], A.is_equal, 0.0, b, 4))
+    op("v", ["pmi"], ["pma"], lambda: V.tensor_scalar(T.pma[:], T.pmi[:], 15, None, A.bitwise_and))
+    op("v", ["him"], ["hia"], lambda: V.tensor_scalar(T.hia[:], T.him[:], 15, None, A.bitwise_and))
+    op("v", ["pma"], ["sub"], lambda: V.tensor_scalar(T["sub"][:], T.pma[:, 0:1], -512.0, 7680.0, A.mult, A.add))
+    op("v", ["pma"], ["cs"], lambda: V.tensor_scalar(T.cs[:], T.pma[:, 0:1], -511.0, 7680.0, A.mult, A.add))
+    op("v", ["hia"], ["mk"], lambda: V.tensor_scalar(T.mk[:], T.hia[:], 0.0, -16896.0, A.is_equal, A.mult))
+    op("v", ["pma"], ["cp"], lambda: V.tensor_scalar(T.cp[:], T.pma[:, 0:1], -2.0, 30.0, A.mult, A.add))
+    op("v", ["pma"], ["cp2"], lambda: V.tensor_scalar(T.cp2[:], T.pma[:, 0:1], -4.0, 61.0, A.mult, A.add))
+    op("v", ["c16", "cs"], ["ciw"], lambda: V.tensor_scalar(T.ciw[:], T.c16[:], T.cs[:], None, A.add))
+    op("s", ["mk"], ["hold"], lambda: S.activation(T.hold[:], T.mk[:], AF.Copy, bias=512.0))
+    op("s", ["mk"], ["holdb"], lambda: S.activation(T.holdb[:], T.mk[:], AF.Copy, bias=2.0, scale=0.00390625))
+
+    nsc = [0]
+
+    def wrap_scan(row, rtok):
+        nsc[0] += 1
+        b = ("sca", "scb")[nsc[0] % 2]
+        op("v", [rtok, "hold"], [b], lambda: V.tensor_tensor_scan(T[b][:], T.hold[:], row, 0.0, A.add, A.max))
+        return b
+
+    def wrap_out(b, out, otok):
+        op("v", [b, "sub"], [otok], lambda: V.tensor_scalar(out, T[b][:, 15:C:16], T["sub"][:], None, A.subtract))
+
+    def wrap(row, rtok, out, otok):
+        wrap_out(wrap_scan(row, rtok), out, otok)
+
+    def spread(name, off, otok, win="cio"):
+        op("s", [win, otok], [name], lambda: S.activation(T[name][:], pick(win, off), AF.Copy))
+
+    def scatter(n):
+        op("v", ["enc%d" % n, "cio"], ["pr%d" % n], lambda: V.tensor_copy(T["pr%d" % n][:, 0:C].indirect(lst("enc%d" % n)), T.cio[:]))
+
+    def vertices(n):
+        b = wrap_scan(T["pr%d" % n][:], "pr%d" % n)
+
+        def rest():
+            op("v", [b], ["lo"], lambda: V.tensor_tensor(T.lohi[:, 0:10], T[b][:, 15:HC:16], T[b][:, HC + 15:C:16], A.min))
+            op("v", [b], ["hi"], lambda: V.tensor_tensor(T.lohi[:, 10:20], T[b][:, 15:HC:16], T[b][:, HC + 15:C:16], A.max))
+            op("v", ["lo", "hi", "sub"], ["lhu%d" % n], lambda: V.tensor_scalar(T["lhu%d" % n][:], T.lohi[:], T["sub"][:], None, A.subtract))
+        return rest
+
+    def places(n, src, stok):
+        m = n % 2
+        op("v", [stok], ["hv%d" % m], lambda: V.tensor_copy(T["hv%d" % m][:], src))
+        op("v", [stok], ["hvs%d" % m], lambda: V.tensor_scalar(T["hvs%d" % m][:], src, 2.0, 1.0, A.mult, A.add))
+
+    def rows(n):
+        spread("lhr%d" % (n % 2), lst("lhu%d" % n), "lhu%d" % n)
+
+    def role_pick(n):
+        m = n % 2
+        op("s", ["lhr%d" % m, "hv%d" % m], ["ajr"], lambda: S.activation(T.ajr[:], pick("lhr%d" % m, lst("hv%d" % m), 0, HC), AF.Copy))
+
+    def role(n):
+        m = n % 2
+        b = wrap_scan(T.ajr[:], "ajr")
+        op("v", [b, "ciw"], ["rr"], lambda: V.tensor_tensor(T.rr[:], T[b][:, 15:C:16], T.ciw[:], A.not_equal))
+        op("v", ["rr"], ["g2%d" % m], lambda: V.tensor_scalar(T.g2[:, 20 * m:20 * m + 20], T.rr[:], 2.0, -1.0, A.mult, A.add))
+        op("v", ["rr", "cp", "cp2"], ["q2%d" % m], lambda: V.tensor_scalar(
+            T.q2[:, 20 * m:20 * m + 20], T.rr[:], T.cp2[:], T.cp[:], A.mult, A.subtract))
+
+    def cand_pick(n):
+        i = (n - 1) % 2
+        for h in (0, 1):
+            op("s", ["pr%d" % n, "hv%d" % i], ["kjr%d" % h], lambda: S.activation(
+                T.kjr[:, C * h:C * h + C], pick("pr%d" % n, lst("hv%d" % i), HC * h, HC), AF.Copy))
+
+    def cand_scan(n):
+        for h in (0, 1):
+            op("v", ["kjr%d" % h, "hold"], ["kjs%d" % h], lambda: V.tensor_tensor_scan(
+                T.kjs[:, C * h:C * h + C], T.hold[:], T.kjr[:, C * h:C * h + C], 0.0, A.add, A.max))
+
+    def cand(n):
+        i = (n - 1) % 2
+        a, b = T.kjs[:, 15:C:16], T.kjs[:, C + 15:2 * C:16]
+        op("v", ["kjs0", "kjs1"], ["kx"], lambda: V.tensor_tensor(T.kx[:], a, b, A.max))
+        op("v", ["kjs0", "kjs1"], ["kc"], lambda: V.tensor_tensor(T.kc[:], a, b, A.min))
+        op("v", ["kx", "kc"], ["ddc"], lambda: V.tensor_tensor(T.ddc[:], T.kx[:], T.kc[:], A.subtract))
+
+    def cand_b(n):
+        i = (n - 1) % 2
+        op("v", ["ddc", "q2%d" % i], ["kq"], lambda: V.tensor_tensor(T.kq[:], T.ddc[:], T.q2[:, 20 * i:20 * i + 20], A.mult))
+        op("v", ["ddc", "g2%d" % i], ["kd"], lambda: V.tensor_tensor(T.kd[:], T.ddc[:], T.g2[:, 20 * i:20 * i + 20], A.mult))
+        op("v", ["kx", "kq"], ["k1"], lambda: V.tensor_tensor(T.k1[:], T.kx[:], T.kq[:], A.subtract))
+
+    op("v", ["hlt"], ["hb"], lambda: V.tensor_scalar(T.hb[:], T.hlt[:], 1, None, A.bitwise_and))
+    op("v", ["hlt"], ["hv"], lambda: V.tensor_scalar(T.hv[:], T.hlt[:], 1, None, A.arith_shift_right))
+    op("v", ["hb"], ["hb2"], lambda: V.tensor_scalar(T.hb2[:], T.hb[:], 160, None, A.mult))
+    op("v", ["hb2", "hv"], ["enci"], lambda: V.tensor_tensor(T.enci[:], T.hb2[:], T.hv[:], A.add))
+    for n in (1, 0):
+        op("v", ["enci"], ["enc%d" % n], lambda: V.tensor_copy(T["enc%d" % n][:], T.enci[:, 20 * n:20 * n + 20]))
+    scatter(1)
+    fin = vertices(1)
+    places(0, T.hv[:, 0:20], "hv")
+    fin()
+    op("v", ["ut"], ["qu"], lambda: V.quantize_mx(T.qu[:], T.su[:], T.ut[:]))
+    op("v", ["uoi"], ["uof"], lambda: V.tensor_copy(T.uof[:], T.uoi[:]))
+
+    def quant_x(name):
+        for c in (0, 1):
+            op("v", ["%s.%d" % (name, b) for b in range(4)], ["qx%d" % c], lambda: V.quantize_mx(
+                T.qx[:, HC * c:HC * c + HC], T.sx[:, HC * c:HC * c + HC], T[name][:, 640 * c:640 * c + 640]))
+
+    def plane(b, name):
+        op("s", ["%s.%d" % (name, b)], ["xp%d" % b], lambda: S.activation(T.xp[:, C * b:C * b + C], T[name][:, b:1280:4], AF.Copy))
+
+    quant_x("xi0")
+    for b in range(3):
+        plane(b, "xi0")
+    op("v", ["qu", "uof"], ["qu2"], lambda: V.tensor_copy(T.qu2[:].bitcast(dt.uint32), T.qu[:].bitcast(dt.uint32).indirect(T.uof[:])))
+    op("s", ["qu", "uof"], ["su2"], lambda: S.activation(T.su2[:], T.su[:].indirect(T.uof[:]), AF.Copy))
+    cand_pick(1)
+    rows(1)
+    scatter(0)
+    vertices(0)()
+    rows(0)
+    role_pick(0)
+
+    for r in (1, 2, 3):
+        last = r == 3
+        peer = T.cores[rank ^ STEP[r - 1]]
+        rid, pid = topo.addr(peer)[0], topo.addr(peer)[1]
+        mask = topo.mask(core, peer)
+        neng = len(topo.engines(core, peer))
+        xo, xn = "xi%d" % ((r - 1) % 2), "xi%d" % (r % 2)
+        ai, ao = "lhu%d" % (r - 1), "lhu%d" % r
+
+        for k in (1, 0):
+            for c in (0, 1):
+                op("t", ["qx%d" % c, "qu2", "su2"], ["bk%d" % (2 * k + c)], lambda: P.matmul_mx(
+                    bank(2 * k + c, HC), T.qu2[:, 128 * k:128 * k + 128], T.su2[:, 128 * k:128 * k + 128],
+                    T.qx[:, HC * c:HC * c + HC], T.sx[:, HC * c:HC * c + HC], True, True))
+        for k in (1, 0):
+            for c in (0, 1):
+                out, in_, tok = T["sk%d" % k][:, HC * c:HC * c + HC], bank(2 * k + c, HC), ["bk%d" % (2 * k + c), "sk%d.%d" % (k, c)]
+                if r > 1 and (k, c) == (1, 0):
+                    op("s", [], tok, lambda: S.activation(out, in_, AF.Copy))
+                else:
+                    op("v", [], tok, lambda: V.tensor_copy(out, in_))
+        if r == 1:
+            cand_scan(1)
+        cand(r)
+        for k in (1, 0):
+            sk, ga, bt = "sk%d" % k, "ga%d" % k, "bit%d" % k
+            for i, w in ((0, ai), (1, ao)):
+                op("s", [sk + ".0", sk + ".1", w], [ga + ".%d" % i], lambda: S.activation(
+                    T.ga[:, C * k + HC * i:C * k + HC * i + HC], pick(sk, lst(w, 0, 10)), AF.Copy))
+            for i, w in ((0, ai), (1, ao)):
+                op("v", [sk + ".0", sk + ".1", w, ga + ".%d" % i], [bt + ".%d" % i], lambda: V.tensor_tensor(
+                    T.bit[:, C * k + i:C * k + C:2], pick(sk, lst(w, 10, 20)), T.ga[:, C * k + HC * i:C * k + HC * i + HC], A.is_gt))
+            op("v", [bt + ".0", bt + ".1", "alt"], ["sum%d" % k], lambda: V.tensor_tensor_scan(
+                T["sum%d" % k][:], T.alt[:], T.bit[:, C * k:C * k + C], 0.0, A.mult, A.add))
+            if k == 1 and r == 1:
+                role(0)
+        if r == 1:
+            places(1, T.hv[:, 20:40], "hv")
+        cand_b(r)
+        hvs = "hvs%d" % ((r - 1) % 2)
+        for k in (1, 0):
+            op("s", ["sum%d" % k, hvs], ["nx%d" % k], lambda: S.activation(T["nx%d" % k][:], pick("sum%d" % k, lst(hvs)), AF.Square, bias=-1.0))
+
+        if r == 1:
+            plane(3, "xi0")
+
+        def yadd(b):
+            op("v", ["xp%d" % b, "%s.%d" % (xo, b), "mw1"], ["y%d" % b], lambda: V.tensor_tensor(
+                T.y32[:, C * b:C * b + C], pick("xp", lst("mw1"), C * b), T[xo][:, b:1280:4], A.add))
+
+        def move(k, i):
+            if i == 0:
+                op("v", ["nx%d" % k, "holdb"], ["w%d" % k], lambda: V.tensor_tensor_scan(T["w%d" % k][:], T.holdb[:], T["nx%d" % k][:], 0.0, A.add, A.max))
+            if i == 1:
+                op("v", ["w%d" % k, "kd"], ["mt%d" % k], lambda: V.tensor_tensor(T.mt[:, 20 * k:20 * k + 20], T["w%d" % k][:, 15:C:16], T.kd[:], A.mult))
+            if i == 2:
+                op("v", ["mt%d" % k, "k1"], ["mf%d" % k], lambda: V.tensor_tensor(T.mf[:, 20 * k:20 * k + 20], T.mt[:, 20 * k:20 * k + 20], T.k1[:], A.add))
+            if i == 3:
+                op("v", ["mf%d" % k, "sub"], ["mw%d" % k], lambda: V.tensor_scalar(
+                    T["mw%d" % k][:], T.mf[:, 20 * k:20 * k + 20], T["sub"][:], None, A.subtract))
+
+        fw, fp = "fw%d" % r, "fp%d" % r
+        for k, i in ((1, 0), (1, 1), (1, 2), (0, 0), (1, 3), (0, 1), (0, 2), (0, 3)):
+            move(k, i)
+        for b in (0, 1, 2):
+            yadd(b)
+        spread("m1r", lst("mw1"), "mw1")
+
+        def pick_f():
+            op("s", ["m1r", "mw0"], ["fr"], lambda: S.activation(T.fr[:], pick("m1r", lst("mw0")), AF.Copy))
+
+        def send_f():
+            order("g", [fw], [])
+            g.remote_dma(T[fp][:], T[fw][:], T.sem["a%df" % r], T.sem.lsem, pid, rid, mask)
+            cnt["lsem"] = cnt.get("lsem", 0) + neng
+
+        def heads():
+            if r == 1:
+                role(1)
+            elif r == 2:
+                wrap(T.tr[:], "tr", T.hv0[:], "hv0")
+                op("v", ["hv0"], ["hvs0"], lambda: V.tensor_scalar(T.hvs0[:], T.hv0[:], 2.0, 1.0, A.mult, A.add))
+
+        pick_f()
+        wrap(T.fr[:], "fr", T[fw][:], fw)
+        send_f()
+        yadd(3)
+
+        for b in range(3):
+            op("s", ["y%d" % b, "mw0"], ["z%d" % b], lambda: S.activation(T.zt[:, b:1280:4], pick("y32", lst("mw0"), C * b), AF.Copy, scale=0.5))
+        op("v", ["y3", "mw0"], ["z3"], lambda: V.tensor_scalar(T.zt[:, 3:640:4], pick("y32", lst("mw0", 0, 10), 3 * C), 0.5, None, A.mult))
+        op("s", ["y3", "mw0"], ["z4"], lambda: S.activation(T.zt[:, 643:1280:4], pick("y32", lst("mw0", 10, 20), 3 * C), AF.Copy, scale=0.5))
+        for c in (0, 1):
+            op("v", ["z0", "z1", "z2", "z%d" % (3 + c)], ["qz%d" % c], lambda: V.quantize_mx(
+                T.qz[:, HC * c:HC * c + HC], T.sz[:, HC * c:HC * c + HC], T.zt[:, 640 * c:640 * c + 640]))
+            for b in range(4):
+                op("t", ["qz%d" % c, "qw"], ["bk%d" % (4 * c + b)], lambda: P.matmul_mx(
+                    bank(4 * c + b, HC), T.qw[:, 128 * b:128 * b + 128], T.sw[:, 128 * b:128 * b + 128],
+                    T.qz[:, HC * c:HC * c + HC], T.sz[:, HC * c:HC * c + HC], True, True))
+        qh, sh, lc, ls = "qh%d" % r, "sh%d" % r, "lc%d" % r, "ls%d" % r
+        if r == 1:
+            role_pick(1)
+        for c in (0, 1):
+            for b in range(4):
+                if (c, b) == (0, 2):
+                    heads()
+                out = T.ht[:, 640 * c + b:640 * c + 640:4]
+                if b % 2 == 0:
+                    op("v", [], ["bk%d" % (4 * c + b), "h%d%d" % (c, b)], lambda: V.tensor_scalar(out, bank(4 * c + b, HC), 0.03125, None, A.mult))
+                else:
+                    op("s", [], ["bk%d" % (4 * c + b), "h%d%d" % (c, b)], lambda: S.activation(out, bank(4 * c + b, HC), AF.Copy, scale=0.03125))
+            op("v", ["h%d%d" % (c, b) for b in range(4)], [qh + str(c)], lambda: V.quantize_mx(
+                T[qh][:, HC * c:HC * c + HC], T[sh][:, HC * c:HC * c + HC], T.ht[:, 640 * c:640 * c + 640]))
+            order("g", [qh + str(c)], [])
+            for out, in_ in ((T[lc][:, HC * c:HC * c + HC].bitcast(dt.uint8), T[qh][:, HC * c:HC * c + HC].bitcast(dt.uint8)),
+                             (T[ls][:, HC * c:HC * c + HC], T[sh][:, HC * c:HC * c + HC])):
+                g.remote_dma(out, in_, T.sem["a%dc%d" % (r, c)], T.sem.lsem, pid, rid, mask)
+                cnt["lsem"] += neng
+        for sem, n in [("a%df" % r, neng), ("a%dc0" % r, 2 * neng), ("a%dc1" % r, 2 * neng)]:
+            cnt[sem] = n
+        wrote[fp] = {"a%df" % r: neng}
+        for c in (0, 1):
+            wrote["ld%d%d" % (r, c)] = {"a%dc%d" % (r, c): 2 * neng}
+
+        n = r + 1
+        if not last:
+            op("v", [fp, "cio"], ["fi"], lambda: V.tensor_copy(T.fi[:, 0:C].indirect(lst(fp)), T.cio[:]))
+            if r == 1:
+                for b in range(4):
+                    op("v", ["et%d" % b], ["qe%d" % b], lambda: V.quantize_mx(
+                        T.qe[:, 128 * b:128 * b + 128], T.se[:, 128 * b:128 * b + 128], T.et[:, 512 * b:512 * b + 512]))
+        else:
+            op("v", ["vt"], ["qv"], lambda: V.quantize_mx(T.qv[:], T.sv[:], T.vt[:]))
+        op("s", ["fr", fp], ["lr"], lambda: S.activation(T.lr[:], pick("fr", lst(fp)), AF.Copy))
+        if not last:
+            if r == 1:
+                op("s", ["cvm", "enc0"], ["hvr"], lambda: S.activation(T.hvr[:], pick("cvm", lst("enc0")), AF.Copy))
+            else:
+                rows(2)
+                role_pick(2)
+            op("s", ["fi", "lhu%d" % (r - 1)], ["pr%d" % n], lambda: S.activation(T["pr%d" % n][:], pick("fi", lst("lhu%d" % (r - 1))), AF.Copy))
+            wrap(T.lr[:], "lr", T.lw[:], "lw")
+            vertices(n)()
+            cand_pick(n)
+            if r == 2:
+                role(2)
+            cand_scan(n)
+        else:
+            spread("raw0", lst("enc0"), "enc0", "dec")
+            spread("raw2", lst("fp1"), "fp1", "raw0")
+            wrap(T.lr[:], "lr", T.lw[:], "lw")
+            op("s", ["raw2", fp], ["tpr"], lambda: S.activation(T.tpr[:], pick("raw2", lst(fp)), AF.Copy))
+            dma("y", "ot", T.tp[:], T.tpr[0:128:16, :], rd=["tpr"])
+
+        if r == 1:
+            op("s", ["hvr", fp], ["tr"], lambda: S.activation(T.tr[:], pick("hvr", lst(fp)), AF.Copy))
+        for c in (0, 1):
+            for b in range(4):
+                op("t", ["ld%d%d" % (r, c), "qe%d" % b], ["bk%d" % (4 * c + b)], lambda: P.matmul_mx(
+                    bank(4 * c + b, HC), T.qe[:, 128 * b:128 * b + 128], T.se[:, 128 * b:128 * b + 128],
+                    T[lc][:, HC * c:HC * c + HC], T[ls][:, HC * c:HC * c + HC], True, True))
+            for b in range(4):
+                out = T.dd[:, C * b + HC * c:C * b + HC * c + HC]
+                if b == 0 and c == 1:
+                    op("v", [], ["bk%d" % (4 * c + b), "d%d%d" % (c, b)], lambda: V.tensor_copy(out, bank(4 * c + b, HC)))
+                else:
+                    op("s", [], ["bk%d" % (4 * c + b), "d%d%d" % (c, b)], lambda: S.activation(out, bank(4 * c + b, HC), AF.Copy))
+        for b in range(4):
+            op("v", ["d0%d" % b, "d1%d" % b, "lw", "%s.%d" % (xo, b)], ["%s.%d" % (xn, b)], lambda: V.tensor_tensor(
+                T[xn][:, b:1280:4], pick("dd", lst("lw"), C * b), T[xo][:, b:1280:4], A.add))
+        toks = ["%s.%d" % (xn, b) for b in range(4)]
+        if not last:
+            quant_x(xn)
+            for b in range(4):
+                plane(b, xn)
+        else:
+            for c in (0, 1):
+                op("v", toks, ["qo%d" % c], lambda: V.quantize_mx(
+                    T.qo[:, HC * c:HC * c + HC], T.so[:, HC * c:HC * c + HC], T[xn][:, 640 * c:640 * c + 640]))
+
+    dma("y", "oq", T.oc[:], T.qo[:].bitcast(dt.uint8), rd=["qo0", "qo1"], total=80)
+    for k in range(4):
+        dma("y", "oq", T.osc[4 * k:4 * k + 4, :], T.so[32 * k:32 * k + 4, :], rd=["qo0", "qo1"], total=80)
+    for c in (0, 1):
+        op("t", ["qo%d" % c, "qv"], ["bk%d" % c], lambda: P.matmul_mx(
+            bank(c, HC), T.qv[:], T.sv[:], T.qo[:, HC * c:HC * c + HC], T.so[:, HC * c:HC * c + HC], True, True))
+    op("v", [], ["bk0", "yo0"], lambda: V.tensor_copy(T.yo[:, 0:HC], bank(0, HC)))
+    op("s", [], ["bk1", "yo1"], lambda: S.activation(T.yo[:, HC:C], bank(1, HC), AF.Copy))
+    for c in (0, 1):
+        dma("s", "oy", T.y[:, HC * c:HC * c + HC], T.yo[:, HC * c:HC * c + HC], rd=["yo%d" % c], total=32)
+    for sem in sorted(cnt):
+        need("g", sem, cnt[sem])

@@ -6,24 +6,26 @@ C = 320
 HC = 160
 STEP = [1, 2, 4]
 CODE = "float8_e4m3fn_x4"
+K1 = 24
 
 SCRATCH = {
-    "cio": ("sbuf", [128, 320], "float32"), "dec": ("sbuf", [128, 320], "float32"),
-    "him": ("sbuf", [128, 320], "int32"), "hia": ("sbuf", [128, 320], "int32"), "mk": ("sbuf", [128, 320], "float32"),
-    "hold": ("sbuf", [128, 320], "float32"), "holdb": ("sbuf", [128, 320], "bfloat16"), "alt": ("sbuf", [128, 320], "bfloat16"),
+    "cio": ("sbuf", [128, 320], "float32"), "j16": ("sbuf", [128, 320], "bfloat16"), "mk": ("sbuf", [128, 320], "float32"),
+    "hold": ("sbuf", [128, 320], "float32"), "alt": ("sbuf", [128, 320], "bfloat16"),
     "pmi": ("sbuf", [128, 2], "int32"), "pma": ("sbuf", [128, 2], "int32"), "sub": ("sbuf", [128, 1], "float32"),
-    "cp": ("sbuf", [128, 1], "float32"), "cp2": ("sbuf", [128, 1], "float32"), "cs": ("sbuf", [128, 1], "float32"),
+    "i17": ("sbuf", [128, 2], "int32"), "s16": ("sbuf", [128, 2], "int32"), "s21": ("sbuf", [128, 1], "float32"),
+    "pmf": ("sbuf", [128, 1], "float32"), "p16": ("sbuf", [128, 1], "float32"), "cs": ("sbuf", [128, 1], "float32"),
     "c16": ("sbuf", [128, 20], "float32"), "ciw": ("sbuf", [128, 20], "float32"),
-    "uoi": ("sbuf", [128, 16], "int32"), "uof": ("sbuf", [128, 16], "uint16"),
+    "n16": ("sbuf", [128, 4], "float32"), "n24": ("sbuf", [128, 4], "float32"), "n48": ("sbuf", [128, 4], "float32"),
+    "c256": ("sbuf", [128, 4], "float32"), "tof": ("sbuf", [128, 4], "uint16"),
     "one": ("sbuf", [128, 512], "bfloat16"), "et": ("sbuf", [128, 2048], "bfloat16"),
     "qe": ("sbuf", [128, 512], CODE), "se": ("sbuf", [128, 512], "uint8"),
     "ut": ("sbuf", [128, 512], "bfloat16"), "vt": ("sbuf", [128, 512], "bfloat16"),
     "qu": ("sbuf", [128, 128], CODE), "su": ("sbuf", [128, 128], "uint8"),
-    "qu2": ("sbuf", [128, 256], CODE), "su2": ("sbuf", [128, 256], "uint8"),
     "qv": ("sbuf", [128, 128], CODE), "sv": ("sbuf", [128, 128], "uint8"),
     "qw": ("sbuf", [128, 512], CODE), "sw": ("sbuf", [128, 512], "uint8"),
     "hlt": ("sbuf", [128, 40], "int32"), "hb": ("sbuf", [128, 40], "int32"), "hv": ("sbuf", [128, 40], "int32"),
-    "hb2": ("sbuf", [128, 40], "int32"), "enci": ("sbuf", [128, 40], "int32"),
+    "hb2": ("sbuf", [128, 40], "int32"), "enci": ("sbuf", [128, 40], "int32"), "spi": ("sbuf", [128, 40], "int32"),
+    "enc": ("sbuf", [128, 40], "uint16"), "sp": ("sbuf", [128, 40], "uint16"), "hu": ("sbuf", [128, 20], "uint16"),
     "xp": ("sbuf", [128, 1280], "bfloat16"), "y32": ("sbuf", [128, 1280], "float32"), "zt": ("sbuf", [128, 1280], "bfloat16"),
     "ht": ("sbuf", [128, 1280], "bfloat16"), "dd": ("sbuf", [128, 1280], "bfloat16"),
     "qz": ("sbuf", [128, 320], CODE), "sz": ("sbuf", [128, 320], "uint8"),
@@ -31,35 +33,29 @@ SCRATCH = {
     "qo": ("sbuf", [128, 320], CODE), "so": ("sbuf", [128, 320], "uint8"),
     "yo": ("sbuf", [128, 320], "float32"), "tpr": ("sbuf", [128, 320], "float32"),
     "ps": ("psum", [128, 4096], "float32"),
-    "fi": ("sbuf", [128, 320], "float32"),
-    "mt": ("sbuf", [128, 40], "float32"), "mf": ("sbuf", [128, 40], "float32"),
-    "g2": ("sbuf", [128, 40], "float32"), "q2": ("sbuf", [128, 40], "float32"),
-    "ga": ("sbuf", [128, 640], "float32"), "bit": ("sbuf", [128, 640], "bfloat16"),
-    "sca": ("sbuf", [128, 320], "float32"), "scb": ("sbuf", [128, 320], "float32"),
+    "sk": ("sbuf", [128, 320], "float32"), "ga": ("sbuf", [128, 320], "float32"), "bit": ("sbuf", [128, 320], "bfloat16"),
+    "sum": ("sbuf", [128, 320], "bfloat16"), "nx": ("sbuf", [128, 352], "bfloat16"), "tt": ("sbuf", [128, 672], "bfloat16"),
+    "kd": ("sbuf", [128, 48], "float32"), "k1": ("sbuf", [128, 48], "float32"),
+    "mt": ("sbuf", [128, 48], "float32"), "mf": ("sbuf", [128, 48], "float32"), "mw": ("sbuf", [128, 48], "uint16"),
+    "fi": ("sbuf", [128, 320], "float32"), "g2": ("sbuf", [128, 20], "float32"), "rr": ("sbuf", [128, 20], "float32"),
+    "sca": ("sbuf", [128, 320], "float32"), "scb": ("sbuf", [128, 320], "float32"), "scr": ("sbuf", [128, 320], "float32"),
     "m1r": ("sbuf", [128, 320], "float32"), "fr": ("sbuf", [128, 320], "float32"), "lr": ("sbuf", [128, 320], "float32"),
     "lw": ("sbuf", [128, 20], "uint16"), "ajr": ("sbuf", [128, 320], "float32"),
     "kjr": ("sbuf", [128, 640], "float32"), "kjs": ("sbuf", [128, 640], "float32"),
-    "ddc": ("sbuf", [128, 20], "float32"), "kd": ("sbuf", [128, 20], "float32"), "kq": ("sbuf", [128, 20], "float32"),
-    "k1": ("sbuf", [128, 20], "float32"), "kx": ("sbuf", [128, 20], "float32"), "kc": ("sbuf", [128, 20], "float32"),
-    "tr": ("sbuf", [128, 320], "float32"), "cvm": ("sbuf", [128, 320], "float32"), "hvr": ("sbuf", [128, 320], "float32"),
+    "ddc": ("sbuf", [128, 20], "float32"), "kq": ("sbuf", [128, 20], "float32"),
+    "kx": ("sbuf", [128, 20], "float32"), "kc": ("sbuf", [128, 20], "float32"),
+    "tr": ("sbuf", [128, 320], "float32"), "hvr": ("sbuf", [128, 320], "float32"), "lor": ("sbuf", [128, 160], "float32"),
     "raw0": ("sbuf", [128, 320], "float32"), "raw2": ("sbuf", [128, 320], "float32"),
-    "lohi": ("sbuf", [128, 20], "float32"), "rr": ("sbuf", [128, 20], "float32"),
+    "lohi": ("sbuf", [128, 20], "float32"),
 }
 for _k in (0, 1):
-    SCRATCH["sk%d" % _k] = ("sbuf", [128, 320], "float32")
-    SCRATCH["sum%d" % _k] = ("sbuf", [128, 320], "bfloat16")
-    SCRATCH["nx%d" % _k] = ("sbuf", [128, 320], "bfloat16")
-    SCRATCH["w%d" % _k] = ("sbuf", [128, 320], "bfloat16")
-    SCRATCH["mw%d" % _k] = ("sbuf", [128, 20], "uint16")
     SCRATCH["xi%d" % _k] = ("sbuf", [128, 1280], "bfloat16")
-    SCRATCH["hvs%d" % _k] = ("sbuf", [128, 20], "uint16")
-    SCRATCH["hv%d" % _k] = ("sbuf", [128, 20], "uint16")
-    SCRATCH["lhr%d" % _k] = ("sbuf", [128, 320], "float32")
 for _n in range(4):
-    if _n < 2:
-        SCRATCH["enc%d" % _n] = ("sbuf", [128, 20], "uint16")
     SCRATCH["pr%d" % _n] = ("sbuf", [128, 320], "float32")
     SCRATCH["lhu%d" % _n] = ("sbuf", [128, 20], "uint16")
+    if _n < 3:
+        SCRATCH["hvs%d" % _n] = ("sbuf", [128, 20], "uint16")
+        SCRATCH["hv%d" % _n] = ("sbuf", [128, 20], "uint16")
 for _r in (1, 2, 3):
     SCRATCH["qh%d" % _r] = ("sbuf", [128, 320], CODE)
     SCRATCH["sh%d" % _r] = ("sbuf", [128, 320], "uint8")
@@ -95,7 +91,7 @@ def rank_program(g, core, T, topo):
     def order(q, rd, wr):
         deps = {}
         for t in rd:
-            for k, w in wrote.get(t, {}).items():
+            for k, w in wrote[t].items():
                 deps[k] = max(deps.get(k, 0), w)
         for t in wr:
             for d in (wrote.get(t, {}), read.get(t, {})):
@@ -137,6 +133,14 @@ def rank_program(g, core, T, topo):
     def pick(name, off, a=0, n=C):
         return T[name][:, a:a + n].indirect(off)
 
+    def ts(out, in_, s1, s2, *ops, to=None):
+        names = [s for s in (s1, s2) if isinstance(s, str)]
+        a, b = [T[s][:] if isinstance(s, str) else s for s in (s1, s2)]
+        op("v", [in_] + names, [out], lambda: V.tensor_scalar(T[out][:] if to is None else to[0], T[in_][:] if to is None else to[1], a, b, *ops))
+
+    def tt(out, in0, in1, o):
+        op("v", [in0, in1], [out], lambda: V.tensor_tensor(T[out][:], T[in0][:], T[in1][:], o))
+
     dma("s", "dl", T.hlt[:, 0:20], T.hl[:], wr=["hlt"], total=32)
     dma("y", "dl", T.hlt[:, 20:40], T.tl[:], total=32)
     dma("y", "dx", T.xi0[:], T.x[:], wr=["xi0.%d" % b for b in range(4)])
@@ -146,132 +150,170 @@ def rank_program(g, core, T, topo):
     dma("y", "dv", T.vt[:], T.v[:], wr=["vt"])
 
     op("g", [], ["pmi"], lambda: g.iota(T.pmi[:], [[0, 2]], 0, 1))
-    op("g", [], ["him"], lambda: g.iota(T.him[:], [[1, 320]], 128, -1))
-    op("g", [], ["c16"], lambda: g.iota(T.c16[:], [[16, 20]], 0, 0, allow_small_or_imprecise_dtypes=True))
-    op("g", [], ["cio"], lambda: g.iota(T.cio[:], [[1, 320]], 0, 0, allow_small_or_imprecise_dtypes=True))
-    op("g", [], ["uoi"], lambda: g.iota(T.uoi[:], [[1, 2], [16, 8]], 0, 0))
-    op("g", [], ["alt"], lambda: g.iota(T.alt[:], [[0, 160], [1, 2]], 0, 0, allow_small_or_imprecise_dtypes=True))
-    op("g", [], ["cvm"], lambda: g.iota(T.cvm[:], [[0, 2], [1, 160]], 0, 0, allow_small_or_imprecise_dtypes=True))
-    op("g", [], ["dec"], lambda: g.iota(T.dec[:], [[1, 2], [2, 160]], 0, 0, allow_small_or_imprecise_dtypes=True))
+    op("g", [], ["i17"], lambda: g.iota(T.i17[:], [[0, 2]], 0, 17))
+    for name, pattern in (("c256", [[256, 4]]), ("c16", [[16, 20]]), ("j16", [[0, 20], [1, 16]]), ("cio", [[1, 320]]), ("alt", [[0, 160], [1, 2]])):
+        op("g", [], [name], lambda: g.iota(T[name][:], pattern, 0, 0, allow_small_or_imprecise_dtypes=True))
     op("v", [], ["one"], lambda: V.memset(T.one[:], 1.0))
+    op("v", [], ["nx0", "nx1"], lambda: V.memset(T.nx[:], 0.0))
+    op("v", [], ["kd0", "kd1"], lambda: V.memset(T.kd[:], 0.0))
+    op("v", [], ["k10", "k11"], lambda: V.memset(T.k1[:], 0.0))
     for b in range(4):
         op("g", ["one"], ["et%d" % b], lambda: g.affine_select(T.et[:, 512 * b:512 * b + 512], T.one[:], [[-1, 512]], A.is_equal, 0.0, b, 4))
-    op("v", ["pmi"], ["pma"], lambda: V.tensor_scalar(T.pma[:], T.pmi[:], 15, None, A.bitwise_and))
-    op("v", ["him"], ["hia"], lambda: V.tensor_scalar(T.hia[:], T.him[:], 15, None, A.bitwise_and))
-    op("v", ["pma"], ["sub"], lambda: V.tensor_scalar(T["sub"][:], T.pma[:, 0:1], -512.0, 7680.0, A.mult, A.add))
-    op("v", ["pma"], ["cs"], lambda: V.tensor_scalar(T.cs[:], T.pma[:, 0:1], -511.0, 7680.0, A.mult, A.add))
-    op("v", ["hia"], ["mk"], lambda: V.tensor_scalar(T.mk[:], T.hia[:], 0.0, -16896.0, A.is_equal, A.mult))
-    op("v", ["pma"], ["cp"], lambda: V.tensor_scalar(T.cp[:], T.pma[:, 0:1], -2.0, 30.0, A.mult, A.add))
-    op("v", ["pma"], ["cp2"], lambda: V.tensor_scalar(T.cp2[:], T.pma[:, 0:1], -4.0, 61.0, A.mult, A.add))
-    op("v", ["c16", "cs"], ["ciw"], lambda: V.tensor_scalar(T.ciw[:], T.c16[:], T.cs[:], None, A.add))
+    ts("pma", "pmi", 15, None, A.bitwise_and)
+    ts("s16", "i17", 16, None, A.bitwise_and)
+    for name, a, b in (("sub", -512.0, 7680.0), ("cs", -511.0, 7680.0), ("p16", 16.0, 0.0), ("pmf", 1.0, 0.0)):
+        ts(name, "pma", a, b, A.mult, A.add, to=(T[name][:], T.pma[:, 0:1]))
+    ts("s21", "s16", 21.0, None, A.mult, to=(T.s21[:], T.s16[:, 0:1]))
+    ts("n16", "c256", "p16", None, A.add)
+    ts("ciw", "c16", "cs", None, A.add)
+    ts("n24", "n16", 16.0 * K1, 1.0 - 16.0 * K1, A.is_ge, A.mult)
+    ts("mk", "j16", "pmf", -16896.0, A.is_equal, A.mult)
+    tt("n48", "n16", "n24", A.add)
     op("s", ["mk"], ["hold"], lambda: S.activation(T.hold[:], T.mk[:], AF.Copy, bias=512.0))
-    op("s", ["mk"], ["holdb"], lambda: S.activation(T.holdb[:], T.mk[:], AF.Copy, bias=2.0, scale=0.00390625))
+    ts("tof", "n48", "s21", 671.0, A.add, A.min)
 
     nsc = [0]
 
-    def wrap_scan(row, rtok):
-        nsc[0] += 1
-        b = ("sca", "scb")[nsc[0] % 2]
+    def wrap_scan(row, rtok, b=None):
+        if b is None:
+            nsc[0] += 1
+            b = ("sca", "scb")[nsc[0] % 2]
         op("v", [rtok, "hold"], [b], lambda: V.tensor_tensor_scan(T[b][:], T.hold[:], row, 0.0, A.add, A.max))
         return b
 
     def wrap_out(b, out, otok):
         op("v", [b, "sub"], [otok], lambda: V.tensor_scalar(out, T[b][:, 15:C:16], T["sub"][:], None, A.subtract))
 
-    def wrap(row, rtok, out, otok):
-        wrap_out(wrap_scan(row, rtok), out, otok)
-
-    def spread(name, off, otok, win="cio"):
-        op("s", [win, otok], [name], lambda: S.activation(T[name][:], pick(win, off), AF.Copy))
+    def spick(name, win, off, otok, a=0, n=C):
+        op("s", [win, otok], [name], lambda: S.activation(T[name][:], pick(win, off, a, n), AF.Copy))
 
     def scatter(n):
-        op("v", ["enc%d" % n, "cio"], ["pr%d" % n], lambda: V.tensor_copy(T["pr%d" % n][:, 0:C].indirect(lst("enc%d" % n)), T.cio[:]))
+        op("v", ["enc", "cio"], ["pr%d" % n], lambda: V.tensor_copy(T["pr%d" % n][:, 0:C].indirect(lst("enc", 20 * n, 20 * n + 20)), T.cio[:]))
 
     def vertices(n):
         b = wrap_scan(T["pr%d" % n][:], "pr%d" % n)
 
-        def rest():
-            op("v", [b], ["lo"], lambda: V.tensor_tensor(T.lohi[:, 0:10], T[b][:, 15:HC:16], T[b][:, HC + 15:C:16], A.min))
-            op("v", [b], ["hi"], lambda: V.tensor_tensor(T.lohi[:, 10:20], T[b][:, 15:HC:16], T[b][:, HC + 15:C:16], A.max))
-            op("v", ["lo", "hi", "sub"], ["lhu%d" % n], lambda: V.tensor_scalar(T["lhu%d" % n][:], T.lohi[:], T["sub"][:], None, A.subtract))
+        def rest(i):
+            if i == 0:
+                op("v", [b], ["lo"], lambda: V.tensor_tensor(T.lohi[:, 0:10], T[b][:, 15:HC:16], T[b][:, HC + 15:C:16], A.min))
+                op("v", [b], ["hi"], lambda: V.tensor_tensor(T.lohi[:, 10:20], T[b][:, 15:HC:16], T[b][:, HC + 15:C:16], A.max))
+            else:
+                op("v", ["lo", "hi", "sub"], ["lhu%d" % n], lambda: V.tensor_scalar(T["lhu%d" % n][:], T.lohi[:], T["sub"][:], None, A.subtract))
         return rest
 
-    def places(n, src, stok):
-        m = n % 2
-        op("v", [stok], ["hv%d" % m], lambda: V.tensor_copy(T["hv%d" % m][:], src))
-        op("v", [stok], ["hvs%d" % m], lambda: V.tensor_scalar(T["hvs%d" % m][:], src, 2.0, 1.0, A.mult, A.add))
-
-    def rows(n):
-        spread("lhr%d" % (n % 2), lst("lhu%d" % n), "lhu%d" % n)
+    def places(n):
+        src = T.hv[:, 20 * n:20 * n + 20]
+        op("v", ["hv"], ["hv%d" % n], lambda: V.tensor_copy(T["hv%d" % n][:], src))
+        op("v", ["hv"], ["hvs%d" % n], lambda: V.tensor_scalar(T["hvs%d" % n][:], src, 2.0, 1.0, A.mult, A.add))
 
     def role_pick(n):
-        m = n % 2
-        op("s", ["lhr%d" % m, "hv%d" % m], ["ajr"], lambda: S.activation(T.ajr[:], pick("lhr%d" % m, lst("hv%d" % m), 0, HC), AF.Copy))
+        if n < 2:
+            spick("ajr", "pr%d" % n, lst("sp", 20 * n, 20 * n + 20), "sp")
+        else:
+            spick("lor", "cio", lst("lhu%d" % n, 0, 10), "lhu%d" % n)
+            spick("ajr", "lor", lst("hv%d" % n), "hv%d" % n, 0, HC)
 
-    def role(n):
-        m = n % 2
-        b = wrap_scan(T.ajr[:], "ajr")
-        op("v", [b, "ciw"], ["rr"], lambda: V.tensor_tensor(T.rr[:], T[b][:, 15:C:16], T.ciw[:], A.not_equal))
-        op("v", ["rr"], ["g2%d" % m], lambda: V.tensor_scalar(T.g2[:, 20 * m:20 * m + 20], T.rr[:], 2.0, -1.0, A.mult, A.add))
-        op("v", ["rr", "cp", "cp2"], ["q2%d" % m], lambda: V.tensor_scalar(
-            T.q2[:, 20 * m:20 * m + 20], T.rr[:], T.cp2[:], T.cp[:], A.mult, A.subtract))
+    def role(i):
+        if i == 0:
+            wrap_scan(T.ajr[:], "ajr", "scr")
+        if i == 1:
+            op("v", ["scr", "ciw"], ["rr"], lambda: V.tensor_tensor(T.rr[:], T.scr[:, 15:C:16], T.ciw[:], A.is_lt))
+        if i == 2:
+            ts("g2", "rr", 2.0, -1.0, A.mult, A.add)
 
     def cand_pick(n):
-        i = (n - 1) % 2
         for h in (0, 1):
-            op("s", ["pr%d" % n, "hv%d" % i], ["kjr%d" % h], lambda: S.activation(
-                T.kjr[:, C * h:C * h + C], pick("pr%d" % n, lst("hv%d" % i), HC * h, HC), AF.Copy))
+            op("s", ["pr%d" % n, "hv%d" % (n - 1)], ["kjr%d" % h], lambda: S.activation(
+                T.kjr[:, C * h:C * h + C], pick("pr%d" % n, lst("hv%d" % (n - 1)), HC * h, HC), AF.Copy))
 
-    def cand_scan(n):
-        for h in (0, 1):
-            op("v", ["kjr%d" % h, "hold"], ["kjs%d" % h], lambda: V.tensor_tensor_scan(
-                T.kjs[:, C * h:C * h + C], T.hold[:], T.kjr[:, C * h:C * h + C], 0.0, A.add, A.max))
+    def cand_scan(h):
+        op("v", ["kjr%d" % h, "hold"], ["kjs%d" % h], lambda: V.tensor_tensor_scan(
+            T.kjs[:, C * h:C * h + C], T.hold[:], T.kjr[:, C * h:C * h + C], 0.0, A.add, A.max))
 
-    def cand(n):
-        i = (n - 1) % 2
+    def cand(i):
         a, b = T.kjs[:, 15:C:16], T.kjs[:, C + 15:2 * C:16]
-        op("v", ["kjs0", "kjs1"], ["kx"], lambda: V.tensor_tensor(T.kx[:], a, b, A.max))
-        op("v", ["kjs0", "kjs1"], ["kc"], lambda: V.tensor_tensor(T.kc[:], a, b, A.min))
-        op("v", ["kx", "kc"], ["ddc"], lambda: V.tensor_tensor(T.ddc[:], T.kx[:], T.kc[:], A.subtract))
+        if i == 0:
+            op("v", ["kjs0", "kjs1"], ["kx"], lambda: V.tensor_tensor(T.kx[:], a, b, A.max))
+            op("v", ["kjs0", "kjs1"], ["kc"], lambda: V.tensor_tensor(T.kc[:], a, b, A.min))
+        if i == 1:
+            tt("ddc", "kx", "kc", A.subtract)
+        if i == 2:
+            tt("kq", "ddc", "rr", A.mult)
+            for k in (0, 1):
+                op("v", ["ddc", "g2"], ["kd%d" % k], lambda: V.tensor_tensor(T.kd[:, K1 * k:K1 * k + 20], T.ddc[:], T.g2[:], A.mult))
+        if i == 3:
+            for k in (0, 1):
+                op("v", ["kx", "kq"], ["k1%d" % k], lambda: V.tensor_tensor(T.k1[:, K1 * k:K1 * k + 20], T.kx[:], T.kq[:], A.subtract))
 
-    def cand_b(n):
-        i = (n - 1) % 2
-        op("v", ["ddc", "q2%d" % i], ["kq"], lambda: V.tensor_tensor(T.kq[:], T.ddc[:], T.q2[:, 20 * i:20 * i + 20], A.mult))
-        op("v", ["ddc", "g2%d" % i], ["kd"], lambda: V.tensor_tensor(T.kd[:], T.ddc[:], T.g2[:, 20 * i:20 * i + 20], A.mult))
-        op("v", ["kx", "kq"], ["k1"], lambda: V.tensor_tensor(T.k1[:], T.kx[:], T.kq[:], A.subtract))
+    def quant_x(name, c, q="qx", s="sx"):
+        op("v", ["%s.%d" % (name, b) for b in range(4)], ["%s%d" % (q, c)], lambda: V.quantize_mx(
+            T[q][:, HC * c:HC * c + HC], T[s][:, HC * c:HC * c + HC], T[name][:, 640 * c:640 * c + 640]))
 
-    op("v", ["hlt"], ["hb"], lambda: V.tensor_scalar(T.hb[:], T.hlt[:], 1, None, A.bitwise_and))
-    op("v", ["hlt"], ["hv"], lambda: V.tensor_scalar(T.hv[:], T.hlt[:], 1, None, A.arith_shift_right))
-    op("v", ["hb"], ["hb2"], lambda: V.tensor_scalar(T.hb2[:], T.hb[:], 160, None, A.mult))
-    op("v", ["hb2", "hv"], ["enci"], lambda: V.tensor_tensor(T.enci[:], T.hb2[:], T.hv[:], A.add))
-    for n in (1, 0):
-        op("v", ["enci"], ["enc%d" % n], lambda: V.tensor_copy(T["enc%d" % n][:], T.enci[:, 20 * n:20 * n + 20]))
+    def plane(q, b, name):
+        out, in_ = T.xp[:, C * b:C * b + C], T[name][:, b:1280:4]
+        if q == "s":
+            op("s", ["%s.%d" % (name, b)], ["xp%d" % b], lambda: S.activation(out, in_, AF.Copy))
+        else:
+            op("g", ["%s.%d" % (name, b)], ["xp%d" % b], lambda: g.affine_select(out, in_, [[1, C]], A.is_ge, 0.0, 0, 0))
+
+    def evac(q, out, k, tok, scale=None):
+        toks = ["bk%d" % k, tok]
+        if q == "s":
+            op("s", [], toks, lambda: S.activation(out, bank(k, HC), AF.Copy, scale=scale or 1.0))
+        elif scale:
+            op("v", [], toks, lambda: V.tensor_scalar(out, bank(k, HC), scale, None, A.mult))
+        else:
+            op("v", [], toks, lambda: V.tensor_copy(out, bank(k, HC)))
+
+    def product(k, w, b, x, c, toks):
+        op("t", toks, ["bk%d" % k], lambda: P.matmul_mx(
+            bank(k, HC), T[w[0]][:, 128 * b:128 * b + 128], T[w[1]][:, 128 * b:128 * b + 128],
+            T[x[0]][:, HC * c:HC * c + HC], T[x[1]][:, HC * c:HC * c + HC], True, True))
+
+    def scores(qs):
+        for c in (0, 1):
+            product(c, ("qu", "su"), 0, ("qx", "sx"), c, ["qx%d" % c, "qu"])
+        for c in (0, 1):
+            evac(qs[c], T.sk[:, HC * c:HC * c + HC], c, "sk%d" % c)
+
+    def lower(i, w):
+        op("s", ["sk0", "sk1", w], ["ga%d" % i], lambda: S.activation(T.ga[:, HC * i:HC * i + HC], pick("sk", lst(w, 0, 10)), AF.Copy))
+
+    def higher(i, w):
+        op("v", ["sk0", "sk1", w, "ga%d" % i], ["bit%d" % i], lambda: V.tensor_tensor(
+            T.bit[:, i:C:2], pick("sk", lst(w, 10, 20)), T.ga[:, HC * i:HC * i + HC], A.is_gt))
+
+    ts("hb", "hlt", 1, None, A.bitwise_and)
+    ts("hv", "hlt", 1, None, A.arith_shift_right)
+    ts("hb2", "hb", HC, None, A.mult)
+    places(0)
+    tt("enci", "hb2", "hv", A.add)
+    tt("spi", "hv", "hb2", A.subtract)
+    op("v", ["enci"], ["enc"], lambda: V.tensor_copy(T.enc[:], T.enci[:]))
+    ts("sp", "spi", float(HC), None, A.add)
     scatter(1)
     fin = vertices(1)
-    places(0, T.hv[:, 0:20], "hv")
-    fin()
     op("v", ["ut"], ["qu"], lambda: V.quantize_mx(T.qu[:], T.su[:], T.ut[:]))
-    op("v", ["uoi"], ["uof"], lambda: V.tensor_copy(T.uof[:], T.uoi[:]))
-
-    def quant_x(name):
-        for c in (0, 1):
-            op("v", ["%s.%d" % (name, b) for b in range(4)], ["qx%d" % c], lambda: V.quantize_mx(
-                T.qx[:, HC * c:HC * c + HC], T.sx[:, HC * c:HC * c + HC], T[name][:, 640 * c:640 * c + 640]))
-
-    def plane(b, name):
-        op("s", ["%s.%d" % (name, b)], ["xp%d" % b], lambda: S.activation(T.xp[:, C * b:C * b + C], T[name][:, b:1280:4], AF.Copy))
-
-    quant_x("xi0")
-    for b in range(3):
-        plane(b, "xi0")
-    op("v", ["qu", "uof"], ["qu2"], lambda: V.tensor_copy(T.qu2[:].bitcast(dt.uint32), T.qu[:].bitcast(dt.uint32).indirect(T.uof[:])))
-    op("s", ["qu", "uof"], ["su2"], lambda: S.activation(T.su2[:], T.su[:].indirect(T.uof[:]), AF.Copy))
+    fin(0)
+    quant_x("xi0", 0)
+    fin(1)
+    quant_x("xi0", 1)
+    for b in range(2):
+        plane("s", b, "xi0")
     cand_pick(1)
-    rows(1)
     scatter(0)
-    vertices(0)()
-    rows(0)
+    scores("ss")
+    lower(1, "lhu1")
     role_pick(0)
+    fin = vertices(0)
+    higher(1, "lhu1")
+    fin(0)
+    cand_scan(0)
+    fin(1)
+    lower(0, "lhu0")
+    plane("s", 2, "xi0")
+    cand_scan(1)
+    higher(0, "lhu0")
 
     for r in (1, 2, 3):
         last = r == 3
@@ -281,109 +323,74 @@ def rank_program(g, core, T, topo):
         neng = len(topo.engines(core, peer))
         xo, xn = "xi%d" % ((r - 1) % 2), "xi%d" % (r % 2)
         ai, ao = "lhu%d" % (r - 1), "lhu%d" % r
+        hvs = "hvs%d" % (r - 1)
 
-        for k in (1, 0):
-            for c in (0, 1):
-                op("t", ["qx%d" % c, "qu2", "su2"], ["bk%d" % (2 * k + c)], lambda: P.matmul_mx(
-                    bank(2 * k + c, HC), T.qu2[:, 128 * k:128 * k + 128], T.su2[:, 128 * k:128 * k + 128],
-                    T.qx[:, HC * c:HC * c + HC], T.sx[:, HC * c:HC * c + HC], True, True))
-        for k in (1, 0):
-            for c in (0, 1):
-                out, in_, tok = T["sk%d" % k][:, HC * c:HC * c + HC], bank(2 * k + c, HC), ["bk%d" % (2 * k + c), "sk%d.%d" % (k, c)]
-                if r > 1 and (k, c) == (1, 0):
-                    op("s", [], tok, lambda: S.activation(out, in_, AF.Copy))
-                else:
-                    op("v", [], tok, lambda: V.tensor_copy(out, in_))
+        if r > 1:
+            scores("sv")
+            lower(0, ai)
+            lower(1, ao)
+            cand(0)
+            role(1)
+            cand(1)
+            role(2)
+            higher(0, ai)
+            higher(1, ao)
+        op("v", ["bit0", "bit1", "alt"], ["sum"], lambda: V.tensor_tensor_scan(T["sum"][:], T.alt[:], T.bit[:], 0.0, A.mult, A.add))
+        op("s", ["sum", hvs], ["nx0", "nx1"], lambda: S.activation(T.nx[:, 16:16 + C], pick("sum", lst(hvs)), AF.Square, bias=-1.0))
         if r == 1:
-            cand_scan(1)
-        cand(r)
-        for k in (1, 0):
-            sk, ga, bt = "sk%d" % k, "ga%d" % k, "bit%d" % k
-            for i, w in ((0, ai), (1, ao)):
-                op("s", [sk + ".0", sk + ".1", w], [ga + ".%d" % i], lambda: S.activation(
-                    T.ga[:, C * k + HC * i:C * k + HC * i + HC], pick(sk, lst(w, 0, 10)), AF.Copy))
-            for i, w in ((0, ai), (1, ao)):
-                op("v", [sk + ".0", sk + ".1", w, ga + ".%d" % i], [bt + ".%d" % i], lambda: V.tensor_tensor(
-                    T.bit[:, C * k + i:C * k + C:2], pick(sk, lst(w, 10, 20)), T.ga[:, C * k + HC * i:C * k + HC * i + HC], A.is_gt))
-            op("v", [bt + ".0", bt + ".1", "alt"], ["sum%d" % k], lambda: V.tensor_tensor_scan(
-                T["sum%d" % k][:], T.alt[:], T.bit[:, C * k:C * k + C], 0.0, A.mult, A.add))
-            if k == 1 and r == 1:
-                role(0)
+            role(0)
+            cand(0)
+            role(1)
+            cand(1)
+            role(2)
+            plane("s", 3, "xi0")
+        if r == 2:
+            hs = wrap_scan(T.tr[:], "tr")
+        cand(2)
+        if r == 2:
+            wrap_out(hs, T.hv2[:], "hv2")
+        cand(3)
         if r == 1:
-            places(1, T.hv[:, 20:40], "hv")
-        cand_b(r)
-        hvs = "hvs%d" % ((r - 1) % 2)
-        for k in (1, 0):
-            op("s", ["sum%d" % k, hvs], ["nx%d" % k], lambda: S.activation(T["nx%d" % k][:], pick("sum%d" % k, lst(hvs)), AF.Square, bias=-1.0))
-
-        if r == 1:
-            plane(3, "xi0")
+            role_pick(1)
+        if r == 2:
+            role_pick(2)
+        op("v", ["nx0", "nx1"], ["tt0"], lambda: V.transpose(T.tt[:, 0:C], T.nx[:, 16:16 + C]))
+        op("v", ["nx0", "nx1"], ["tt1"], lambda: V.transpose(T.tt[:, C:2 * C + 32], T.nx[:]))
+        op("v", ["tt0", "tt1", "tof", "kd0", "kd1"], ["mt"], lambda: V.tensor_tensor(T.mt[:], pick("tt", lst("tof", 0, 3), 0, 2 * C + 32), T.kd[:], A.mult))
+        op("v", ["mt", "k10", "k11"], ["mf"], lambda: V.tensor_tensor(T.mf[:], T.mt[:], T.k1[:], A.add))
+        ts("mw", "mf", "sub", None, A.subtract)
+        m0, m1 = lst("mw"), lst("mw", K1, K1 + 20)
 
         def yadd(b):
-            op("v", ["xp%d" % b, "%s.%d" % (xo, b), "mw1"], ["y%d" % b], lambda: V.tensor_tensor(
-                T.y32[:, C * b:C * b + C], pick("xp", lst("mw1"), C * b), T[xo][:, b:1280:4], A.add))
-
-        def move(k, i):
-            if i == 0:
-                op("v", ["nx%d" % k, "holdb"], ["w%d" % k], lambda: V.tensor_tensor_scan(T["w%d" % k][:], T.holdb[:], T["nx%d" % k][:], 0.0, A.add, A.max))
-            if i == 1:
-                op("v", ["w%d" % k, "kd"], ["mt%d" % k], lambda: V.tensor_tensor(T.mt[:, 20 * k:20 * k + 20], T["w%d" % k][:, 15:C:16], T.kd[:], A.mult))
-            if i == 2:
-                op("v", ["mt%d" % k, "k1"], ["mf%d" % k], lambda: V.tensor_tensor(T.mf[:, 20 * k:20 * k + 20], T.mt[:, 20 * k:20 * k + 20], T.k1[:], A.add))
-            if i == 3:
-                op("v", ["mf%d" % k, "sub"], ["mw%d" % k], lambda: V.tensor_scalar(
-                    T["mw%d" % k][:], T.mf[:, 20 * k:20 * k + 20], T["sub"][:], None, A.subtract))
+            op("v", ["xp%d" % b, "%s.%d" % (xo, b), "mw"], ["y%d" % b], lambda: V.tensor_tensor(
+                T.y32[:, C * b:C * b + C], pick("xp", m1, C * b), T[xo][:, b:1280:4], A.add))
 
         fw, fp = "fw%d" % r, "fp%d" % r
-        for k, i in ((1, 0), (1, 1), (1, 2), (0, 0), (1, 3), (0, 1), (0, 2), (0, 3)):
-            move(k, i)
+        spick("m1r", "cio", m1, "mw")
+        spick("fr", "m1r", m0, "mw")
         for b in (0, 1, 2):
             yadd(b)
-        spread("m1r", lst("mw1"), "mw1")
-
-        def pick_f():
-            op("s", ["m1r", "mw0"], ["fr"], lambda: S.activation(T.fr[:], pick("m1r", lst("mw0")), AF.Copy))
-
-        def send_f():
-            order("g", [fw], [])
-            g.remote_dma(T[fp][:], T[fw][:], T.sem["a%df" % r], T.sem.lsem, pid, rid, mask)
-            cnt["lsem"] = cnt.get("lsem", 0) + neng
-
-        def heads():
-            if r == 1:
-                role(1)
-            elif r == 2:
-                wrap(T.tr[:], "tr", T.hv0[:], "hv0")
-                op("v", ["hv0"], ["hvs0"], lambda: V.tensor_scalar(T.hvs0[:], T.hv0[:], 2.0, 1.0, A.mult, A.add))
-
-        pick_f()
-        wrap(T.fr[:], "fr", T[fw][:], fw)
-        send_f()
+        wrap_out(wrap_scan(T.fr[:], "fr"), T[fw][:], fw)
         yadd(3)
+        order("g", [fw], [])
+        g.remote_dma(T[fp][:], T[fw][:], T.sem["a%df" % r], T.sem.lsem, pid, rid, mask)
+        cnt["lsem"] = cnt.get("lsem", 0) + neng
 
         for b in range(3):
-            op("s", ["y%d" % b, "mw0"], ["z%d" % b], lambda: S.activation(T.zt[:, b:1280:4], pick("y32", lst("mw0"), C * b), AF.Copy, scale=0.5))
-        op("v", ["y3", "mw0"], ["z3"], lambda: V.tensor_scalar(T.zt[:, 3:640:4], pick("y32", lst("mw0", 0, 10), 3 * C), 0.5, None, A.mult))
-        op("s", ["y3", "mw0"], ["z4"], lambda: S.activation(T.zt[:, 643:1280:4], pick("y32", lst("mw0", 10, 20), 3 * C), AF.Copy, scale=0.5))
+            op("s", ["y%d" % b, "mw"], ["z%d" % b], lambda: S.activation(T.zt[:, b:1280:4], pick("y32", m0, C * b), AF.Copy, scale=0.5))
+        for c in (0, 1):
+            op("v", ["y3", "mw"], ["z%d" % (3 + c)], lambda: V.tensor_scalar(
+                T.zt[:, 640 * c + 3:640 * c + 640:4], pick("y32", lst("mw", 10 * c, 10 * c + 10), 3 * C), 0.5, None, A.mult))
+
         for c in (0, 1):
             op("v", ["z0", "z1", "z2", "z%d" % (3 + c)], ["qz%d" % c], lambda: V.quantize_mx(
                 T.qz[:, HC * c:HC * c + HC], T.sz[:, HC * c:HC * c + HC], T.zt[:, 640 * c:640 * c + 640]))
             for b in range(4):
-                op("t", ["qz%d" % c, "qw"], ["bk%d" % (4 * c + b)], lambda: P.matmul_mx(
-                    bank(4 * c + b, HC), T.qw[:, 128 * b:128 * b + 128], T.sw[:, 128 * b:128 * b + 128],
-                    T.qz[:, HC * c:HC * c + HC], T.sz[:, HC * c:HC * c + HC], True, True))
+                product(4 * c + b, ("qw", "sw"), b, ("qz", "sz"), c, ["qz%d" % c, "qw"])
         qh, sh, lc, ls = "qh%d" % r, "sh%d" % r, "lc%d" % r, "ls%d" % r
-        if r == 1:
-            role_pick(1)
         for c in (0, 1):
             for b in range(4):
-                if (c, b) == (0, 2):
-                    heads()
-                out = T.ht[:, 640 * c + b:640 * c + 640:4]
-                if b % 2 == 0:
-                    op("v", [], ["bk%d" % (4 * c + b), "h%d%d" % (c, b)], lambda: V.tensor_scalar(out, bank(4 * c + b, HC), 0.03125, None, A.mult))
-                else:
-                    op("s", [], ["bk%d" % (4 * c + b), "h%d%d" % (c, b)], lambda: S.activation(out, bank(4 * c + b, HC), AF.Copy, scale=0.03125))
+                evac(("svsv", "ssvs")[c][b], T.ht[:, 640 * c + b:640 * c + 640:4], 4 * c + b, "h%d%d" % (c, b), 0.03125)
             op("v", ["h%d%d" % (c, b) for b in range(4)], [qh + str(c)], lambda: V.quantize_mx(
                 T[qh][:, HC * c:HC * c + HC], T[sh][:, HC * c:HC * c + HC], T.ht[:, 640 * c:640 * c + 640]))
             order("g", [qh + str(c)], [])
@@ -398,69 +405,64 @@ def rank_program(g, core, T, topo):
             wrote["ld%d%d" % (r, c)] = {"a%dc%d" % (r, c): 2 * neng}
 
         n = r + 1
+        if r == 1:
+            spick("hvr", "cio", lst("hv0"), "hv0")
+            places(1)
+            role(0)
+            for b in range(4):
+                op("v", ["et%d" % b], ["qe%d" % b], lambda: V.quantize_mx(
+                    T.qe[:, 128 * b:128 * b + 128], T.se[:, 128 * b:128 * b + 128], T.et[:, 512 * b:512 * b + 512]))
+        spick("lr", "fr", lst(fp), fp)
         if not last:
             op("v", [fp, "cio"], ["fi"], lambda: V.tensor_copy(T.fi[:, 0:C].indirect(lst(fp)), T.cio[:]))
-            if r == 1:
-                for b in range(4):
-                    op("v", ["et%d" % b], ["qe%d" % b], lambda: V.quantize_mx(
-                        T.qe[:, 128 * b:128 * b + 128], T.se[:, 128 * b:128 * b + 128], T.et[:, 512 * b:512 * b + 512]))
-        else:
-            op("v", ["vt"], ["qv"], lambda: V.quantize_mx(T.qv[:], T.sv[:], T.vt[:]))
-        op("s", ["fr", fp], ["lr"], lambda: S.activation(T.lr[:], pick("fr", lst(fp)), AF.Copy))
-        if not last:
-            if r == 1:
-                op("s", ["cvm", "enc0"], ["hvr"], lambda: S.activation(T.hvr[:], pick("cvm", lst("enc0")), AF.Copy))
-            else:
-                rows(2)
-                role_pick(2)
-            op("s", ["fi", "lhu%d" % (r - 1)], ["pr%d" % n], lambda: S.activation(T["pr%d" % n][:], pick("fi", lst("lhu%d" % (r - 1))), AF.Copy))
-            wrap(T.lr[:], "lr", T.lw[:], "lw")
-            vertices(n)()
+            spick("pr%d" % n, "fi", lst("lhu%d" % (r - 1)), "lhu%d" % (r - 1))
+            ws = wrap_scan(T.lr[:], "lr")
+            if r == 2:
+                ts("hvs2", "hv2", 2.0, 1.0, A.mult, A.add)
+            wrap_out(ws, T.lw[:], "lw")
+            fin = vertices(n)
             cand_pick(n)
             if r == 2:
-                role(2)
-            cand_scan(n)
+                role(0)
+            fin(0)
+            fin(1)
+            cand_scan(0)
+            cand_scan(1)
+            if r == 1:
+                spick("tr", "hvr", lst(fp), fp)
         else:
-            spread("raw0", lst("enc0"), "enc0", "dec")
-            spread("raw2", lst("fp1"), "fp1", "raw0")
-            wrap(T.lr[:], "lr", T.lw[:], "lw")
-            op("s", ["raw2", fp], ["tpr"], lambda: S.activation(T.tpr[:], pick("raw2", lst(fp)), AF.Copy))
+            op("v", ["hlt"], ["hu"], lambda: V.tensor_copy(T.hu[:], T.hlt[:, 0:20]))
+            op("v", ["vt"], ["qv"], lambda: V.quantize_mx(T.qv[:], T.sv[:], T.vt[:]))
+            spick("raw0", "cio", lst("hu"), "hu")
+            spick("raw2", "raw0", lst("fp1"), "fp1")
+            wrap_out(wrap_scan(T.lr[:], "lr"), T.lw[:], "lw")
+            spick("tpr", "raw2", lst(fp), fp)
             dma("y", "ot", T.tp[:], T.tpr[0:128:16, :], rd=["tpr"])
 
-        if r == 1:
-            op("s", ["hvr", fp], ["tr"], lambda: S.activation(T.tr[:], pick("hvr", lst(fp)), AF.Copy))
         for c in (0, 1):
             for b in range(4):
-                op("t", ["ld%d%d" % (r, c), "qe%d" % b], ["bk%d" % (4 * c + b)], lambda: P.matmul_mx(
-                    bank(4 * c + b, HC), T.qe[:, 128 * b:128 * b + 128], T.se[:, 128 * b:128 * b + 128],
-                    T[lc][:, HC * c:HC * c + HC], T[ls][:, HC * c:HC * c + HC], True, True))
+                product(4 * c + b, ("qe", "se"), b, (lc, ls), c, ["ld%d%d" % (r, c), "qe%d" % b])
             for b in range(4):
-                out = T.dd[:, C * b + HC * c:C * b + HC * c + HC]
-                if b == 0 and c == 1:
-                    op("v", [], ["bk%d" % (4 * c + b), "d%d%d" % (c, b)], lambda: V.tensor_copy(out, bank(4 * c + b, HC)))
-                else:
-                    op("s", [], ["bk%d" % (4 * c + b), "d%d%d" % (c, b)], lambda: S.activation(out, bank(4 * c + b, HC), AF.Copy))
+                evac(("ssss", "vsss")[c][b], T.dd[:, C * b + HC * c:C * b + HC * c + HC], 4 * c + b, "d%d%d" % (c, b))
         for b in range(4):
             op("v", ["d0%d" % b, "d1%d" % b, "lw", "%s.%d" % (xo, b)], ["%s.%d" % (xn, b)], lambda: V.tensor_tensor(
                 T[xn][:, b:1280:4], pick("dd", lst("lw"), C * b), T[xo][:, b:1280:4], A.add))
-        toks = ["%s.%d" % (xn, b) for b in range(4)]
+        for c in (0, 1):
+            if last:
+                quant_x(xn, c, "qo", "so")
+            else:
+                quant_x(xn, c)
         if not last:
-            quant_x(xn)
             for b in range(4):
-                plane(b, xn)
-        else:
-            for c in (0, 1):
-                op("v", toks, ["qo%d" % c], lambda: V.quantize_mx(
-                    T.qo[:, HC * c:HC * c + HC], T.so[:, HC * c:HC * c + HC], T[xn][:, 640 * c:640 * c + 640]))
+                plane("g", b, xn)
 
     dma("y", "oq", T.oc[:], T.qo[:].bitcast(dt.uint8), rd=["qo0", "qo1"], total=80)
     for k in range(4):
         dma("y", "oq", T.osc[4 * k:4 * k + 4, :], T.so[32 * k:32 * k + 4, :], rd=["qo0", "qo1"], total=80)
     for c in (0, 1):
-        op("t", ["qo%d" % c, "qv"], ["bk%d" % c], lambda: P.matmul_mx(
-            bank(c, HC), T.qv[:], T.sv[:], T.qo[:, HC * c:HC * c + HC], T.so[:, HC * c:HC * c + HC], True, True))
-    op("v", [], ["bk0", "yo0"], lambda: V.tensor_copy(T.yo[:, 0:HC], bank(0, HC)))
-    op("s", [], ["bk1", "yo1"], lambda: S.activation(T.yo[:, HC:C], bank(1, HC), AF.Copy))
+        product(c, ("qv", "sv"), 0, ("qo", "so"), c, ["qo%d" % c, "qv"])
+    for c in (0, 1):
+        evac("vs"[c], T.yo[:, HC * c:HC * c + HC], c, "yo%d" % c)
     for c in (0, 1):
         dma("s", "oy", T.y[:, HC * c:HC * c + HC], T.yo[:, HC * c:HC * c + HC], rd=["yo%d" % c], total=32)
     for sem in sorted(cnt):

@@ -8,6 +8,22 @@ STEP = [1, 2, 4]
 CODE = "float8_e4m3fn_x4"
 K1 = 24
 
+LAYER = "m1r fr y0 y1 y2 fs y3 f zs00 zs01 zs02 zv03 l0 zs10 zs11 zs12 zs13 l1 %s hv00 hs01 hv02 hs03 send0 hs10 hv11 hs12 hv13 send1"
+MEET = "u0 ds00 ds01 ds02 ds03 u1 dv10 ds11 ds12 ds13"
+OPT = {
+    "a1": "enc scat1 qu vs1 q0 vm1 q1 vc1 pg et mm es0 es1 row1 scat0 lo rp0 kp0 vs0 ho vm0 rs vc0 li kp1 ks0 rr hi g2v sum nx "
+          "ks1 dd kq kd k1 rp1 turn heads1 gm ad mw",
+    "b1": (LAYER % "rs").replace("send0", "qe0 send0").replace("send1", "qe1 send1"),
+    "c1": "qe2 qe3 lr hvr fi ls lw pr2 vs2 vm2 vc2 " + MEET + " row2 kp0 kp1 tr a0 a1 a2 a3",
+    "a2": "q0 q1 pg mm es0 es1 ks0 ks1 li lo rr dd g2 hi ho sum nx kq kd k1 hs turn hw rp2 gm hvs ad mw",
+    "b2": LAYER % "rs",
+    "c2": "lr fi pr3 ls lw vs3 vm3 vc3 " + MEET + " row3 kp0 kp1 a0 a1 a2 a3",
+    "a3": "q0 q1 pg mm es0 es1 ks0 ks1 li lo rr dd g2 hi ho sum nx kq kd k1 turn gm ad mw",
+    "b3": LAYER % "",
+    "c3": "lr hu qv raw ls lw tp " + MEET + " a00 a01 a02 a03 o0 oc0 ym0 es0 oy0 a10 a11 a12 a13 o1 ym1 oc1 os ev1 oy1",
+    "oq": 96,
+}
+
 SCRATCH = {
     "cio": ("sbuf", [128, 320], "float32"), "j16": ("sbuf", [128, 320], "bfloat16"), "mk": ("sbuf", [128, 320], "float32"),
     "hold": ("sbuf", [128, 320], "float32"), "alt": ("sbuf", [128, 320], "bfloat16"),
@@ -38,21 +54,23 @@ SCRATCH = {
     "kd": ("sbuf", [128, 48], "float32"), "k1": ("sbuf", [128, 48], "float32"),
     "mt": ("sbuf", [128, 48], "float32"), "mf": ("sbuf", [128, 48], "float32"), "mw": ("sbuf", [128, 48], "uint16"),
     "fi": ("sbuf", [128, 320], "float32"), "g2": ("sbuf", [128, 20], "float32"), "rr": ("sbuf", [128, 20], "float32"),
-    "sca": ("sbuf", [128, 320], "float32"), "scb": ("sbuf", [128, 320], "float32"), "scr": ("sbuf", [128, 320], "float32"),
     "m1r": ("sbuf", [128, 320], "float32"), "fr": ("sbuf", [128, 320], "float32"), "lr": ("sbuf", [128, 320], "float32"),
     "lw": ("sbuf", [128, 20], "uint16"), "ajr": ("sbuf", [128, 320], "float32"),
     "kjr": ("sbuf", [128, 640], "float32"), "kjs": ("sbuf", [128, 640], "float32"),
     "ddc": ("sbuf", [128, 20], "float32"), "kq": ("sbuf", [128, 20], "float32"),
-    "kx": ("sbuf", [128, 20], "float32"), "kc": ("sbuf", [128, 20], "float32"),
-    "tr": ("sbuf", [128, 320], "float32"), "hvr": ("sbuf", [128, 320], "float32"), "lor": ("sbuf", [128, 160], "float32"),
+    "tr": ("sbuf", [128, 320], "float32"), "hvr": ("sbuf", [128, 320], "float32"),
     "raw0": ("sbuf", [128, 320], "float32"), "raw2": ("sbuf", [128, 320], "float32"),
     "lohi": ("sbuf", [128, 20], "float32"),
 }
+for _n in ("v", "r", "h", "f", "l"):
+    SCRATCH["sc" + _n] = ("sbuf", [128, 320], "float32")
 for _k in (0, 1):
     SCRATCH["xi%d" % _k] = ("sbuf", [128, 1280], "bfloat16")
 for _n in range(4):
     SCRATCH["pr%d" % _n] = ("sbuf", [128, 320], "float32")
     SCRATCH["lhu%d" % _n] = ("sbuf", [128, 20], "uint16")
+    if _n > 0:
+        SCRATCH["row%d" % _n] = ("sbuf", [128, 320], "float32")
     if _n < 3:
         SCRATCH["hvs%d" % _n] = ("sbuf", [128, 20], "uint16")
         SCRATCH["hv%d" % _n] = ("sbuf", [128, 20], "uint16")
@@ -141,9 +159,15 @@ def rank_program(g, core, T, topo):
     def tt(out, in0, in1, o):
         op("v", [in0, in1], [out], lambda: V.tensor_tensor(T[out][:], T[in0][:], T[in1][:], o))
 
+    def affine(out, in_, scale, bias):
+        if isinstance(bias, str):
+            op("s", [in_, bias], [out], lambda: S.activation(T[out][:], T[in_][:], AF.Identity, bias=T[bias][:], scale=scale))
+        else:
+            op("s", [in_], [out], lambda: S.activation(T[out][:], T[in_][:], AF.Copy, bias=bias, scale=scale))
+
     dma("s", "dl", T.hlt[:, 0:20], T.hl[:], wr=["hlt"], total=32)
     dma("y", "dl", T.hlt[:, 20:40], T.tl[:], total=32)
-    dma("y", "dx", T.xi0[:], T.x[:], wr=["xi0.%d" % b for b in range(4)])
+    dma("y", "dx", T.xi0[:], T.x[:], wr=["x0.%d%d" % (c, b) for c in (0, 1) for b in range(4)])
     dma("s", "du", T.ut[:], T.u[:], wr=["ut"])
     dma("y", "dw", T.qw[:].bitcast(dt.uint8), T.wc[:], wr=["qw"], total=32)
     dma("y", "dw", T.sw[:], T.ws[:], total=32)
@@ -151,110 +175,73 @@ def rank_program(g, core, T, topo):
 
     op("g", [], ["pmi"], lambda: g.iota(T.pmi[:], [[0, 2]], 0, 1))
     op("g", [], ["i17"], lambda: g.iota(T.i17[:], [[0, 2]], 0, 17))
-    for name, pattern in (("c256", [[256, 4]]), ("c16", [[16, 20]]), ("j16", [[0, 20], [1, 16]]), ("cio", [[1, 320]]), ("alt", [[0, 160], [1, 2]])):
+    for name, pattern in (("c256", [[256, 4]]), ("j16", [[0, 20], [1, 16]]), ("cio", [[1, 320]]), ("c16", [[16, 20]]), ("alt", [[0, 160], [1, 2]])):
         op("g", [], [name], lambda: g.iota(T[name][:], pattern, 0, 0, allow_small_or_imprecise_dtypes=True))
     op("v", [], ["one"], lambda: V.memset(T.one[:], 1.0))
-    op("v", [], ["nx0", "nx1"], lambda: V.memset(T.nx[:], 0.0))
-    op("v", [], ["kd0", "kd1"], lambda: V.memset(T.kd[:], 0.0))
-    op("v", [], ["k10", "k11"], lambda: V.memset(T.k1[:], 0.0))
-    for b in range(4):
-        op("g", ["one"], ["et%d" % b], lambda: g.affine_select(T.et[:, 512 * b:512 * b + 512], T.one[:], [[-1, 512]], A.is_equal, 0.0, b, 4))
     ts("pma", "pmi", 15, None, A.bitwise_and)
     ts("s16", "i17", 16, None, A.bitwise_and)
-    for name, a, b in (("sub", -512.0, 7680.0), ("cs", -511.0, 7680.0), ("p16", 16.0, 0.0), ("pmf", 1.0, 0.0)):
-        ts(name, "pma", a, b, A.mult, A.add, to=(T[name][:], T.pma[:, 0:1]))
+    op("v", [], ["nx0", "nx1"], lambda: V.memset(T.nx[:], 0.0))
+    ts("pmf", "pma", 1.0, None, A.mult, to=(T.pmf[:], T.pma[:, 0:1]))
     ts("s21", "s16", 21.0, None, A.mult, to=(T.s21[:], T.s16[:, 0:1]))
-    ts("n16", "c256", "p16", None, A.add)
-    ts("ciw", "c16", "cs", None, A.add)
-    ts("n24", "n16", 16.0 * K1, 1.0 - 16.0 * K1, A.is_ge, A.mult)
+    op("v", [], ["kd0", "kd1"], lambda: V.memset(T.kd[:], 0.0))
+    op("v", [], ["k10", "k11"], lambda: V.memset(T.k1[:], 0.0))
     ts("mk", "j16", "pmf", -16896.0, A.is_equal, A.mult)
-    tt("n48", "n16", "n24", A.add)
-    op("s", ["mk"], ["hold"], lambda: S.activation(T.hold[:], T.mk[:], AF.Copy, bias=512.0))
-    ts("tof", "n48", "s21", 671.0, A.add, A.min)
+    for name, a, b in (("p16", 16.0, 0.0), ("sub", -512.0, 7680.0), ("cs", -511.0, 7680.0)):
+        affine(name, "pmf", a, b)
+    affine("n16", "c256", 1.0, "p16")
+    affine("hold", "mk", 1.0, 512.0)
+    affine("ciw", "c16", 1.0, "cs")
 
-    nsc = [0]
+    def scan(b, row):
+        op("v", [row, "hold"], [b], lambda: V.tensor_tensor_scan(T[b][:], T.hold[:], T[row][:], 0.0, A.add, A.max))
 
-    def wrap_scan(row, rtok, b=None):
-        if b is None:
-            nsc[0] += 1
-            b = ("sca", "scb")[nsc[0] % 2]
-        op("v", [rtok, "hold"], [b], lambda: V.tensor_tensor_scan(T[b][:], T.hold[:], row, 0.0, A.add, A.max))
-        return b
+    def wrapped(out, b):
+        op("v", [b, "sub"], [out], lambda: V.tensor_scalar(T[out][:], T[b][:, 15:C:16], T["sub"][:], None, A.subtract))
 
-    def wrap_out(b, out, otok):
-        op("v", [b, "sub"], [otok], lambda: V.tensor_scalar(out, T[b][:, 15:C:16], T["sub"][:], None, A.subtract))
+    def spick(name, win, off, a=0, b=20, n=C):
+        op("s", [win, off], [name], lambda: S.activation(T[name][:], pick(win, lst(off, a, b), 0, n), AF.Copy))
 
-    def spick(name, win, off, otok, a=0, n=C):
-        op("s", [win, otok], [name], lambda: S.activation(T[name][:], pick(win, off, a, n), AF.Copy))
+    def places():
+        ts("hb", "hlt", 1, None, A.bitwise_and)
+        ts("hv", "hlt", 1, None, A.arith_shift_right)
+        ts("n24", "n16", 16.0 * K1, 1.0 - 16.0 * K1, A.is_ge, A.mult)
+        ts("hb2", "hb", HC, None, A.mult)
+        heads(0)
+        tt("enci", "hb2", "hv", A.add)
+        tt("spi", "hv", "hb2", A.subtract)
+        tt("n48", "n16", "n24", A.add)
+        op("v", ["enci"], ["enc"], lambda: V.tensor_copy(T.enc[:], T.enci[:]))
+        ts("sp", "spi", float(HC), None, A.add)
+        ts("tof", "n48", "s21", 671.0, A.add, A.min)
+
+    def units():
+        for b in range(4):
+            op("g", ["one"], ["et%d" % b], lambda: g.affine_select(T.et[:, 512 * b:512 * b + 512], T.one[:], [[-1, 512]], A.is_equal, 0.0, b, 4))
 
     def scatter(n):
         op("v", ["enc", "cio"], ["pr%d" % n], lambda: V.tensor_copy(T["pr%d" % n][:, 0:C].indirect(lst("enc", 20 * n, 20 * n + 20)), T.cio[:]))
 
-    def vertices(n):
-        b = wrap_scan(T["pr%d" % n][:], "pr%d" % n)
+    def sort2(n):
+        op("v", ["scv"], ["lo"], lambda: V.tensor_tensor(T.lohi[:, 0:10], T.scv[:, 15:HC:16], T.scv[:, HC + 15:C:16], A.min))
+        op("v", ["scv"], ["hi"], lambda: V.tensor_tensor(T.lohi[:, 10:20], T.scv[:, 15:HC:16], T.scv[:, HC + 15:C:16], A.max))
 
-        def rest(i):
-            if i == 0:
-                op("v", [b], ["lo"], lambda: V.tensor_tensor(T.lohi[:, 0:10], T[b][:, 15:HC:16], T[b][:, HC + 15:C:16], A.min))
-                op("v", [b], ["hi"], lambda: V.tensor_tensor(T.lohi[:, 10:20], T[b][:, 15:HC:16], T[b][:, HC + 15:C:16], A.max))
-            else:
-                op("v", ["lo", "hi", "sub"], ["lhu%d" % n], lambda: V.tensor_scalar(T["lhu%d" % n][:], T.lohi[:], T["sub"][:], None, A.subtract))
-        return rest
+    def sorted_list(n):
+        op("v", ["lo", "hi", "sub"], ["lhu%d" % n], lambda: V.tensor_scalar(T["lhu%d" % n][:], T.lohi[:], T["sub"][:], None, A.subtract))
 
-    def places(n):
+    def heads(n):
         src = T.hv[:, 20 * n:20 * n + 20]
         op("v", ["hv"], ["hv%d" % n], lambda: V.tensor_copy(T["hv%d" % n][:], src))
         op("v", ["hv"], ["hvs%d" % n], lambda: V.tensor_scalar(T["hvs%d" % n][:], src, 2.0, 1.0, A.mult, A.add))
 
     def role_pick(n):
         if n < 2:
-            spick("ajr", "pr%d" % n, lst("sp", 20 * n, 20 * n + 20), "sp")
+            spick("ajr", "pr%d" % n, "sp", 20 * n, 20 * n + 20)
         else:
-            spick("lor", "cio", lst("lhu%d" % n, 0, 10), "lhu%d" % n)
-            spick("ajr", "lor", lst("hv%d" % n), "hv%d" % n, 0, HC)
+            spick("ajr", "row%d" % n, "hv%d" % n, n=HC)
 
-    def role(i):
-        if i == 0:
-            wrap_scan(T.ajr[:], "ajr", "scr")
-        if i == 1:
-            op("v", ["scr", "ciw"], ["rr"], lambda: V.tensor_tensor(T.rr[:], T.scr[:, 15:C:16], T.ciw[:], A.is_lt))
-        if i == 2:
-            ts("g2", "rr", 2.0, -1.0, A.mult, A.add)
-
-    def cand_pick(n):
-        for h in (0, 1):
-            op("s", ["pr%d" % n, "hv%d" % (n - 1)], ["kjr%d" % h], lambda: S.activation(
-                T.kjr[:, C * h:C * h + C], pick("pr%d" % n, lst("hv%d" % (n - 1)), HC * h, HC), AF.Copy))
-
-    def cand_scan(h):
-        op("v", ["kjr%d" % h, "hold"], ["kjs%d" % h], lambda: V.tensor_tensor_scan(
-            T.kjs[:, C * h:C * h + C], T.hold[:], T.kjr[:, C * h:C * h + C], 0.0, A.add, A.max))
-
-    def cand(i):
-        a, b = T.kjs[:, 15:C:16], T.kjs[:, C + 15:2 * C:16]
-        if i == 0:
-            op("v", ["kjs0", "kjs1"], ["kx"], lambda: V.tensor_tensor(T.kx[:], a, b, A.max))
-            op("v", ["kjs0", "kjs1"], ["kc"], lambda: V.tensor_tensor(T.kc[:], a, b, A.min))
-        if i == 1:
-            tt("ddc", "kx", "kc", A.subtract)
-        if i == 2:
-            tt("kq", "ddc", "rr", A.mult)
-            for k in (0, 1):
-                op("v", ["ddc", "g2"], ["kd%d" % k], lambda: V.tensor_tensor(T.kd[:, K1 * k:K1 * k + 20], T.ddc[:], T.g2[:], A.mult))
-        if i == 3:
-            for k in (0, 1):
-                op("v", ["kx", "kq"], ["k1%d" % k], lambda: V.tensor_tensor(T.k1[:, K1 * k:K1 * k + 20], T.kx[:], T.kq[:], A.subtract))
-
-    def quant_x(name, c, q="qx", s="sx"):
-        op("v", ["%s.%d" % (name, b) for b in range(4)], ["%s%d" % (q, c)], lambda: V.quantize_mx(
-            T[q][:, HC * c:HC * c + HC], T[s][:, HC * c:HC * c + HC], T[name][:, 640 * c:640 * c + 640]))
-
-    def plane(q, b, name):
-        out, in_ = T.xp[:, C * b:C * b + C], T[name][:, b:1280:4]
-        if q == "s":
-            op("s", ["%s.%d" % (name, b)], ["xp%d" % b], lambda: S.activation(out, in_, AF.Copy))
-        else:
-            op("g", ["%s.%d" % (name, b)], ["xp%d" % b], lambda: g.affine_select(out, in_, [[1, C]], A.is_ge, 0.0, 0, 0))
+    def both(name, in0, t0, in1, t1, o):
+        for k in (0, 1):
+            op("v", [t0, t1], ["%s%d" % (name, k)], lambda: V.tensor_tensor(T[name][:, K1 * k:K1 * k + 20], in0, in1, o))
 
     def evac(q, out, k, tok, scale=None):
         toks = ["bk%d" % k, tok]
@@ -270,200 +257,190 @@ def rank_program(g, core, T, topo):
             bank(k, HC), T[w[0]][:, 128 * b:128 * b + 128], T[w[1]][:, 128 * b:128 * b + 128],
             T[x[0]][:, HC * c:HC * c + HC], T[x[1]][:, HC * c:HC * c + HC], True, True))
 
-    def scores(qs):
-        for c in (0, 1):
-            product(c, ("qu", "su"), 0, ("qx", "sx"), c, ["qx%d" % c, "qu"])
-        for c in (0, 1):
-            evac(qs[c], T.sk[:, HC * c:HC * c + HC], c, "sk%d" % c)
+    def quantise(q, s, tile, c, toks):
+        op("v", toks, ["%s.%d" % (q, c)], lambda: V.quantize_mx(
+            T[q][:, HC * c:HC * c + HC], T[s][:, HC * c:HC * c + HC], T[tile][:, 640 * c:640 * c + 640]))
 
-    def lower(i, w):
-        op("s", ["sk0", "sk1", w], ["ga%d" % i], lambda: S.activation(T.ga[:, HC * i:HC * i + HC], pick("sk", lst(w, 0, 10)), AF.Copy))
-
-    def higher(i, w):
-        op("v", ["sk0", "sk1", w, "ga%d" % i], ["bit%d" % i], lambda: V.tensor_tensor(
-            T.bit[:, i:C:2], pick("sk", lst(w, 10, 20)), T.ga[:, HC * i:HC * i + HC], A.is_gt))
-
-    ts("hb", "hlt", 1, None, A.bitwise_and)
-    ts("hv", "hlt", 1, None, A.arith_shift_right)
-    ts("hb2", "hb", HC, None, A.mult)
-    places(0)
-    tt("enci", "hb2", "hv", A.add)
-    tt("spi", "hv", "hb2", A.subtract)
-    op("v", ["enci"], ["enc"], lambda: V.tensor_copy(T.enc[:], T.enci[:]))
-    ts("sp", "spi", float(HC), None, A.add)
-    scatter(1)
-    fin = vertices(1)
-    op("v", ["ut"], ["qu"], lambda: V.quantize_mx(T.qu[:], T.su[:], T.ut[:]))
-    fin(0)
-    quant_x("xi0", 0)
-    fin(1)
-    quant_x("xi0", 1)
-    for b in range(2):
-        plane("s", b, "xi0")
-    cand_pick(1)
-    scatter(0)
-    scores("ss")
-    lower(1, "lhu1")
-    role_pick(0)
-    fin = vertices(0)
-    higher(1, "lhu1")
-    fin(0)
-    cand_scan(0)
-    fin(1)
-    lower(0, "lhu0")
-    plane("s", 2, "xi0")
-    cand_scan(1)
-    higher(0, "lhu0")
+    def runs(c):
+        return (0, 2) if c == 2 else (c, 1)
 
     for r in (1, 2, 3):
-        last = r == 3
         peer = T.cores[rank ^ STEP[r - 1]]
         rid, pid = topo.addr(peer)[0], topo.addr(peer)[1]
         mask = topo.mask(core, peer)
         neng = len(topo.engines(core, peer))
         xo, xn = "xi%d" % ((r - 1) % 2), "xi%d" % (r % 2)
-        ai, ao = "lhu%d" % (r - 1), "lhu%d" % r
-        hvs = "hvs%d" % (r - 1)
+        to, tn = "x%d.%%d%%d" % (r - 1), "x%d.%%d%%d" % r
+        ai, ao, hv, hvs = "lhu%d" % (r - 1), "lhu%d" % r, "hv%d" % (r - 1), "hvs%d" % (r - 1)
+        fw, fp, qh, sh, lc, ls = ["%s%d" % (w, r) for w in ("fw", "fp", "qh", "sh", "lc", "ls")]
+        m1 = lst("mw", K1, K1 + 20)
+        lo_out, hi_out = T.kjs[:, 15:C:16], T.kjs[:, C + 15:2 * C:16]
+        wrote[fp] = {"a%df" % r: neng}
+        cnt["a%df" % r] = neng
+        for c in (0, 1):
+            wrote["ld%d" % c] = {"a%dc%d" % (r, c): 2 * neng}
+            cnt["a%dc%d" % (r, c)] = 2 * neng
 
-        if r > 1:
-            scores("sv")
-            lower(0, ai)
-            lower(1, ao)
-            cand(0)
-            role(1)
-            cand(1)
-            role(2)
-            higher(0, ai)
-            higher(1, ao)
-        op("v", ["bit0", "bit1", "alt"], ["sum"], lambda: V.tensor_tensor_scan(T["sum"][:], T.alt[:], T.bit[:], 0.0, A.mult, A.add))
-        op("s", ["sum", hvs], ["nx0", "nx1"], lambda: S.activation(T.nx[:, 16:16 + C], pick("sum", lst(hvs)), AF.Square, bias=-1.0))
-        if r == 1:
-            role(0)
-            cand(0)
-            role(1)
-            cand(1)
-            role(2)
-            plane("s", 3, "xi0")
-        if r == 2:
-            hs = wrap_scan(T.tr[:], "tr")
-        cand(2)
-        if r == 2:
-            wrap_out(hs, T.hv2[:], "hv2")
-        cand(3)
-        if r == 1:
-            role_pick(1)
-        if r == 2:
-            role_pick(2)
-        op("v", ["nx0", "nx1"], ["tt0"], lambda: V.transpose(T.tt[:, 0:C], T.nx[:, 16:16 + C]))
-        op("v", ["nx0", "nx1"], ["tt1"], lambda: V.transpose(T.tt[:, C:2 * C + 32], T.nx[:]))
-        op("v", ["tt0", "tt1", "tof", "kd0", "kd1"], ["mt"], lambda: V.tensor_tensor(T.mt[:], pick("tt", lst("tof", 0, 3), 0, 2 * C + 32), T.kd[:], A.mult))
-        op("v", ["mt", "k10", "k11"], ["mf"], lambda: V.tensor_tensor(T.mf[:], T.mt[:], T.k1[:], A.add))
-        ts("mw", "mf", "sub", None, A.subtract)
-        m0, m1 = lst("mw"), lst("mw", K1, K1 + 20)
+        def plane(q, b):
+            out, in_, toks = T.xp[:, C * b:C * b + C], T[xo][:, b:1280:4], [to % (c, b) for c in (0, 1)]
+            if q == "s":
+                op("s", toks, ["xp%d" % b], lambda: S.activation(out, in_, AF.Copy))
+            else:
+                op("g", toks, ["xp%d" % b], lambda: g.affine_select(out, in_, [[1, C]], A.is_ge, 0.0, 0, 0))
+
+        def lower(i, w):
+            op("s", ["sk0", "sk1", w], ["ga%d" % i], lambda: S.activation(T.ga[:, HC * i:HC * i + HC], pick("sk", lst(w, 0, 10)), AF.Copy))
+
+        def higher(i, w):
+            op("v", ["sk0", "sk1", w, "ga%d" % i], ["bit%d" % i], lambda: V.tensor_tensor(
+                T.bit[:, i:C:2], pick("sk", lst(w, 10, 20)), T.ga[:, HC * i:HC * i + HC], A.is_gt))
+
+        def straight(q, c):
+            a, n = runs(c)
+            out, in_ = T.nx[:, 16 + HC * a:16 + HC * (a + n)], pick("sum", lst(hvs, 10 * a, 10 * (a + n)))
+            toks = ["nx%d" % (a + i) for i in range(n)]
+            if q == "s":
+                op("s", ["sum", hvs], toks, lambda: S.activation(out, in_, AF.Square, bias=-1.0))
+            else:
+                op("v", ["sum", hvs], toks, lambda: V.tensor_scalar(out, in_, 1.0, None, A.not_equal))
+
+        def turn():
+            op("v", ["nx0", "nx1"], ["tt0"], lambda: V.transpose(T.tt[:, 0:C], T.nx[:, 16:16 + C]))
+            op("v", ["nx0", "nx1"], ["tt1"], lambda: V.transpose(T.tt[:, C:2 * C + 32], T.nx[:]))
+
+        def cand_pick(h, n):
+            op("s", ["row%d" % n, "hv%d" % (n - 1)], ["kjr%d" % h], lambda: S.activation(
+                T.kjr[:, C * h:C * h + C], pick("row%d" % n, lst("hv%d" % (n - 1)), HC * h, HC), AF.Copy))
+
+        def cand_scan(h):
+            op("v", ["kjr%d" % h, "hold"], ["kjs%d" % h], lambda: V.tensor_tensor_scan(
+                T.kjs[:, C * h:C * h + C], T.hold[:], T.kjr[:, C * h:C * h + C], 0.0, A.add, A.max))
 
         def yadd(b):
-            op("v", ["xp%d" % b, "%s.%d" % (xo, b), "mw"], ["y%d" % b], lambda: V.tensor_tensor(
+            op("v", ["xp%d" % b, to % (0, b), to % (1, b), "mw"], ["y%d" % b], lambda: V.tensor_tensor(
                 T.y32[:, C * b:C * b + C], pick("xp", m1, C * b), T[xo][:, b:1280:4], A.add))
 
-        fw, fp = "fw%d" % r, "fp%d" % r
-        spick("m1r", "cio", m1, "mw")
-        spick("fr", "m1r", m0, "mw")
-        for b in (0, 1, 2):
-            yadd(b)
-        wrap_out(wrap_scan(T.fr[:], "fr"), T[fw][:], fw)
-        yadd(3)
-        order("g", [fw], [])
-        g.remote_dma(T[fp][:], T[fw][:], T.sem["a%df" % r], T.sem.lsem, pid, rid, mask)
-        cnt["lsem"] = cnt.get("lsem", 0) + neng
+        def zpick(q, c, b):
+            a, n = runs(c)
+            out, in_ = T.zt[:, 640 * a + b:640 * (a + n):4], pick("y32", lst("mw", 10 * a, 10 * (a + n)), C * b)
+            toks = ["z%d%d" % (a + i, b) for i in range(n)]
+            if q == "s":
+                op("s", ["y%d" % b, "mw"], toks, lambda: S.activation(out, in_, AF.Copy, scale=0.5))
+            else:
+                op("v", ["y%d" % b, "mw"], toks, lambda: V.tensor_scalar(out, in_, 0.5, None, A.mult))
 
-        for b in range(3):
-            op("s", ["y%d" % b, "mw"], ["z%d" % b], lambda: S.activation(T.zt[:, b:1280:4], pick("y32", m0, C * b), AF.Copy, scale=0.5))
-        for c in (0, 1):
-            op("v", ["y3", "mw"], ["z%d" % (3 + c)], lambda: V.tensor_scalar(
-                T.zt[:, 640 * c + 3:640 * c + 640:4], pick("y32", lst("mw", 10 * c, 10 * c + 10), 3 * C), 0.5, None, A.mult))
+        def layer(c):
+            quantise("qz", "sz", "zt", c, ["z%d%d" % (c, b) for b in range(4)])
+            for b in range(4):
+                product(4 * c + b, ("qw", "sw"), b, ("qz", "sz"), c, ["qz.%d" % c, "qw"])
 
-        for c in (0, 1):
-            op("v", ["z0", "z1", "z2", "z%d" % (3 + c)], ["qz%d" % c], lambda: V.quantize_mx(
-                T.qz[:, HC * c:HC * c + HC], T.sz[:, HC * c:HC * c + HC], T.zt[:, 640 * c:640 * c + 640]))
-            for b in range(4):
-                product(4 * c + b, ("qw", "sw"), b, ("qz", "sz"), c, ["qz%d" % c, "qw"])
-        qh, sh, lc, ls = "qh%d" % r, "sh%d" % r, "lc%d" % r, "ls%d" % r
-        for c in (0, 1):
-            for b in range(4):
-                evac(("svsv", "ssvs")[c][b], T.ht[:, 640 * c + b:640 * c + 640:4], 4 * c + b, "h%d%d" % (c, b), 0.03125)
-            op("v", ["h%d%d" % (c, b) for b in range(4)], [qh + str(c)], lambda: V.quantize_mx(
-                T[qh][:, HC * c:HC * c + HC], T[sh][:, HC * c:HC * c + HC], T.ht[:, 640 * c:640 * c + 640]))
-            order("g", [qh + str(c)], [])
-            for out, in_ in ((T[lc][:, HC * c:HC * c + HC].bitcast(dt.uint8), T[qh][:, HC * c:HC * c + HC].bitcast(dt.uint8)),
-                             (T[ls][:, HC * c:HC * c + HC], T[sh][:, HC * c:HC * c + HC])):
-                g.remote_dma(out, in_, T.sem["a%dc%d" % (r, c)], T.sem.lsem, pid, rid, mask)
-                cnt["lsem"] += neng
-        for sem, n in [("a%df" % r, neng), ("a%dc0" % r, 2 * neng), ("a%dc1" % r, 2 * neng)]:
-            cnt[sem] = n
-        wrote[fp] = {"a%df" % r: neng}
-        for c in (0, 1):
-            wrote["ld%d%d" % (r, c)] = {"a%dc%d" % (r, c): 2 * neng}
+        def send(out, in_, sem):
+            g.remote_dma(out, in_, T.sem[sem], T.sem.lsem, pid, rid, mask)
+            cnt["lsem"] = cnt.get("lsem", 0) + neng
 
-        n = r + 1
-        if r == 1:
-            spick("hvr", "cio", lst("hv0"), "hv0")
-            places(1)
-            role(0)
+        def send_h(c):
+            quantise(qh, sh, "ht", c, ["h%d%d" % (c, b) for b in range(4)])
+            order("g", ["%s.%d" % (qh, c)], [])
+            send(T[lc][:, HC * c:HC * c + HC].bitcast(dt.uint8), T[qh][:, HC * c:HC * c + HC].bitcast(dt.uint8), "a%dc%d" % (r, c))
+            send(T[ls][:, HC * c:HC * c + HC], T[sh][:, HC * c:HC * c + HC], "a%dc%d" % (r, c))
+
+        def send_f():
+            wrapped(fw, "scf")
+            order("g", [fw], [])
+            send(T[fp][:], T[fw][:], "a%df" % r)
+
+        def unpack(c):
             for b in range(4):
-                op("v", ["et%d" % b], ["qe%d" % b], lambda: V.quantize_mx(
-                    T.qe[:, 128 * b:128 * b + 128], T.se[:, 128 * b:128 * b + 128], T.et[:, 512 * b:512 * b + 512]))
-        spick("lr", "fr", lst(fp), fp)
-        if not last:
-            op("v", [fp, "cio"], ["fi"], lambda: V.tensor_copy(T.fi[:, 0:C].indirect(lst(fp)), T.cio[:]))
-            spick("pr%d" % n, "fi", lst("lhu%d" % (r - 1)), "lhu%d" % (r - 1))
-            ws = wrap_scan(T.lr[:], "lr")
-            if r == 2:
-                ts("hvs2", "hv2", 2.0, 1.0, A.mult, A.add)
-            wrap_out(ws, T.lw[:], "lw")
-            fin = vertices(n)
-            cand_pick(n)
-            if r == 2:
-                role(0)
-            fin(0)
-            fin(1)
-            cand_scan(0)
-            cand_scan(1)
-            if r == 1:
-                spick("tr", "hvr", lst(fp), fp)
-        else:
-            op("v", ["hlt"], ["hu"], lambda: V.tensor_copy(T.hu[:], T.hlt[:, 0:20]))
-            op("v", ["vt"], ["qv"], lambda: V.quantize_mx(T.qv[:], T.sv[:], T.vt[:]))
-            spick("raw0", "cio", lst("hu"), "hu")
-            spick("raw2", "raw0", lst("fp1"), "fp1")
-            wrap_out(wrap_scan(T.lr[:], "lr"), T.lw[:], "lw")
-            spick("tpr", "raw2", lst(fp), fp)
+                product(4 * c + b, ("qe", "se"), b, (lc, ls), c, ["ld%d" % c, "qe%d" % b])
+
+        def meet(c, b):
+            a, n = runs(c)
+            cols = slice(640 * a + b, 640 * (a + n), 4)
+            op("v", ["d0%d" % b, "d1%d" % b, "lw"] + [to % (a + i, b) for i in range(n)],
+               [tn % (a + i, b) for i in range(n)] + ["%s.%d%d" % (xn, a + i, b) for i in range(n)],
+               lambda: V.tensor_tensor(T[xn][:, cols], pick("dd", lst("lw", 10 * a, 10 * (a + n)), C * b), T[xo][:, cols], A.add))
+
+        def tails():
+            spick("tpr", "raw2", fp)
             dma("y", "ot", T.tp[:], T.tpr[0:128:16, :], rd=["tpr"])
 
-        for c in (0, 1):
-            for b in range(4):
-                product(4 * c + b, ("qe", "se"), b, (lc, ls), c, ["ld%d%d" % (r, c), "qe%d" % b])
-            for b in range(4):
-                evac(("ssss", "vsss")[c][b], T.dd[:, C * b + HC * c:C * b + HC * c + HC], 4 * c + b, "d%d%d" % (c, b))
-        for b in range(4):
-            op("v", ["d0%d" % b, "d1%d" % b, "lw", "%s.%d" % (xo, b)], ["%s.%d" % (xn, b)], lambda: V.tensor_tensor(
-                T[xn][:, b:1280:4], pick("dd", lst("lw"), C * b), T[xo][:, b:1280:4], A.add))
-        for c in (0, 1):
-            if last:
-                quant_x(xn, c, "qo", "so")
-            else:
-                quant_x(xn, c)
-        if not last:
-            for b in range(4):
-                plane("g", b, xn)
+        def ones(b):
+            op("v", ["et%d" % b], ["qe%d" % b], lambda: V.quantize_mx(
+                T.qe[:, 128 * b:128 * b + 128], T.se[:, 128 * b:128 * b + 128], T.et[:, 512 * b:512 * b + 512]))
 
-    dma("y", "oq", T.oc[:], T.qo[:].bitcast(dt.uint8), rd=["qo0", "qo1"], total=80)
-    for k in range(4):
-        dma("y", "oq", T.osc[4 * k:4 * k + 4, :], T.so[32 * k:32 * k + 4, :], rd=["qo0", "qo1"], total=80)
-    for c in (0, 1):
-        product(c, ("qv", "sv"), 0, ("qo", "so"), c, ["qo%d" % c, "qv"])
-    for c in (0, 1):
-        evac("vs"[c], T.yo[:, HC * c:HC * c + HC], c, "yo%d" % c)
-    for c in (0, 1):
-        dma("s", "oy", T.y[:, HC * c:HC * c + HC], T.yo[:, HC * c:HC * c + HC], rd=["yo%d" % c], total=32)
+        def store_scales():
+            for k in range(4):
+                dma("y", "oq", T.osc[4 * k:4 * k + 4, :], T.so[32 * k:32 * k + 4, :], rd=["qo.0", "qo.1"], total=OPT.get("oq", 80))
+
+        def store_codes(c):
+            a, n = runs(c)
+            dma("y", "oq", T.oc[:, 640 * a:640 * (a + n)], T.qo[:, HC * a:HC * (a + n)].bitcast(dt.uint8),
+                rd=["qo.%d" % (a + i) for i in range(n)], total=OPT.get("oq", 80))
+
+        steps = {
+            "enc": places, "et": units, "turn": turn, "f": send_f, "tp": tails, "os": store_scales,
+            "gm": lambda: op("v", ["tt0", "tt1", "tof", "kd0", "kd1"], ["mt"], lambda: V.tensor_tensor(
+                T.mt[:], pick("tt", lst("tof", 0, 3), 0, 2 * C + 32), T.kd[:], A.mult)),
+            "ad": lambda: op("v", ["mt", "k10", "k11"], ["mf"], lambda: V.tensor_tensor(T.mf[:], T.mt[:], T.k1[:], A.add)),
+            "mw": lambda: ts("mw", "mf", "sub", None, A.subtract), "fs": lambda: scan("scf", "fr"),
+            "qu": lambda: op("v", ["ut"], ["qu"], lambda: V.quantize_mx(T.qu[:], T.su[:], T.ut[:])),
+            "qv": lambda: op("v", ["vt"], ["qv"], lambda: V.quantize_mx(T.qv[:], T.sv[:], T.vt[:])),
+            "mm": lambda: [product(c, ("qu", "su"), 0, ("qx", "sx"), c, ["qx.%d" % c, "qu"]) for c in (0, 1)],
+            "pg": lambda: [plane("g", b) for b in range(4)],
+            "li": lambda: lower(0, ai), "lo": lambda: lower(1, ao), "hi": lambda: higher(0, ai), "ho": lambda: higher(1, ao),
+            "sum": lambda: op("v", ["bit0", "bit1", "alt"], ["sum"], lambda: V.tensor_tensor_scan(T["sum"][:], T.alt[:], T.bit[:], 0.0, A.mult, A.add)),
+            "nx": lambda: straight("s", 2), "nxs": lambda: straight("s", 0), "nxv": lambda: straight("v", 1),
+            "rs": lambda: scan("scr", "ajr"),
+            "rr": lambda: op("v", ["scr", "ciw"], ["rr"], lambda: V.tensor_tensor(T.rr[:], T.scr[:, 15:C:16], T.ciw[:], A.is_lt)),
+            "g2": lambda: affine("g2", "rr", 2.0, -1.0), "g2v": lambda: ts("g2", "rr", 2.0, -1.0, A.mult, A.add),
+            "dd": lambda: op("v", ["kjs0", "kjs1"], ["ddc"], lambda: V.tensor_tensor(T.ddc[:], hi_out, lo_out, A.subtract)),
+            "kq": lambda: tt("kq", "ddc", "rr", A.mult),
+            "kd": lambda: both("kd", T.ddc[:], "ddc", T.g2[:], "g2", A.mult),
+            "k1": lambda: both("k1", hi_out, "kjs1", T.kq[:], "kq", A.subtract),
+            "m1r": lambda: spick("m1r", "cio", "mw", K1, K1 + 20), "fr": lambda: spick("fr", "m1r", "mw"),
+            "lr": lambda: spick("lr", "fr", fp), "ls": lambda: scan("scl", "lr"), "lw": lambda: wrapped("lw", "scl"),
+            "fi": lambda: op("v", [fp, "cio"], ["fi"], lambda: V.tensor_copy(T.fi[:, 0:C].indirect(lst(fp)), T.cio[:])),
+            "hvr": lambda: spick("hvr", "cio", "hv0"), "tr": lambda: spick("tr", "hvr", "fp1"),
+            "hs": lambda: scan("sch", "tr"), "hw": lambda: wrapped("hv2", "sch"),
+            "hvs": lambda: ts("hvs2", "hv2", 2.0, 1.0, A.mult, A.add),
+            "hu": lambda: op("v", ["hlt"], ["hu"], lambda: V.tensor_copy(T.hu[:], T.hlt[:, 0:20])),
+            "raw": lambda: [spick("raw0", "cio", "hu"), spick("raw2", "raw0", "fp1")],
+            "ym": lambda: [product(c, ("qv", "sv"), 0, ("qo", "so"), c, ["qo.%d" % c, "qv"]) for c in (0, 1)],
+            "oc": lambda: store_codes(2),
+        }
+        for n in range(4):
+            steps.update({
+                "scat%d" % n: lambda n=n: scatter(n), "heads%d" % n: lambda n=n: heads(n), "rp%d" % n: lambda n=n: role_pick(n),
+                "vs%d" % n: lambda n=n: scan("scv", "pr%d" % n), "vm%d" % n: lambda n=n: sort2(n), "vc%d" % n: lambda n=n: sorted_list(n),
+                "row%d" % n: lambda n=n: spick("row%d" % n, "cio", "lhu%d" % n),
+                "pr%d" % n: lambda n=n: spick("pr%d" % n, "fi", "lhu%d" % (n - 2)),
+                "qe%d" % n: lambda n=n: ones(n), "ps%d" % n: lambda n=n: plane("s", n), "y%d" % n: lambda n=n: yadd(n), "a%d" % n: lambda n=n: meet(2, n),
+            })
+        for c in (0, 1):
+            steps.update({
+                "q%d" % c: lambda c=c: quantise("qx", "sx", xo, c, [to % (c, b) for b in range(4)]),
+                "o%d" % c: lambda c=c: quantise("qo", "so", xn, c, [tn % (c, b) for b in range(4)]),
+                "ks%d" % c: lambda c=c: cand_scan(c), "l%d" % c: lambda c=c: layer(c), "send%d" % c: lambda c=c: send_h(c),
+                "u%d" % c: lambda c=c: unpack(c), "oc%d" % c: lambda c=c: store_codes(c),
+                "ym%d" % c: lambda c=c: product(c, ("qv", "sv"), 0, ("qo", "so"), c, ["qo.%d" % c, "qv"]),
+                "oy%d" % c: lambda c=c: dma("s", "oy", T.y[:, HC * c:HC * c + HC], T.yo[:, HC * c:HC * c + HC], rd=["yo%d" % c], total=32),
+            })
+            for b in range(4):
+                steps["a%d%d" % (c, b)] = lambda c=c, b=b: meet(c, b)
+        for part in "abc":
+            for c in (0, 1):
+                steps["kp%d" % c] = lambda c=c: cand_pick(c, r + (part == "c"))
+                for q in "sv":
+                    res = "yo" if part == "c" else "sk"
+                    steps["e%s%d" % (q, c)] = lambda q=q, c=c, res=res: evac(q, T[res][:, HC * c:HC * c + HC], c, "%s%d" % (res, c))
+                    for b in range(4):
+                        steps["z%s%d%d" % (q, c, b)] = lambda q=q, c=c, b=b: zpick(q, c, b)
+                        steps["z%s2%d" % (q, b)] = lambda q=q, b=b: zpick(q, 2, b)
+                        steps["h%s%d%d" % (q, c, b)] = lambda q=q, c=c, b=b: evac(
+                            q, T.ht[:, 640 * c + b:640 * c + 640:4], 4 * c + b, "h%d%d" % (c, b), 0.03125)
+                        steps["d%s%d%d" % (q, c, b)] = lambda q=q, c=c, b=b: evac(
+                            q, T.dd[:, C * b + HC * c:C * b + HC * c + HC], 4 * c + b, "d%d%d" % (c, b))
+            for w in OPT["%s%d" % (part, r)].split():
+                steps[w]()
     for sem in sorted(cnt):
         need("g", sem, cnt[sem])

@@ -8,32 +8,43 @@ STEP = [1, 2, 4]
 CODE = "float8_e4m3fn_x4"
 K1 = 24
 
-LAYER = "m1r fr y0 y1 y2 fs y3 f zs00 zs01 zs02 zv03 l0 zs10 zs11 zs12 zs13 l1 %s hv00 hs01 hv02 hs03 send0 hs10 hv11 hs12 hv13 send1"
-MEET = "u0 ds00 ds01 ds02 ds03 u1 dv10 ds11 ds12 ds13"
-OPT = {
-    "a1": "enc scat1 qu vs1 q0 vm1 q1 vc1 pg et mm es0 es1 row1 scat0 lo rp0 kp0 vs0 ho vm0 rs vc0 li kp1 ks0 rr hi g2v sum nx "
-          "ks1 dd kq kd k1 rp1 turn heads1 gm ad mw",
-    "b1": (LAYER % "rs").replace("send0", "qe0 send0").replace("send1", "qe1 send1"),
-    "c1": "qe2 qe3 lr hvr fi ls lw pr2 vs2 vm2 vc2 " + MEET + " row2 kp0 kp1 tr a0 a1 a2 a3",
-    "a2": "q0 q1 pg mm es0 es1 ks0 ks1 li lo rr dd g2 hi ho sum nx kq kd k1 hs turn hw rp2 gm hvs ad mw",
-    "b2": LAYER % "rs",
-    "c2": "lr fi pr3 ls lw vs3 vm3 vc3 " + MEET + " row3 kp0 kp1 a0 a1 a2 a3",
-    "a3": "q0 q1 pg mm es0 es1 ks0 ks1 li lo rr dd g2 hi ho sum nx kq kd k1 turn gm ad mw",
-    "b3": LAYER % "",
-    "c3": "lr hu qv raw ls lw tp " + MEET + " a00 a01 a02 a03 o0 oc0 ym0 es0 oy0 a10 a11 a12 a13 o1 ym1 oc1 os ev1 oy1",
-    "oq": 96,
-}
+LAYER = "m1r fr y0 y1 y2 FS y3 F zs20 zs21 zs02 zv03 zs12 l0 zs13 l1 hv00 hs01 hv02 hs03 send0 hs10 hs11 hv12 hs13 send1"
+RUNS = "u0 ds00 ds01 ds02 ds03", "u1 dv10 ds11 ds12 ds13"
+OPT = {"oq": 96, "fsend": "123", "cut": 192}
+OPT["a1"] = ("encf scat1 qu vs1 q0 vm1 q1 vc1 pg et mm es0 es1 row1 scat0 lo rp0 kp0 vs0 ho vm0 rs vc0 li kp1 ks0 rr hi g2 sum nx "
+             "ks1 dd kq kd k1 turn rp1 gm ad mw")
+OPT["b1"] = LAYER.replace("send0", "qe0 send0").replace("send1", "qe1 send1")
+OPT["c1"] = "qe2 qe3 rs hvr rr lr fi ls g2 lw pr2 vs2 vm2 vc2 %s %s row2 kp0 kp1 tr a0 a1 a2 a03 a13" % RUNS
+OPT["a2"] = "q0 q1 pg mm es0 es1 ks0 ks1 li lo dd hi kq ho kd sum k1 nxs nxv turn gm ad mw"
+OPT["b2"] = LAYER
+OPT["c2"] = "lr fi pr3 ls hs lw hw rp2 vs3 vm3 vc3 %s %s row3 kp0 kp1 a0 a1 a2 a03 a13" % RUNS
+OPT["a3"] = "q0 q1 pg mm es0 es1 ks0 ks1 li lo rs dd hi rr ho sum nx g2 kq kd k1 turn gm ad mw"
+OPT["b3"] = "m1r y0 y1 y2 y3 zs20 zs21 fr zs02 zv03 zs12 l0 FS zs13 l1 F hs00 hv01 hs02 hs03 send0 hs10 hv11 hs12 hv13 send1"
+OPT["c3"] = "hu raw qv lr ls lw %s %s TP a00 a01 a02 a03 a10 o0 oc0 ym0 es0 oy0 a11 a12 a13 o1 ym1 oc1 os ev1 oy1" % RUNS
+OPT.update({
+    "cut": 160, "uq": "y",
+    "a1": "encf scat1 q0 vs1 q1 vm1 qu vc1 pg et row1 mm es0 es1 kp0 scat0 lo vs0 vm0 vc0 ks0 li ho rp0 kp1 hi sum rs nx rr ks1 g2 dd turn kq kd k1 rp1 gm ad mw",
+    "b1": "m1r fr y0 y1 y2 FS y3 F zs20 zs21 zs22 zv03 zs13 l0 qe0 l1 qe1 hs00 hv01 hs02 hv03 send0 hs10 hs11 hs12 hv13 send1",
+    "c1": "qe2 qe3 hvr lr tr fi ls pr2 rs lw rr %s vs2 g2 vm2 %s vc2 a0 row2 kp0 kp1 a1 a2 a03 a13" % RUNS,
+    "a2": "q0 q1 pg mm es0 es1 ks hs li lo dd hw hi kq ho sum kd nxs nxv k1 turn rp2 gm ad mw",
+    "b2": "m1r fr y0 y1 y2 y3 zv03 FS zs20 zs21 zs02 zs12 zs13 l0 F l1 hs00 hv01 hs02 hv03 send0 hs10 hs11 hv12 hv13 send1",
+    "c2": "lr fi pr3 ls rs lw rr %s vs3 g2 vm3 %s vc3 a0 row3 kp0 kp1 a1 a2 a03 a13" % RUNS,
+    "a3": "q0 q1 pg mm es0 es1 ks li lo dd kq kd k1 hi ho sum nxs nxv turn gm ad mw",
+    "b3": "m1r y0 y1 y2 y3 zs20 fr zs21 zs02 zv03 zs12 l0 FS zs13 l1 F hs00 hv01 hs02 hv03 send0 hs10 hs11 hv12 hv13 send1",
+    "c3": "hu raw qv lr ls lw %s %s TP cut a00 a01 a02 a03 a10 o0 oc0 ym0 es0 oy0 a11 a12 a13 o1 ym1 oc1 os es1 oy1" % RUNS,
+})
 
 SCRATCH = {
     "cio": ("sbuf", [128, 320], "float32"), "j16": ("sbuf", [128, 320], "bfloat16"), "mk": ("sbuf", [128, 320], "float32"),
-    "hold": ("sbuf", [128, 320], "float32"), "alt": ("sbuf", [128, 320], "bfloat16"),
+    "sg": ("sbuf", [128, 320], "bfloat16"),
+    "hold": ("sbuf", [128, 640], "float32"), "alt": ("sbuf", [128, 320], "bfloat16"),
     "pmi": ("sbuf", [128, 2], "int32"), "pma": ("sbuf", [128, 2], "int32"), "sub": ("sbuf", [128, 1], "float32"),
     "i17": ("sbuf", [128, 2], "int32"), "s16": ("sbuf", [128, 2], "int32"), "s21": ("sbuf", [128, 1], "float32"),
     "pmf": ("sbuf", [128, 1], "float32"), "p16": ("sbuf", [128, 1], "float32"), "cs": ("sbuf", [128, 1], "float32"),
     "c16": ("sbuf", [128, 20], "float32"), "ciw": ("sbuf", [128, 20], "float32"),
     "n16": ("sbuf", [128, 4], "float32"), "n24": ("sbuf", [128, 4], "float32"), "n48": ("sbuf", [128, 4], "float32"),
     "c256": ("sbuf", [128, 4], "float32"), "tof": ("sbuf", [128, 4], "uint16"),
-    "one": ("sbuf", [128, 512], "bfloat16"), "et": ("sbuf", [128, 2048], "bfloat16"),
+    "one": ("sbuf", [128, 516], "bfloat16"), "et": ("sbuf", [128, 516], "bfloat16"),
     "qe": ("sbuf", [128, 512], CODE), "se": ("sbuf", [128, 512], "uint8"),
     "ut": ("sbuf", [128, 512], "bfloat16"), "vt": ("sbuf", [128, 512], "bfloat16"),
     "qu": ("sbuf", [128, 128], CODE), "su": ("sbuf", [128, 128], "uint8"),
@@ -51,8 +62,11 @@ SCRATCH = {
     "ps": ("psum", [128, 4096], "float32"),
     "sk": ("sbuf", [128, 320], "float32"), "ga": ("sbuf", [128, 320], "float32"), "bit": ("sbuf", [128, 320], "bfloat16"),
     "sum": ("sbuf", [128, 320], "bfloat16"), "nx": ("sbuf", [128, 352], "bfloat16"), "tt": ("sbuf", [128, 672], "bfloat16"),
-    "kd": ("sbuf", [128, 48], "float32"), "k1": ("sbuf", [128, 48], "float32"),
-    "mt": ("sbuf", [128, 48], "float32"), "mf": ("sbuf", [128, 48], "float32"), "mw": ("sbuf", [128, 48], "uint16"),
+    "kk": ("sbuf", [128, 96], "float32"),
+    "pr0": ("sbuf", [128, 320], "float32"), "pr1": ("sbuf", [128, 320], "float32"), "row": ("sbuf", [128, 640], "float32"),
+    "hvs": ("sbuf", [128, 40], "uint16"), "hvs2": ("sbuf", [128, 20], "uint16"),
+    "mt": ("sbuf", [128, 48], "float32"), "mf": ("sbuf", [128, 48], "float32"),
+    "m1p": ("sbuf", [128, 320], "float32"), "fpr": ("sbuf", [128, 320], "float32"),
     "fi": ("sbuf", [128, 320], "float32"), "g2": ("sbuf", [128, 20], "float32"), "rr": ("sbuf", [128, 20], "float32"),
     "m1r": ("sbuf", [128, 320], "float32"), "fr": ("sbuf", [128, 320], "float32"), "lr": ("sbuf", [128, 320], "float32"),
     "lw": ("sbuf", [128, 20], "uint16"), "ajr": ("sbuf", [128, 320], "float32"),
@@ -60,25 +74,21 @@ SCRATCH = {
     "ddc": ("sbuf", [128, 20], "float32"), "kq": ("sbuf", [128, 20], "float32"),
     "tr": ("sbuf", [128, 320], "float32"), "hvr": ("sbuf", [128, 320], "float32"),
     "raw0": ("sbuf", [128, 320], "float32"), "raw2": ("sbuf", [128, 320], "float32"),
-    "lohi": ("sbuf", [128, 20], "float32"),
+    "lohi": ("sbuf", [128, 40], "float32"),
 }
-for _n in ("v", "r", "h", "f", "l"):
+for _n in ("v0", "v1", "r", "h", "f", "l"):
     SCRATCH["sc" + _n] = ("sbuf", [128, 320], "float32")
 for _k in (0, 1):
     SCRATCH["xi%d" % _k] = ("sbuf", [128, 1280], "bfloat16")
 for _n in range(4):
-    SCRATCH["pr%d" % _n] = ("sbuf", [128, 320], "float32")
     SCRATCH["lhu%d" % _n] = ("sbuf", [128, 20], "uint16")
-    if _n > 0:
-        SCRATCH["row%d" % _n] = ("sbuf", [128, 320], "float32")
-    if _n < 3:
-        SCRATCH["hvs%d" % _n] = ("sbuf", [128, 20], "uint16")
-        SCRATCH["hv%d" % _n] = ("sbuf", [128, 20], "uint16")
 for _r in (1, 2, 3):
     SCRATCH["qh%d" % _r] = ("sbuf", [128, 320], CODE)
     SCRATCH["sh%d" % _r] = ("sbuf", [128, 320], "uint8")
     SCRATCH["lc%d" % _r] = ("sbuf", [128, 320], CODE)
     SCRATCH["ls%d" % _r] = ("sbuf", [128, 320], "uint8")
+    SCRATCH["mw%d" % _r] = ("sbuf", [128, 48], "uint16")
+    SCRATCH["mp%d" % _r] = ("sbuf", [128, 48], "uint16")
     SCRATCH["fw%d" % _r] = ("sbuf", [128, 20], "uint16")
     SCRATCH["fp%d" % _r] = ("sbuf", [128, 20], "uint16")
 
@@ -168,101 +178,144 @@ def rank_program(g, core, T, topo):
     dma("s", "dl", T.hlt[:, 0:20], T.hl[:], wr=["hlt"], total=32)
     dma("y", "dl", T.hlt[:, 20:40], T.tl[:], total=32)
     dma("y", "dx", T.xi0[:], T.x[:], wr=["x0.%d%d" % (c, b) for c in (0, 1) for b in range(4)])
-    dma("s", "du", T.ut[:], T.u[:], wr=["ut"])
+    dma(OPT.get("uq", "s"), "du", T.ut[:], T.u[:], wr=["ut"])
     dma("y", "dw", T.qw[:].bitcast(dt.uint8), T.wc[:], wr=["qw"], total=32)
     dma("y", "dw", T.sw[:], T.ws[:], total=32)
     dma("y", "dv", T.vt[:], T.v[:], wr=["vt"])
 
     op("g", [], ["pmi"], lambda: g.iota(T.pmi[:], [[0, 2]], 0, 1))
     op("g", [], ["i17"], lambda: g.iota(T.i17[:], [[0, 2]], 0, 17))
-    for name, pattern in (("c256", [[256, 4]]), ("j16", [[0, 20], [1, 16]]), ("cio", [[1, 320]]), ("c16", [[16, 20]]), ("alt", [[0, 160], [1, 2]])):
-        op("g", [], [name], lambda: g.iota(T[name][:], pattern, 0, 0, allow_small_or_imprecise_dtypes=True))
-    op("v", [], ["one"], lambda: V.memset(T.one[:], 1.0))
-    ts("pma", "pmi", 15, None, A.bitwise_and)
-    ts("s16", "i17", 16, None, A.bitwise_and)
+    for name, pattern in (("c256", [[256, 4]]), ("j16", [[0, 20], [1, 16]]), ("cio", [[1, C]]), ("c16", [[16, 20]]),
+                          ("row", [[0, C]]), ("alt", [[0, HC], [1, 2]])):
+        out = T.row[:, 0:2 * C:2] if name == "row" else T[name][:]
+        op("g", [], [name], lambda: g.iota(out, pattern, 0, 0, allow_small_or_imprecise_dtypes=True))
     op("v", [], ["nx0", "nx1"], lambda: V.memset(T.nx[:], 0.0))
+    ts("pma", "pmi", 15, None, A.bitwise_and)
+    op("v", [], ["kd0", "kd1", "k10", "k11"], lambda: V.memset(T.kk[:], 0.0))
+    ts("s16", "i17", 16, None, A.bitwise_and)
+    ts("p16", "pma", 16.0, None, A.mult, to=(T.p16[:], T.pma[:, 0:1]))
     ts("pmf", "pma", 1.0, None, A.mult, to=(T.pmf[:], T.pma[:, 0:1]))
     ts("s21", "s16", 21.0, None, A.mult, to=(T.s21[:], T.s16[:, 0:1]))
-    op("v", [], ["kd0", "kd1"], lambda: V.memset(T.kd[:], 0.0))
-    op("v", [], ["k10", "k11"], lambda: V.memset(T.k1[:], 0.0))
-    ts("mk", "j16", "pmf", -16896.0, A.is_equal, A.mult)
-    for name, a, b in (("p16", 16.0, 0.0), ("sub", -512.0, 7680.0), ("cs", -511.0, 7680.0)):
-        affine(name, "pmf", a, b)
-    affine("n16", "c256", 1.0, "p16")
-    affine("hold", "mk", 1.0, 512.0)
+    ts("n16", "c256", "p16", None, A.add)
+    ts("n24", "n16", 16.0 * K1, 1.0 - 16.0 * K1, A.is_ge, A.mult)
+    tt("n48", "n16", "n24", A.add)
+    ts("tof", "n48", "s21", 671.0, A.add, A.min)
+    affine("sub", "pmf", -512.0, 7680.0)
+    if OPT.get("old"):
+        ts("mk", "j16", "pmf", 16384.0, A.not_equal, A.mult)
+    else:
+        op("s", ["j16", "pmf"], ["sg"], lambda: S.activation(T.sg[:], T.j16[:], AF.Sign, bias=T.pmf[:], scale=-1.0))
+        op("s", ["sg"], ["mk"], lambda: S.activation(T.mk[:], T.sg[:], AF.Square, scale=128.0))
+    op("s", ["mk"], ["hold0"], lambda: S.activation(T.hold[:, 0:C], T.mk[:], AF.Copy, bias=512.0 - 128.0 ** 2))
+    affine("cs", "pmf", -511.0, 7680.0)
     affine("ciw", "c16", 1.0, "cs")
 
     def scan(b, row):
-        op("v", [row, "hold"], [b], lambda: V.tensor_tensor_scan(T[b][:], T.hold[:], T[row][:], 0.0, A.add, A.max))
+        op("v", [row, "hold0"], [b], lambda: V.tensor_tensor_scan(T[b][:], T.hold[:, 0:C], T[row][:], 0.0, A.add, A.max))
 
     def wrapped(out, b):
         op("v", [b, "sub"], [out], lambda: V.tensor_scalar(T[out][:], T[b][:, 15:C:16], T["sub"][:], None, A.subtract))
 
-    def spick(name, win, off, a=0, b=20, n=C):
-        op("s", [win, off], [name], lambda: S.activation(T[name][:], pick(win, lst(off, a, b), 0, n), AF.Copy))
+    eng = ["s"]
 
-    def places():
-        ts("hb", "hlt", 1, None, A.bitwise_and)
-        ts("hv", "hlt", 1, None, A.arith_shift_right)
-        ts("n24", "n16", 16.0 * K1, 1.0 - 16.0 * K1, A.is_ge, A.mult)
-        ts("hb2", "hb", HC, None, A.mult)
-        heads(0)
-        tt("enci", "hb2", "hv", A.add)
-        tt("spi", "hv", "hb2", A.subtract)
-        tt("n48", "n16", "n24", A.add)
-        op("v", ["enci"], ["enc"], lambda: V.tensor_copy(T.enc[:], T.enci[:]))
-        ts("sp", "spi", float(HC), None, A.add)
-        ts("tof", "n48", "s21", 671.0, A.add, A.min)
+    def copy(rd, wr, out, in_):
+        if eng[0] == "s":
+            op("s", rd, wr, lambda: S.activation(out, in_, AF.Copy))
+        else:
+            op("v", rd, wr, lambda: V.tensor_copy(out, in_))
+
+    def spick(name, win, off, a=0, b=20, n=C, pairs=False):
+        out = T[name][:, 1:32 * (b - a):2] if pairs else T[name][:]
+        copy([win, off], [name], out, pick(win, lst(off, a, b), 0, n))
+
+    def places(i):
+        if i == 0:
+            ts("hb", "hlt", 1, None, A.bitwise_and)
+            ts("hv", "hlt", 1, None, A.arith_shift_right)
+            ts("hb2", "hb", HC, None, A.mult)
+            tt("enci", "hb2", "hv", A.add)
+            op("v", ["enci"], ["enc"], lambda: V.tensor_copy(T.enc[:], T.enci[:]))
+        if i == 3:
+            ts("hb", "hlt", 1, None, A.bitwise_and)
+            ts("hv", "hlt", 1, None, A.arith_shift_right)
+            ts("hb2", "hb", HC, None, A.mult)
+            places(1)
+            tt("enci", "hb2", "hv", A.add)
+            tt("spi", "hv", "hb2", A.subtract)
+            op("v", ["enci"], ["enc"], lambda: V.tensor_copy(T.enc[:], T.enci[:]))
+            ts("sp", "spi", float(HC), None, A.add)
+        if i == 1:
+            ts("hvs", "hv", 2.0, 1.0, A.mult, A.add)
+        if i == 2:
+            tt("spi", "hv", "hb2", A.subtract)
+            ts("sp", "spi", float(HC), None, A.add)
 
     def units():
-        for b in range(4):
-            op("g", ["one"], ["et%d" % b], lambda: g.affine_select(T.et[:, 512 * b:512 * b + 512], T.one[:], [[-1, 512]], A.is_equal, 0.0, b, 4))
+        op("g", ["hold0"], ["hold1"], lambda: g.affine_select(T.hold[:, C:2 * C], T.hold[:, 0:C], [[1, C]], A.is_ge, 0.0, 0, 0))
+        op("g", [], ["one"], lambda: g.iota(T.one[:], [[0, 516]], 1, 0, allow_small_or_imprecise_dtypes=True))
+        op("g", ["one"], ["et"], lambda: g.affine_select(T.et[:], T.one[:], [[-1, 516]], A.is_equal, 0.0, 3, 4))
 
     def scatter(n):
-        op("v", ["enc", "cio"], ["pr%d" % n], lambda: V.tensor_copy(T["pr%d" % n][:, 0:C].indirect(lst("enc", 20 * n, 20 * n + 20)), T.cio[:]))
+        op("v", ["enc", "cio"], ["pr%d" % n], lambda: V.tensor_copy(T["pr%d" % n][:].indirect(lst("enc", 20 * n, 20 * n + 20)), T.cio[:]))
 
     def sort2(n):
-        op("v", ["scv"], ["lo"], lambda: V.tensor_tensor(T.lohi[:, 0:10], T.scv[:, 15:HC:16], T.scv[:, HC + 15:C:16], A.min))
-        op("v", ["scv"], ["hi"], lambda: V.tensor_tensor(T.lohi[:, 10:20], T.scv[:, 15:HC:16], T.scv[:, HC + 15:C:16], A.max))
+        b, a = "scv%d" % (n % 2), 20 * (n % 2)
+        op("v", [b], ["lo%d" % a], lambda: V.tensor_tensor(T.lohi[:, a:a + 10], T[b][:, 15:HC:16], T[b][:, HC + 15:C:16], A.min))
+        op("v", [b], ["hi%d" % a], lambda: V.tensor_tensor(T.lohi[:, a + 10:a + 20], T[b][:, 15:HC:16], T[b][:, HC + 15:C:16], A.max))
 
     def sorted_list(n):
-        op("v", ["lo", "hi", "sub"], ["lhu%d" % n], lambda: V.tensor_scalar(T["lhu%d" % n][:], T.lohi[:], T["sub"][:], None, A.subtract))
+        a = 20 * (n % 2)
+        op("v", ["lo%d" % a, "hi%d" % a, "sub"], ["lhu%d" % n], lambda: V.tensor_scalar(T["lhu%d" % n][:], T.lohi[:, a:a + 20], T["sub"][:], None, A.subtract))
 
-    def heads(n):
-        src = T.hv[:, 20 * n:20 * n + 20]
-        op("v", ["hv"], ["hv%d" % n], lambda: V.tensor_copy(T["hv%d" % n][:], src))
-        op("v", ["hv"], ["hvs%d" % n], lambda: V.tensor_scalar(T["hvs%d" % n][:], src, 2.0, 1.0, A.mult, A.add))
+    def heads(n, a=0, b=20):
+        return ("hvs", 20 * n + a, 20 * n + b) if n < 2 else ("hvs2", a, b)
 
     def role_pick(n):
         if n < 2:
             spick("ajr", "pr%d" % n, "sp", 20 * n, 20 * n + 20)
         else:
-            spick("ajr", "row%d" % n, "hv%d" % n, n=HC)
+            spick("ajr", "row", *heads(n))
 
     def both(name, in0, t0, in1, t1, o):
+        a = 48 * (name == "k1")
         for k in (0, 1):
-            op("v", [t0, t1], ["%s%d" % (name, k)], lambda: V.tensor_tensor(T[name][:, K1 * k:K1 * k + 20], in0, in1, o))
-
-    def evac(q, out, k, tok, scale=None):
-        toks = ["bk%d" % k, tok]
-        if q == "s":
-            op("s", [], toks, lambda: S.activation(out, bank(k, HC), AF.Copy, scale=scale or 1.0))
-        elif scale:
-            op("v", [], toks, lambda: V.tensor_scalar(out, bank(k, HC), scale, None, A.mult))
-        else:
-            op("v", [], toks, lambda: V.tensor_copy(out, bank(k, HC)))
-
-    def product(k, w, b, x, c, toks):
-        op("t", toks, ["bk%d" % k], lambda: P.matmul_mx(
-            bank(k, HC), T[w[0]][:, 128 * b:128 * b + 128], T[w[1]][:, 128 * b:128 * b + 128],
-            T[x[0]][:, HC * c:HC * c + HC], T[x[1]][:, HC * c:HC * c + HC], True, True))
-
-    def quantise(q, s, tile, c, toks):
-        op("v", toks, ["%s.%d" % (q, c)], lambda: V.quantize_mx(
-            T[q][:, HC * c:HC * c + HC], T[s][:, HC * c:HC * c + HC], T[tile][:, 640 * c:640 * c + 640]))
+            if k == 1 and OPT.get("dup") == "s":
+                op("s", [name + "0"], [name + "1"], lambda: S.activation(T.kk[:, a + K1:a + K1 + 20], T.kk[:, a:a + 20], AF.Copy))
+            else:
+                op("v", [t0, t1], ["%s%d" % (name, k)], lambda: V.tensor_tensor(T.kk[:, a + K1 * k:a + K1 * k + 20], in0, in1, o))
 
     def runs(c):
         return (0, 2) if c == 2 else (c, 1)
+
+    def span(c):
+        return ((0, cut[0]), (cut[0], C), (0, C))[c]
+
+    def recut(n):
+        cut[0] = n
+
+    cut = [HC]
+
+    def each(name, c):
+        a, n = runs(c)
+        return [name % (a + i) for i in range(n)]
+
+    def evac(q, out, k, toks, n, scale=None):
+        toks = ["bk%d" % k] + toks
+        if q == "s":
+            op("s", [], toks, lambda: S.activation(out, bank(k, n), AF.Copy, scale=scale or 1.0))
+        elif scale:
+            op("v", [], toks, lambda: V.tensor_scalar(out, bank(k, n), scale, None, A.mult))
+        else:
+            op("v", [], toks, lambda: V.tensor_copy(out, bank(k, n)))
+
+    def product(k, w, b, x, c, toks):
+        a, e = span(c)
+        op("t", toks, ["bk%d" % k], lambda: P.matmul_mx(
+            bank(k, e - a), T[w[0]][:, 128 * b:128 * b + 128], T[w[1]][:, 128 * b:128 * b + 128], T[x[0]][:, a:e], T[x[1]][:, a:e], True, True))
+
+    def quantise(q, s, tile, c, toks):
+        a, e = span(c)
+        op("v", toks, each(q + ".%d", c), lambda: V.quantize_mx(T[q][:, a:e], T[s][:, a:e], T[tile][:, 4 * a:4 * e]))
 
     for r in (1, 2, 3):
         peer = T.cores[rank ^ STEP[r - 1]]
@@ -271,68 +324,63 @@ def rank_program(g, core, T, topo):
         neng = len(topo.engines(core, peer))
         xo, xn = "xi%d" % ((r - 1) % 2), "xi%d" % (r % 2)
         to, tn = "x%d.%%d%%d" % (r - 1), "x%d.%%d%%d" % r
-        ai, ao, hv, hvs = "lhu%d" % (r - 1), "lhu%d" % r, "hv%d" % (r - 1), "hvs%d" % (r - 1)
-        fw, fp, qh, sh, lc, ls = ["%s%d" % (w, r) for w in ("fw", "fp", "qh", "sh", "lc", "ls")]
-        m1 = lst("mw", K1, K1 + 20)
+        ai, ao, hvs = "lhu%d" % (r - 1), "lhu%d" % r, heads(r - 1)[0]
+        mw, mp, fw, fp, qh, sh, lc, ls = ["%s%d" % (w, r) for w in ("mw", "mp", "fw", "fp", "qh", "sh", "lc", "ls")]
+        m1 = lst(mw, K1, K1 + 20)
         lo_out, hi_out = T.kjs[:, 15:C:16], T.kjs[:, C + 15:2 * C:16]
-        wrote[fp] = {"a%df" % r: neng}
+        wrote[mp] = {"a%df" % r: neng}
         cnt["a%df" % r] = neng
         for c in (0, 1):
             wrote["ld%d" % c] = {"a%dc%d" % (r, c): 2 * neng}
             cnt["a%dc%d" % (r, c)] = 2 * neng
 
-        def plane(q, b):
-            out, in_, toks = T.xp[:, C * b:C * b + C], T[xo][:, b:1280:4], [to % (c, b) for c in (0, 1)]
-            if q == "s":
-                op("s", toks, ["xp%d" % b], lambda: S.activation(out, in_, AF.Copy))
-            else:
-                op("g", toks, ["xp%d" % b], lambda: g.affine_select(out, in_, [[1, C]], A.is_ge, 0.0, 0, 0))
+        def plane(b):
+            op("g", [to % (c, b) for c in (0, 1)], ["xp%d" % b], lambda: g.affine_select(
+                T.xp[:, C * b:C * b + C], T[xo][:, b:1280:4], [[1, C]], A.is_ge, 0.0, 0, 0))
 
         def lower(i, w):
-            op("s", ["sk0", "sk1", w], ["ga%d" % i], lambda: S.activation(T.ga[:, HC * i:HC * i + HC], pick("sk", lst(w, 0, 10)), AF.Copy))
+            copy(["sk0", "sk1", w], ["ga%d" % i], T.ga[:, HC * i:HC * i + HC], pick("sk", lst(w, 0, 10)))
 
         def higher(i, w):
             op("v", ["sk0", "sk1", w, "ga%d" % i], ["bit%d" % i], lambda: V.tensor_tensor(
                 T.bit[:, i:C:2], pick("sk", lst(w, 10, 20)), T.ga[:, HC * i:HC * i + HC], A.is_gt))
 
         def straight(q, c):
-            a, n = runs(c)
-            out, in_ = T.nx[:, 16 + HC * a:16 + HC * (a + n)], pick("sum", lst(hvs, 10 * a, 10 * (a + n)))
-            toks = ["nx%d" % (a + i) for i in range(n)]
+            a, e = span(c)
+            out, in_ = T.nx[:, 16 + a:16 + e], pick("sum", lst(*heads(r - 1, a // 16, e // 16)))
             if q == "s":
-                op("s", ["sum", hvs], toks, lambda: S.activation(out, in_, AF.Square, bias=-1.0))
+                op("s", ["sum", hvs], each("nx%d", c), lambda: S.activation(out, in_, AF.Square, bias=-1.0))
             else:
-                op("v", ["sum", hvs], toks, lambda: V.tensor_scalar(out, in_, 1.0, None, A.not_equal))
+                op("v", ["sum", hvs], each("nx%d", c), lambda: V.tensor_scalar(out, in_, 1.0, None, A.not_equal))
 
         def turn():
             op("v", ["nx0", "nx1"], ["tt0"], lambda: V.transpose(T.tt[:, 0:C], T.nx[:, 16:16 + C]))
             op("v", ["nx0", "nx1"], ["tt1"], lambda: V.transpose(T.tt[:, C:2 * C + 32], T.nx[:]))
 
         def cand_pick(h, n):
-            op("s", ["row%d" % n, "hv%d" % (n - 1)], ["kjr%d" % h], lambda: S.activation(
-                T.kjr[:, C * h:C * h + C], pick("row%d" % n, lst("hv%d" % (n - 1)), HC * h, HC), AF.Copy))
+            copy(["row", heads(n - 1)[0]], ["kjr%d" % h], T.kjr[:, C * h:C * h + C], pick("row", lst(*heads(n - 1)), C * h))
 
         def cand_scan(h):
-            op("v", ["kjr%d" % h, "hold"], ["kjs%d" % h], lambda: V.tensor_tensor_scan(
-                T.kjs[:, C * h:C * h + C], T.hold[:], T.kjr[:, C * h:C * h + C], 0.0, A.add, A.max))
+            a, n = runs(h)
+            op("v", each("kjr%d", h) + each("hold%d", h), each("kjs%d", h), lambda: V.tensor_tensor_scan(
+                T.kjs[:, C * a:C * (a + n)], T.hold[:, C * a:C * (a + n)], T.kjr[:, C * a:C * (a + n)], 0.0, A.add, A.max))
 
         def yadd(b):
-            op("v", ["xp%d" % b, to % (0, b), to % (1, b), "mw"], ["y%d" % b], lambda: V.tensor_tensor(
+            op("v", ["xp%d" % b, to % (0, b), to % (1, b), mw], ["y%d" % b], lambda: V.tensor_tensor(
                 T.y32[:, C * b:C * b + C], pick("xp", m1, C * b), T[xo][:, b:1280:4], A.add))
 
         def zpick(q, c, b):
-            a, n = runs(c)
-            out, in_ = T.zt[:, 640 * a + b:640 * (a + n):4], pick("y32", lst("mw", 10 * a, 10 * (a + n)), C * b)
-            toks = ["z%d%d" % (a + i, b) for i in range(n)]
+            a, e = span(c)
+            out, in_ = T.zt[:, 4 * a + b:4 * e:4], pick("y32", lst(mw, a // 16, e // 16), C * b)
             if q == "s":
-                op("s", ["y%d" % b, "mw"], toks, lambda: S.activation(out, in_, AF.Copy, scale=0.5))
+                op("s", ["y%d" % b, mw], each("z%%d%d" % b, c), lambda: S.activation(out, in_, AF.Copy, scale=0.5))
             else:
-                op("v", ["y%d" % b, "mw"], toks, lambda: V.tensor_scalar(out, in_, 0.5, None, A.mult))
+                op("v", ["y%d" % b, mw], each("z%%d%d" % b, c), lambda: V.tensor_scalar(out, in_, 0.5, None, A.mult))
 
         def layer(c):
-            quantise("qz", "sz", "zt", c, ["z%d%d" % (c, b) for b in range(4)])
+            quantise("qz", "sz", "zt", c, [t for b in range(4) for t in each("z%%d%d" % b, c)])
             for b in range(4):
-                product(4 * c + b, ("qw", "sw"), b, ("qz", "sz"), c, ["qz.%d" % c, "qw"])
+                product(4 * (c % 2) + b, ("qw", "sw"), b, ("qz", "sz"), c, each("qz.%d", c) + ["qw"])
 
         def send(out, in_, sem):
             g.remote_dma(out, in_, T.sem[sem], T.sem.lsem, pid, rid, mask)
@@ -341,80 +389,94 @@ def rank_program(g, core, T, topo):
         def send_h(c):
             quantise(qh, sh, "ht", c, ["h%d%d" % (c, b) for b in range(4)])
             order("g", ["%s.%d" % (qh, c)], [])
-            send(T[lc][:, HC * c:HC * c + HC].bitcast(dt.uint8), T[qh][:, HC * c:HC * c + HC].bitcast(dt.uint8), "a%dc%d" % (r, c))
-            send(T[ls][:, HC * c:HC * c + HC], T[sh][:, HC * c:HC * c + HC], "a%dc%d" % (r, c))
+            a, e = span(c)
+            send(T[lc][:, a:e].bitcast(dt.uint8), T[qh][:, a:e].bitcast(dt.uint8), "a%dc%d" % (r, c))
+            send(T[ls][:, a:e], T[sh][:, a:e], "a%dc%d" % (r, c))
+
+        def send_m():
+            ts(mw, "mf", "sub", None, A.subtract)
+            if str(r) not in OPT.get("fsend", ""):
+                order("g", [mw], [])
+                send(T[mp][:], T[mw][:], "a%df" % r)
 
         def send_f():
             wrapped(fw, "scf")
             order("g", [fw], [])
             send(T[fp][:], T[fw][:], "a%df" % r)
+            wrote[fp] = wrote[mp]
 
         def unpack(c):
             for b in range(4):
-                product(4 * c + b, ("qe", "se"), b, (lc, ls), c, ["ld%d" % c, "qe%d" % b])
+                product(4 * (c % 2) + b, ("qe", "se"), b, (lc, ls), c, each("ld%d", c) + ["qe%d" % b])
 
         def meet(c, b):
-            a, n = runs(c)
-            cols = slice(640 * a + b, 640 * (a + n), 4)
-            op("v", ["d0%d" % b, "d1%d" % b, "lw"] + [to % (a + i, b) for i in range(n)],
-               [tn % (a + i, b) for i in range(n)] + ["%s.%d%d" % (xn, a + i, b) for i in range(n)],
-               lambda: V.tensor_tensor(T[xn][:, cols], pick("dd", lst("lw", 10 * a, 10 * (a + n)), C * b), T[xo][:, cols], A.add))
+            (a, e), (k, n) = span(c), runs(c)
+            cols = slice(4 * a + b, 4 * e, 4)
+            op("v", ["d0%d" % b, "d1%d" % b, "lw"] + [to % (k + i, b) for i in range(n)],
+               [tn % (k + i, b) for i in range(n)] + ["%s.%d%d" % (xn, k + i, b) for i in range(n)],
+               lambda: V.tensor_tensor(T[xn][:, cols], pick("dd", lst("lw", a // 16, e // 16), C * b), T[xo][:, cols], A.add))
 
         def tails():
-            spick("tpr", "raw2", fp)
+            spick("raw0", "raw2", mp, K1, K1 + 20)
+            spick("tpr", "raw0", mp)
             dma("y", "ot", T.tp[:], T.tpr[0:128:16, :], rd=["tpr"])
 
         def ones(b):
-            op("v", ["et%d" % b], ["qe%d" % b], lambda: V.quantize_mx(
-                T.qe[:, 128 * b:128 * b + 128], T.se[:, 128 * b:128 * b + 128], T.et[:, 512 * b:512 * b + 512]))
+            op("v", ["et"], ["qe%d" % b], lambda: V.quantize_mx(
+                T.qe[:, 128 * b:128 * b + 128], T.se[:, 128 * b:128 * b + 128], T.et[:, 3 - b:515 - b]))
 
         def store_scales():
             for k in range(4):
-                dma("y", "oq", T.osc[4 * k:4 * k + 4, :], T.so[32 * k:32 * k + 4, :], rd=["qo.0", "qo.1"], total=OPT.get("oq", 80))
+                dma("y", "oq", T.osc[4 * k:4 * k + 4, :], T.so[32 * k:32 * k + 4, :], rd=["qo.0", "qo.1"], total=OPT["oq"])
 
         def store_codes(c):
-            a, n = runs(c)
-            dma("y", "oq", T.oc[:, 640 * a:640 * (a + n)], T.qo[:, HC * a:HC * (a + n)].bitcast(dt.uint8),
-                rd=["qo.%d" % (a + i) for i in range(n)], total=OPT.get("oq", 80))
+            a, e = span(c)
+            dma("y", "oq", T.oc[:, 4 * a:4 * e], T.qo[:, a:e].bitcast(dt.uint8), rd=each("qo.%d", c), total=OPT["oq"])
 
         steps = {
-            "enc": places, "et": units, "turn": turn, "f": send_f, "tp": tails, "os": store_scales,
+            "cut": lambda: recut(192), "encf": lambda: places(3), "g2s": lambda: affine("g2", "rr", 2.0, -1.0), "enc": lambda: places(0), "heads": lambda: places(1), "sib": lambda: places(2), "et": units, "turn": turn,
+            "mw": send_m, "tp": tails, "os": store_scales,
             "gm": lambda: op("v", ["tt0", "tt1", "tof", "kd0", "kd1"], ["mt"], lambda: V.tensor_tensor(
-                T.mt[:], pick("tt", lst("tof", 0, 3), 0, 2 * C + 32), T.kd[:], A.mult)),
-            "ad": lambda: op("v", ["mt", "k10", "k11"], ["mf"], lambda: V.tensor_tensor(T.mf[:], T.mt[:], T.k1[:], A.add)),
-            "mw": lambda: ts("mw", "mf", "sub", None, A.subtract), "fs": lambda: scan("scf", "fr"),
+                T.mt[:], pick("tt", lst("tof", 0, 3), 0, 2 * C + 32), T.kk[:, 0:48], A.mult)),
+            "ad": lambda: op("v", ["mt", "k10", "k11"], ["mf"], lambda: V.tensor_tensor(T.mf[:], T.mt[:], T.kk[:, 48:96], A.add)),
+            "m1p": lambda: spick("m1p", "cio", mp, K1, K1 + 20), "fpr": lambda: spick("fpr", "m1p", mp),
+            "lm": lambda: [spick("m1p", "fr", mp, K1, K1 + 20), spick("lr", "m1p", mp)],
+            "FS": lambda: scan("scf", "fr"), "F": send_f,
+            "TP": lambda: [spick("tpr", "raw2", fp), dma("y", "ot", T.tp[:], T.tpr[0:128:16, :], rd=["tpr"])],
+            "fs": lambda: scan("scf", "fpr"), "f": lambda: wrapped(fp, "scf"),
             "qu": lambda: op("v", ["ut"], ["qu"], lambda: V.quantize_mx(T.qu[:], T.su[:], T.ut[:])),
             "qv": lambda: op("v", ["vt"], ["qv"], lambda: V.quantize_mx(T.qv[:], T.sv[:], T.vt[:])),
             "mm": lambda: [product(c, ("qu", "su"), 0, ("qx", "sx"), c, ["qx.%d" % c, "qu"]) for c in (0, 1)],
-            "pg": lambda: [plane("g", b) for b in range(4)],
+            "mm2": lambda: product(0, ("qu", "su"), 0, ("qx", "sx"), 2, ["qx.0", "qx.1", "qu"]),
+            "pg": lambda: [plane(b) for b in range(4)],
             "li": lambda: lower(0, ai), "lo": lambda: lower(1, ao), "hi": lambda: higher(0, ai), "ho": lambda: higher(1, ao),
             "sum": lambda: op("v", ["bit0", "bit1", "alt"], ["sum"], lambda: V.tensor_tensor_scan(T["sum"][:], T.alt[:], T.bit[:], 0.0, A.mult, A.add)),
-            "nx": lambda: straight("s", 2), "nxs": lambda: straight("s", 0), "nxv": lambda: straight("v", 1),
+            "nx": lambda: straight(eng[0], 2), "nxs": lambda: straight("s", 0), "nxv": lambda: straight("v", 1),
             "rs": lambda: scan("scr", "ajr"),
             "rr": lambda: op("v", ["scr", "ciw"], ["rr"], lambda: V.tensor_tensor(T.rr[:], T.scr[:, 15:C:16], T.ciw[:], A.is_lt)),
-            "g2": lambda: affine("g2", "rr", 2.0, -1.0), "g2v": lambda: ts("g2", "rr", 2.0, -1.0, A.mult, A.add),
+            "g2": lambda: ts("g2", "rr", 2.0, -1.0, A.mult, A.add),
             "dd": lambda: op("v", ["kjs0", "kjs1"], ["ddc"], lambda: V.tensor_tensor(T.ddc[:], hi_out, lo_out, A.subtract)),
             "kq": lambda: tt("kq", "ddc", "rr", A.mult),
             "kd": lambda: both("kd", T.ddc[:], "ddc", T.g2[:], "g2", A.mult),
             "k1": lambda: both("k1", hi_out, "kjs1", T.kq[:], "kq", A.subtract),
-            "m1r": lambda: spick("m1r", "cio", "mw", K1, K1 + 20), "fr": lambda: spick("fr", "m1r", "mw"),
+            "m1r": lambda: spick("m1r", "cio", mw, K1, K1 + 20), "fr": lambda: spick("fr", "m1r", mw),
             "lr": lambda: spick("lr", "fr", fp), "ls": lambda: scan("scl", "lr"), "lw": lambda: wrapped("lw", "scl"),
             "fi": lambda: op("v", [fp, "cio"], ["fi"], lambda: V.tensor_copy(T.fi[:, 0:C].indirect(lst(fp)), T.cio[:])),
-            "hvr": lambda: spick("hvr", "cio", "hv0"), "tr": lambda: spick("tr", "hvr", "fp1"),
-            "hs": lambda: scan("sch", "tr"), "hw": lambda: wrapped("hv2", "sch"),
-            "hvs": lambda: ts("hvs2", "hv2", 2.0, 1.0, A.mult, A.add),
+            "hvr": lambda: spick("hvr", "cio", "hvs"), "tr": lambda: spick("tr", "hvr", "fp1"),
+            "hs": lambda: scan("sch", "tr"), "hw": lambda: wrapped("hvs2", "sch"),
             "hu": lambda: op("v", ["hlt"], ["hu"], lambda: V.tensor_copy(T.hu[:], T.hlt[:, 0:20])),
             "raw": lambda: [spick("raw0", "cio", "hu"), spick("raw2", "raw0", "fp1")],
-            "ym": lambda: [product(c, ("qv", "sv"), 0, ("qo", "so"), c, ["qo.%d" % c, "qv"]) for c in (0, 1)],
-            "oc": lambda: store_codes(2),
+            "ks": lambda: cand_scan(2), "l2": lambda: layer(2), "u2": lambda: unpack(2),
+            "q": lambda: quantise("qx", "sx", xo, 2, [to % (c, b) for c in (0, 1) for b in range(4)]),
         }
         for n in range(4):
             steps.update({
-                "scat%d" % n: lambda n=n: scatter(n), "heads%d" % n: lambda n=n: heads(n), "rp%d" % n: lambda n=n: role_pick(n),
-                "vs%d" % n: lambda n=n: scan("scv", "pr%d" % n), "vm%d" % n: lambda n=n: sort2(n), "vc%d" % n: lambda n=n: sorted_list(n),
-                "row%d" % n: lambda n=n: spick("row%d" % n, "cio", "lhu%d" % n),
-                "pr%d" % n: lambda n=n: spick("pr%d" % n, "fi", "lhu%d" % (n - 2)),
-                "qe%d" % n: lambda n=n: ones(n), "ps%d" % n: lambda n=n: plane("s", n), "y%d" % n: lambda n=n: yadd(n), "a%d" % n: lambda n=n: meet(2, n),
+                "scat%d" % n: lambda n=n: scatter(n), "rp%d" % n: lambda n=n: role_pick(n),
+                "vs%d" % n: lambda n=n: scan("scv%d" % (n % 2), "pr%d" % (n % 2)),
+                "vm%d" % n: lambda n=n: sort2(n), "vc%d" % n: lambda n=n: sorted_list(n),
+                "row%d" % n: lambda n=n: spick("row", "cio", "lhu%d" % n, pairs=True),
+                "pr%d" % n: lambda n=n: spick("pr%d" % (n % 2), "fi", "lhu%d" % (n - 2)),
+                "qe%d" % n: lambda n=n: ones(n), "y%d" % n: lambda n=n: yadd(n), "a%d" % n: lambda n=n: meet(2, n),
             })
         for c in (0, 1):
             steps.update({
@@ -423,24 +485,29 @@ def rank_program(g, core, T, topo):
                 "ks%d" % c: lambda c=c: cand_scan(c), "l%d" % c: lambda c=c: layer(c), "send%d" % c: lambda c=c: send_h(c),
                 "u%d" % c: lambda c=c: unpack(c), "oc%d" % c: lambda c=c: store_codes(c),
                 "ym%d" % c: lambda c=c: product(c, ("qv", "sv"), 0, ("qo", "so"), c, ["qo.%d" % c, "qv"]),
-                "oy%d" % c: lambda c=c: dma("s", "oy", T.y[:, HC * c:HC * c + HC], T.yo[:, HC * c:HC * c + HC], rd=["yo%d" % c], total=32),
+                "oy%d" % c: lambda c=c: dma("s", "oy", T.y[:, slice(*span(c))], T.yo[:, slice(*span(c))], rd=["yo%d" % c], total=32),
             })
             for b in range(4):
                 steps["a%d%d" % (c, b)] = lambda c=c, b=b: meet(c, b)
         for part in "abc":
             for c in (0, 1):
                 steps["kp%d" % c] = lambda c=c: cand_pick(c, r + (part == "c"))
+            for c in (0, 1, 2):
+                a, e = span(c)
                 for q in "sv":
                     res = "yo" if part == "c" else "sk"
-                    steps["e%s%d" % (q, c)] = lambda q=q, c=c, res=res: evac(q, T[res][:, HC * c:HC * c + HC], c, "%s%d" % (res, c))
+                    steps["e%s%d" % (q, c)] = lambda q=q, c=c, res=res: evac(
+                        q, T[res][:, slice(*span(c))], c % 2, each(res + "%d", c), span(c)[1] - span(c)[0])
                     for b in range(4):
+                        steps["u%d%d" % (c, b)] = lambda c=c, b=b: product(
+                            4 * (c % 2) + b, ("qe", "se"), b, (lc, ls), c, each("ld%d", c) + ["qe%d" % b])
                         steps["z%s%d%d" % (q, c, b)] = lambda q=q, c=c, b=b: zpick(q, c, b)
-                        steps["z%s2%d" % (q, b)] = lambda q=q, b=b: zpick(q, 2, b)
-                        steps["h%s%d%d" % (q, c, b)] = lambda q=q, c=c, b=b: evac(
-                            q, T.ht[:, 640 * c + b:640 * c + 640:4], 4 * c + b, "h%d%d" % (c, b), 0.03125)
-                        steps["d%s%d%d" % (q, c, b)] = lambda q=q, c=c, b=b: evac(
-                            q, T.dd[:, C * b + HC * c:C * b + HC * c + HC], 4 * c + b, "d%d%d" % (c, b))
+                        steps["h%s%d%d" % (q, c, b)] = lambda q=q, c=c, a=a, e=e, b=b: evac(
+                            q, T.ht[:, 4 * a + b:4 * e:4], 4 * (c % 2) + b, each("h%%d%d" % b, c), e - a, 0.03125)
+                        steps["d%s%d%d" % (q, c, b)] = lambda q=q, c=c, a=a, e=e, b=b: evac(
+                            q, T.dd[:, C * b + a:C * b + e], 4 * (c % 2) + b, each("d%%d%d" % b, c), e - a)
             for w in OPT["%s%d" % (part, r)].split():
-                steps[w]()
+                eng[0] = "v" if w.endswith("!") else "s"
+                steps[w.rstrip("!")]()
     for sem in sorted(cnt):
         need("g", sem, cnt[sem])

@@ -4,55 +4,43 @@ A = AluOpType
 AF = ActivationFunctionType
 C = 320
 HC = 160
+CUT = 160
 STEP = [1, 2, 4]
 CODE = "float8_e4m3fn_x4"
-K1 = 24
+NP, NQ = 81, 41
+PAD = 64
 
-LAYER = "m1r fr y0 y1 y2 FS y3 F zs20 zs21 zs02 zv03 zs12 l0 zs13 l1 hv00 hs01 hv02 hs03 send0 hs10 hs11 hv12 hs13 send1"
-RUNS = "u0 ds00 ds01 ds02 ds03", "u1 dv10 ds11 ds12 ds13"
-OPT = {"oq": 96, "fsend": "123", "cut": 192}
-OPT["a1"] = ("encf scat1 qu vs1 q0 vm1 q1 vc1 pg et mm es0 es1 row1 scat0 lo rp0 kp0 vs0 ho vm0 rs vc0 li kp1 ks0 rr hi g2 sum nx "
-             "ks1 dd kq kd k1 turn rp1 gm ad mw")
-OPT["b1"] = LAYER.replace("send0", "qe0 send0").replace("send1", "qe1 send1")
-OPT["c1"] = "qe2 qe3 rs hvr rr lr fi ls g2 lw pr2 vs2 vm2 vc2 %s %s row2 kp0 kp1 tr a0 a1 a2 a03 a13" % RUNS
-OPT["a2"] = "q0 q1 pg mm es0 es1 ks0 ks1 li lo dd hi kq ho kd sum k1 nxs nxv turn gm ad mw"
-OPT["b2"] = LAYER
-OPT["c2"] = "lr fi pr3 ls hs lw hw rp2 vs3 vm3 vc3 %s %s row3 kp0 kp1 a0 a1 a2 a03 a13" % RUNS
-OPT["a3"] = "q0 q1 pg mm es0 es1 ks0 ks1 li lo rs dd hi rr ho sum nx g2 kq kd k1 turn gm ad mw"
-OPT["b3"] = "m1r y0 y1 y2 y3 zs20 zs21 fr zs02 zv03 zs12 l0 FS zs13 l1 F hs00 hv01 hs02 hs03 send0 hs10 hv11 hs12 hv13 send1"
-OPT["c3"] = "hu raw qv lr ls lw %s %s TP a00 a01 a02 a03 a10 o0 oc0 ym0 es0 oy0 a11 a12 a13 o1 ym1 oc1 os ev1 oy1" % RUNS
-OPT.update({
-    "cut": 160, "uq": "y",
-    "a1": "encf scat1 q0 vs1 q1 vm1 qu vc1 pg et row1 mm es0 es1 kp0 scat0 lo vs0 vm0 vc0 ks0 li ho rp0 kp1 hi sum rs nx rr ks1 g2 dd turn kq kd k1 rp1 gm ad mw",
-    "b1": "m1r fr y0 y1 y2 FS y3 F zs20 zs21 zs22 zv03 zs13 l0 qe0 l1 qe1 hs00 hv01 hs02 hv03 send0 hs10 hs11 hs12 hv13 send1",
-    "c1": "qe2 qe3 hvr lr tr fi ls pr2 rs lw rr %s vs2 g2 vm2 %s vc2 a0 row2 kp0 kp1 a1 a2 a03 a13" % RUNS,
-    "a2": "q0 q1 pg mm es0 es1 ks hs li lo dd hw hi kq ho sum kd nxs nxv k1 turn rp2 gm ad mw",
-    "b2": "m1r fr y0 y1 y2 y3 zv03 FS zs20 zs21 zs02 zs12 zs13 l0 F l1 hs00 hv01 hs02 hv03 send0 hs10 hs11 hv12 hv13 send1",
-    "c2": "lr fi pr3 ls rs lw rr %s vs3 g2 vm3 %s vc3 a0 row3 kp0 kp1 a1 a2 a03 a13" % RUNS,
-    "a3": "q0 q1 pg mm es0 es1 ks li lo dd kq kd k1 hi ho sum nxs nxv turn gm ad mw",
-    "b3": "m1r y0 y1 y2 y3 zs20 fr zs21 zs02 zv03 zs12 l0 FS zs13 l1 F hs00 hv01 hs02 hv03 send0 hs10 hs11 hv12 hv13 send1",
-    "c3": "hu raw qv lr ls lw %s %s TP cut a00 a01 a02 a03 a10 o0 oc0 ym0 es0 oy0 a11 a12 a13 o1 ym1 oc1 os es1 oy1" % RUNS,
-})
+SCORES = "pg q0 q1 mm es0 ta wrap ev1 li tc nd hi lo rho ho g2 kq sum k1 nxs nxv kd turn"
+LISTS = "g1 g0 m1 m0"
+MEET = "a0 a1 a2 a03 a13"
+ORDER = {
+    "a1": "enc oneg hv own sub altg low sg scat pg qu half q0 et q1 mn mk mm heads cp ta es0 ev1 wrap tc li rho lo nd hi kq ho g2 k1 sum "
+          "nxs kd nxv turn hold " + LISTS,
+    "b1": "m1r fr y0 y1 y2 y3 zs20 zs21 zs22 FS zv03 F l0 qe0 zs13 hs00 l1 qe3 hs02 qe1 hv01 hv03 send0 hs10 qe2 hv11 hs12 hv13 send1",
+    "c1": "sub4 u0 u1 fi lr pr ls lw hu dv01 ds00 dv02 ds03 mn ds11 ds12 ds13 dv10 cp hvr " + MEET,
+    "a2": SCORES + " tr " + LISTS,
+    "b2": "x1 ps0 y0 zs00 ps1 y1 zs01 y2 Z0 m1v zs02 l0 Z1 zv12 zs10 zs11 l1 fr hs00 hs01 hs02 FS hs10 hv03 F send0 lr hv11 hv12 hv13 send1",
+    "c2": "u0 u1 fi hs ls pr hw lw ds00 mn ds02 dv10 ds03 ds11 ds12 ds13 dv01 cp " + MEET,
+    "a3": SCORES + " " + LISTS,
+    "b3": "y0 x1 ps0 y1 zs00 ps1 y2 zs01 M zs02 zs10 Z0 Z1 l0 zv12 zs11 m1r l1 hv00 hs01 hv02 fr hs10 hv03 send0 hv11 hs12 hv13 send1",
+    "c3": "lm1 lm0 ls raw qv lw u0 u1 dv00 ds01 dv02 ds03 dv10 ds11 ds12 ds13 tm1 tm0 " + MEET + " o0 oc0 ym0 o1 ym1 es0 oc1 os ev1 oy0 oy1",
+}
 
 SCRATCH = {
+    "pmi": ("sbuf", [128, 8], "int32"), "pma": ("sbuf", [128, 8], "int32"), "thr": ("sbuf", [128, 5], "float32"),
     "cio": ("sbuf", [128, 320], "float32"), "j16": ("sbuf", [128, 320], "bfloat16"), "mk": ("sbuf", [128, 320], "float32"),
-    "sg": ("sbuf", [128, 320], "bfloat16"),
-    "hold": ("sbuf", [128, 640], "float32"), "alt": ("sbuf", [128, 320], "bfloat16"),
-    "pmi": ("sbuf", [128, 2], "int32"), "pma": ("sbuf", [128, 2], "int32"), "sub": ("sbuf", [128, 1], "float32"),
-    "i17": ("sbuf", [128, 2], "int32"), "s16": ("sbuf", [128, 2], "int32"), "s21": ("sbuf", [128, 1], "float32"),
-    "pmf": ("sbuf", [128, 1], "float32"), "p16": ("sbuf", [128, 1], "float32"), "cs": ("sbuf", [128, 1], "float32"),
-    "c16": ("sbuf", [128, 20], "float32"), "ciw": ("sbuf", [128, 20], "float32"),
-    "n16": ("sbuf", [128, 4], "float32"), "n24": ("sbuf", [128, 4], "float32"), "n48": ("sbuf", [128, 4], "float32"),
-    "c256": ("sbuf", [128, 4], "float32"), "tof": ("sbuf", [128, 4], "uint16"),
+    "sg": ("sbuf", [128, 320], "bfloat16"), "hold": ("sbuf", [128, 320], "float32"), "alt": ("sbuf", [128, 320], "bfloat16"),
+    "pay": ("sbuf", [128, 640], "bfloat16"), "rst": ("sbuf", [128, 640], "bfloat16"), "half": ("sbuf", [128, 320], "float32"),
+    "c16": ("sbuf", [128, 42], "float32"), "ciw": ("sbuf", [128, 42], "float32"),
+    "tfi": ("sbuf", [128, 6], "float32"), "tov": ("sbuf", [128, 4], "uint16"),
     "one": ("sbuf", [128, 516], "bfloat16"), "et": ("sbuf", [128, 516], "bfloat16"),
     "qe": ("sbuf", [128, 512], CODE), "se": ("sbuf", [128, 512], "uint8"),
     "ut": ("sbuf", [128, 512], "bfloat16"), "vt": ("sbuf", [128, 512], "bfloat16"),
     "qu": ("sbuf", [128, 128], CODE), "su": ("sbuf", [128, 128], "uint8"),
     "qv": ("sbuf", [128, 128], CODE), "sv": ("sbuf", [128, 128], "uint8"),
     "qw": ("sbuf", [128, 512], CODE), "sw": ("sbuf", [128, 512], "uint8"),
-    "hlt": ("sbuf", [128, 40], "int32"), "hb": ("sbuf", [128, 40], "int32"), "hv": ("sbuf", [128, 40], "int32"),
-    "hb2": ("sbuf", [128, 40], "int32"), "enci": ("sbuf", [128, 40], "int32"), "spi": ("sbuf", [128, 40], "int32"),
-    "enc": ("sbuf", [128, 40], "uint16"), "sp": ("sbuf", [128, 40], "uint16"), "hu": ("sbuf", [128, 20], "uint16"),
+    "hlt": ("sbuf", [128, 40], "int32"), "hv": ("sbuf", [128, 40], "int32"),
+    "enc": ("sbuf", [128, 40], "uint16"), "hu": ("sbuf", [128, 20], "uint16"),
     "xp": ("sbuf", [128, 1280], "bfloat16"), "y32": ("sbuf", [128, 1280], "float32"), "zt": ("sbuf", [128, 1280], "bfloat16"),
     "ht": ("sbuf", [128, 1280], "bfloat16"), "dd": ("sbuf", [128, 1280], "bfloat16"),
     "qz": ("sbuf", [128, 320], CODE), "sz": ("sbuf", [128, 320], "uint8"),
@@ -61,34 +49,34 @@ SCRATCH = {
     "yo": ("sbuf", [128, 320], "float32"), "tpr": ("sbuf", [128, 320], "float32"),
     "ps": ("psum", [128, 4096], "float32"),
     "sk": ("sbuf", [128, 320], "float32"), "ga": ("sbuf", [128, 320], "float32"), "bit": ("sbuf", [128, 320], "bfloat16"),
-    "sum": ("sbuf", [128, 320], "bfloat16"), "nx": ("sbuf", [128, 352], "bfloat16"), "tt": ("sbuf", [128, 672], "bfloat16"),
-    "kk": ("sbuf", [128, 96], "float32"),
-    "pr0": ("sbuf", [128, 320], "float32"), "pr1": ("sbuf", [128, 320], "float32"), "row": ("sbuf", [128, 640], "float32"),
+    "pr": ("sbuf", [128, 640], "bfloat16"), "ro": ("sbuf", [128, 640 + 2 * PAD], "bfloat16"),
+    "nx": ("sbuf", [128, 688], "bfloat16"), "tt": ("sbuf", [128, 672], "bfloat16"), "tv": ("sbuf", [128, 352], "bfloat16"),
+    "tc": ("sbuf", [128, 672], "bfloat16"), "kk": ("sbuf", [128, 82], "float32"),
     "hvs": ("sbuf", [128, 40], "uint16"), "hvs2": ("sbuf", [128, 20], "uint16"),
-    "mt": ("sbuf", [128, 48], "float32"), "mf": ("sbuf", [128, 48], "float32"),
-    "m1p": ("sbuf", [128, 320], "float32"), "fpr": ("sbuf", [128, 320], "float32"),
-    "fi": ("sbuf", [128, 320], "float32"), "g2": ("sbuf", [128, 20], "float32"), "rr": ("sbuf", [128, 20], "float32"),
+    "ms": ("sbuf", [128, 224], "float32"), "tom": ("sbuf", [128, 2], "uint16"),
+    "fi": ("sbuf", [128, 320], "bfloat16"), "x0h": ("sbuf", [128, 320], "bfloat16"), "x1h": ("sbuf", [128, 320], "bfloat16"),
     "m1r": ("sbuf", [128, 320], "float32"), "fr": ("sbuf", [128, 320], "float32"), "lr": ("sbuf", [128, 320], "float32"),
-    "lw": ("sbuf", [128, 20], "uint16"), "ajr": ("sbuf", [128, 320], "float32"),
-    "kjr": ("sbuf", [128, 640], "float32"), "kjs": ("sbuf", [128, 640], "float32"),
-    "ddc": ("sbuf", [128, 20], "float32"), "kq": ("sbuf", [128, 20], "float32"),
+    "lw": ("sbuf", [128, 20], "uint16"),
     "tr": ("sbuf", [128, 320], "float32"), "hvr": ("sbuf", [128, 320], "float32"),
     "raw0": ("sbuf", [128, 320], "float32"), "raw2": ("sbuf", [128, 320], "float32"),
-    "lohi": ("sbuf", [128, 40], "float32"),
 }
-for _n in ("v0", "v1", "r", "h", "f", "l"):
+for _n in ("p16", "pmf", "sign", "sub", "sub4", "pe", "pv", "low", "nlow"):
+    SCRATCH[_n] = ("sbuf", [128, 1], "float32")
+for _n in ("rho", "g2", "nd", "kq"):
+    SCRATCH[_n] = ("sbuf", [128, NQ], "float32")
+for _n in ("h", "f", "l"):
     SCRATCH["sc" + _n] = ("sbuf", [128, 320], "float32")
 for _k in (0, 1):
     SCRATCH["xi%d" % _k] = ("sbuf", [128, 1280], "bfloat16")
-for _n in range(4):
-    SCRATCH["lhu%d" % _n] = ("sbuf", [128, 20], "uint16")
 for _r in (1, 2, 3):
     SCRATCH["qh%d" % _r] = ("sbuf", [128, 320], CODE)
     SCRATCH["sh%d" % _r] = ("sbuf", [128, 320], "uint8")
     SCRATCH["lc%d" % _r] = ("sbuf", [128, 320], CODE)
     SCRATCH["ls%d" % _r] = ("sbuf", [128, 320], "uint8")
-    SCRATCH["mw%d" % _r] = ("sbuf", [128, 48], "uint16")
-    SCRATCH["mp%d" % _r] = ("sbuf", [128, 48], "uint16")
+    SCRATCH["mw%d" % _r] = ("sbuf", [128, 64], "uint16")
+    SCRATCH["mp%d" % _r] = ("sbuf", [128, 52], "uint16")
+    SCRATCH["lo%d" % _r] = ("sbuf", [128, 32], "uint16")
+    SCRATCH["hi%d" % _r] = ("sbuf", [128, 32], "uint16")
     SCRATCH["fw%d" % _r] = ("sbuf", [128, 20], "uint16")
     SCRATCH["fp%d" % _r] = ("sbuf", [128, 20], "uint16")
 
@@ -156,133 +144,106 @@ def rank_program(g, core, T, topo):
         return T.ps[:, 512 * k:512 * k + n]
 
     def lst(name, a=0, b=20):
+        if name[:2] in ("ma", "mb"):
+            return T["mw" + name[2:]][:, a + 32 * (name[1] == "b"):b + 32 * (name[1] == "b")]
         return T[name][:, a:b]
 
     def pick(name, off, a=0, n=C):
         return T[name][:, a:a + n].indirect(off)
 
-    def ts(out, in_, s1, s2, *ops, to=None):
+    def ts(out, in_, s1, s2, *ops, to=None, rd=None, wr=None):
         names = [s for s in (s1, s2) if isinstance(s, str)]
         a, b = [T[s][:] if isinstance(s, str) else s for s in (s1, s2)]
-        op("v", [in_] + names, [out], lambda: V.tensor_scalar(T[out][:] if to is None else to[0], T[in_][:] if to is None else to[1], a, b, *ops))
+        o, i = to or (T[out][:], T[in_][:])
+        op("v", (rd or [in_]) + names, wr or [out], lambda: V.tensor_scalar(o, i, a, b, *ops))
 
-    def tt(out, in0, in1, o):
-        op("v", [in0, in1], [out], lambda: V.tensor_tensor(T[out][:], T[in0][:], T[in1][:], o))
-
-    def affine(out, in_, scale, bias):
+    def affine(out, in_, scale, bias, view=None):
+        i = T[in_][:] if view is None else view
         if isinstance(bias, str):
-            op("s", [in_, bias], [out], lambda: S.activation(T[out][:], T[in_][:], AF.Identity, bias=T[bias][:], scale=scale))
+            op("s", [in_, bias], [out], lambda: S.activation(T[out][:], i, AF.Identity, bias=T[bias][:], scale=scale))
         else:
-            op("s", [in_], [out], lambda: S.activation(T[out][:], T[in_][:], AF.Copy, bias=bias, scale=scale))
+            op("s", [in_], [out], lambda: S.activation(T[out][:], i, AF.Copy, bias=bias, scale=scale))
+
+    def count(name, out, pattern, base=0, by=0):
+        op("g", [], [name], lambda: g.iota(out, pattern, base, by, allow_small_or_imprecise_dtypes=True))
 
     dma("s", "dl", T.hlt[:, 0:20], T.hl[:], wr=["hlt"], total=32)
     dma("y", "dl", T.hlt[:, 20:40], T.tl[:], total=32)
     dma("y", "dx", T.xi0[:], T.x[:], wr=["x0.%d%d" % (c, b) for c in (0, 1) for b in range(4)])
-    dma(OPT.get("uq", "s"), "du", T.ut[:], T.u[:], wr=["ut"])
+    dma("y", "du", T.ut[:], T.u[:], wr=["ut"])
     dma("y", "dw", T.qw[:].bitcast(dt.uint8), T.wc[:], wr=["qw"], total=32)
     dma("y", "dw", T.sw[:], T.ws[:], total=32)
     dma("y", "dv", T.vt[:], T.v[:], wr=["vt"])
 
-    op("g", [], ["pmi"], lambda: g.iota(T.pmi[:], [[0, 2]], 0, 1))
-    op("g", [], ["i17"], lambda: g.iota(T.i17[:], [[0, 2]], 0, 17))
-    for name, pattern in (("c256", [[256, 4]]), ("j16", [[0, 20], [1, 16]]), ("cio", [[1, C]]), ("c16", [[16, 20]]),
-                          ("row", [[0, C]]), ("alt", [[0, HC], [1, 2]])):
-        out = T.row[:, 0:2 * C:2] if name == "row" else T[name][:]
-        op("g", [], [name], lambda: g.iota(out, pattern, 0, 0, allow_small_or_imprecise_dtypes=True))
-    op("v", [], ["nx0", "nx1"], lambda: V.memset(T.nx[:], 0.0))
-    ts("pma", "pmi", 15, None, A.bitwise_and)
-    op("v", [], ["kd0", "kd1", "k10", "k11"], lambda: V.memset(T.kk[:], 0.0))
-    ts("s16", "i17", 16, None, A.bitwise_and)
-    ts("p16", "pma", 16.0, None, A.mult, to=(T.p16[:], T.pma[:, 0:1]))
-    ts("pmf", "pma", 1.0, None, A.mult, to=(T.pmf[:], T.pma[:, 0:1]))
-    ts("s21", "s16", 21.0, None, A.mult, to=(T.s21[:], T.s16[:, 0:1]))
-    ts("n16", "c256", "p16", None, A.add)
-    ts("n24", "n16", 16.0 * K1, 1.0 - 16.0 * K1, A.is_ge, A.mult)
-    tt("n48", "n16", "n24", A.add)
-    ts("tof", "n48", "s21", 671.0, A.add, A.min)
-    affine("sub", "pmf", -512.0, 7680.0)
-    if OPT.get("old"):
-        ts("mk", "j16", "pmf", 16384.0, A.not_equal, A.mult)
-    else:
-        op("s", ["j16", "pmf"], ["sg"], lambda: S.activation(T.sg[:], T.j16[:], AF.Sign, bias=T.pmf[:], scale=-1.0))
-        op("s", ["sg"], ["mk"], lambda: S.activation(T.mk[:], T.sg[:], AF.Square, scale=128.0))
-    op("s", ["mk"], ["hold0"], lambda: S.activation(T.hold[:, 0:C], T.mk[:], AF.Copy, bias=512.0 - 128.0 ** 2))
-    affine("cs", "pmf", -511.0, 7680.0)
-    affine("ciw", "c16", 1.0, "cs")
+    op("g", [], ["pmi0"], lambda: g.iota(T.pmi[:, 0:3], [[64, 3]], 0, 64))
+    op("g", [], ["pmi1"], lambda: g.iota(T.pmi[:, 3:4], [[0, 1]], 0, 136))
+    op("g", [], ["pmi2"], lambda: g.iota(T.pmi[:, 4:5], [[0, 1]], 0, 16))
+    count("cio", T.cio[:], [[1, C]], -HC)
+    count("tfi1", T.tfi[:, 2:6], [[2, 2], [3, 2]])
+    count("tfi0", T.tfi[:, 0:2], [[256, 2]])
+    count("c16", T.c16[:], [[0, 2], [16, 21]], -HC)
+    count("rst", T.rst[:], [[0, HC], [-1024, 4]], 512)
+    count("j16", T.j16[:], [[0, 20], [16, 16]])
+    op("v", [], ["nx0", "nx1", "nc"], lambda: V.memset(T.nx[:], 0.0))
+    ts("pma", "pmi", 240, None, A.bitwise_and, to=(T.pma[:, 0:5], T.pmi[:, 0:5]), rd=["pmi0", "pmi1", "pmi2"])
+    op("v", [], ["ro"], lambda: V.memset(T.ro[:, 3:2 * C + 2 * PAD:4], 0.0))
+    ts("thr", "pma", 128.0, 512.0, A.is_ge, A.mult, to=(T.thr[:], T.pma[:, 0:5]))
+    ts("p16", "pma", 1.0, None, A.mult, to=(T.p16[:], T.pma[:, 4:5]))
+    op("v", [], ["ms0", "ms1"], lambda: V.memset(T.ms[:], 0.0))
+    ts("sign", "thr", -1.0 / 256, 1.0, A.mult, A.add, to=(T.sign[:], T.thr[:, 1:2]))
+    for name, n in (("pe", C), ("pv", HC)):
+        ts(name, "thr", (n + 16) / 512, "p16", A.mult, A.add, to=(T[name][:], T.thr[:, 3:4]))
+    op("s", ["cio", "sign", "thr"], ["pay1"], lambda: S.activation(T.pay[:, C:2 * C], T.cio[:], AF.Identity, bias=T.thr[:, 0:1], scale=T.sign[:]))
+    op("v", ["cio", "sign", "thr"], ["pay0"], lambda: V.tensor_scalar(T.pay[:, 0:C], T.cio[:], T.sign[:], T.thr[:, 2:3], A.mult, A.add))
+    ts("tov", "tfi", "pv", 2 * HC + 31.0, A.add, A.min, to=(T.tov[:], T.tfi[:, 2:6]), rd=["tfi1"])
+    ts("tom", "tfi", "pe", 1.0 / 8, A.add, A.mult, to=(T.tom[:], T.tfi[:, 0:2]), rd=["tfi0"])
+
+    later = {
+        "own": lambda: [affine("pmf", "p16", 1.0 / 16, 0.0), affine("ciw", "c16", 1.0, "pmf")],
+        "low": lambda: [affine("low", "thr", -1.0 / 512, 1.0, T.thr[:, 4:5]),
+                        affine("nlow", "thr", 1.0 / 512, -1.0, T.thr[:, 4:5])],
+        "sub": lambda: affine("sub", "p16", -32.0, 7680.0 - HC), "sub4": lambda: affine("sub4", "p16", -32.0, 7680.0 - 0.75),
+        "sg": lambda: op("s", ["j16", "p16"], ["sg"], lambda: S.activation(T.sg[:], T.j16[:], AF.Sign, bias=T.p16[:], scale=-1.0)),
+        "mk": lambda: op("s", ["sg"], ["mk"], lambda: S.activation(T.mk[:], T.sg[:], AF.Square, scale=128.0)),
+        "hold": lambda: affine("hold", "mk", 1.0, 512.0 - 128.0 ** 2),
+        "alt": lambda: affine("alt", "rst", -1.0 / 2048, 0.25, T.rst[:, 0:2 * C:2]),
+        "altg": lambda: count("alt", T.alt[:], [[0, HC], [1, 2]]),
+        "one": lambda: affine("one", "rst", 0.0, 1.0, T.rst[:, 0:516]),
+        "oneg": lambda: count("one", T.one[:], [[0, 516]], 1),
+        "half": lambda: count("half", T.half[:], [[1, HC], [0, 2]]),
+        "et": lambda: op("g", ["one"], ["et"], lambda: g.affine_select(T.et[:], T.one[:], [[-1, 516]], A.is_equal, 0.0, 3, 4)),
+    }
 
     def scan(b, row):
-        op("v", [row, "hold0"], [b], lambda: V.tensor_tensor_scan(T[b][:], T.hold[:, 0:C], T[row][:], 0.0, A.add, A.max))
+        op("v", [row, "hold"], [b], lambda: V.tensor_tensor_scan(T[b][:], T.hold[:], T[row][:], 0.0, A.add, A.max))
 
     def wrapped(out, b):
-        op("v", [b, "sub"], [out], lambda: V.tensor_scalar(T[out][:], T[b][:, 15:C:16], T["sub"][:], None, A.subtract))
+        ts(out, b, "sub", None, A.subtract, to=(T[out][:], T[b][:, 15:C:16]))
 
-    eng = ["s"]
+    def spick(name, win, off, a=0, b=20, bias=0.0):
+        op("s", [win, off], [name], lambda: S.activation(T[name][:], pick(win, lst(off, a, b)), AF.Copy, bias=bias))
 
-    def copy(rd, wr, out, in_):
-        if eng[0] == "s":
-            op("s", rd, wr, lambda: S.activation(out, in_, AF.Copy))
-        else:
-            op("v", rd, wr, lambda: V.tensor_copy(out, in_))
+    def places():
+        for n in (0, 1):
+            ts("enc", "hlt", 2.0, float(n), A.mult, A.add, to=(T.enc[:, 20 * n:20 * n + 20], T.hlt[:, 20 * n:20 * n + 20]), wr=["enc%d" % n])
 
-    def spick(name, win, off, a=0, b=20, n=C, pairs=False):
-        out = T[name][:, 1:32 * (b - a):2] if pairs else T[name][:]
-        copy([win, off], [name], out, pick(win, lst(off, a, b), 0, n))
+    def heads(r, a=0, b=20):
+        return ("hvs", 20 * (r - 1) + a, 20 * (r - 1) + b) if r < 3 else ("hvs2", a, b)
 
-    def places(i):
-        if i == 0:
-            ts("hb", "hlt", 1, None, A.bitwise_and)
-            ts("hv", "hlt", 1, None, A.arith_shift_right)
-            ts("hb2", "hb", HC, None, A.mult)
-            tt("enci", "hb2", "hv", A.add)
-            op("v", ["enci"], ["enc"], lambda: V.tensor_copy(T.enc[:], T.enci[:]))
-        if i == 3:
-            ts("hb", "hlt", 1, None, A.bitwise_and)
-            ts("hv", "hlt", 1, None, A.arith_shift_right)
-            ts("hb2", "hb", HC, None, A.mult)
-            places(1)
-            tt("enci", "hb2", "hv", A.add)
-            tt("spi", "hv", "hb2", A.subtract)
-            op("v", ["enci"], ["enc"], lambda: V.tensor_copy(T.enc[:], T.enci[:]))
-            ts("sp", "spi", float(HC), None, A.add)
-        if i == 1:
-            ts("hvs", "hv", 2.0, 1.0, A.mult, A.add)
-        if i == 2:
-            tt("spi", "hv", "hb2", A.subtract)
-            ts("sp", "spi", float(HC), None, A.add)
+    def edges(r, out, high):
+        a = 16 * ((r + out + high) % 2)
+        return ("hi%d" if high else "lo%d") % r, a, a + 10
 
-    def units():
-        op("g", ["hold0"], ["hold1"], lambda: g.affine_select(T.hold[:, C:2 * C], T.hold[:, 0:C], [[1, C]], A.is_ge, 0.0, 0, 0))
-        op("g", [], ["one"], lambda: g.iota(T.one[:], [[0, 516]], 1, 0, allow_small_or_imprecise_dtypes=True))
-        op("g", ["one"], ["et"], lambda: g.affine_select(T.et[:], T.one[:], [[-1, 516]], A.is_equal, 0.0, 3, 4))
+    def turn(out, row, n, view, shifted):
+        op("v", row, [out + "0"], lambda: V.transpose(T[out][:, 0:n], view))
+        op("v", row, [out + "1"], lambda: V.transpose(T[out][:, n:2 * n + 32], shifted))
 
-    def scatter(n):
-        op("v", ["enc", "cio"], ["pr%d" % n], lambda: V.tensor_copy(T["pr%d" % n][:].indirect(lst("enc", 20 * n, 20 * n + 20)), T.cio[:]))
+    def wrap_edges(r):
+        for i, (w, s) in enumerate((("lo%d" % r, 1.0), ("hi%d" % r, -1.0))):
+            ts(w, "tv", s, float(HC), A.mult, A.add, to=(T[w][:], pick("tv", lst("tov", 2 * i, 2 * i + 2), 0, 2 * HC + 32)), rd=["tv0", "tv1", "tov"])
 
-    def sort2(n):
-        b, a = "scv%d" % (n % 2), 20 * (n % 2)
-        op("v", [b], ["lo%d" % a], lambda: V.tensor_tensor(T.lohi[:, a:a + 10], T[b][:, 15:HC:16], T[b][:, HC + 15:C:16], A.min))
-        op("v", [b], ["hi%d" % a], lambda: V.tensor_tensor(T.lohi[:, a + 10:a + 20], T[b][:, 15:HC:16], T[b][:, HC + 15:C:16], A.max))
-
-    def sorted_list(n):
-        a = 20 * (n % 2)
-        op("v", ["lo%d" % a, "hi%d" % a, "sub"], ["lhu%d" % n], lambda: V.tensor_scalar(T["lhu%d" % n][:], T.lohi[:, a:a + 20], T["sub"][:], None, A.subtract))
-
-    def heads(n, a=0, b=20):
-        return ("hvs", 20 * n + a, 20 * n + b) if n < 2 else ("hvs2", a, b)
-
-    def role_pick(n):
-        if n < 2:
-            spick("ajr", "pr%d" % n, "sp", 20 * n, 20 * n + 20)
-        else:
-            spick("ajr", "row", *heads(n))
-
-    def both(name, in0, t0, in1, t1, o):
-        a = 48 * (name == "k1")
-        for k in (0, 1):
-            if k == 1 and OPT.get("dup") == "s":
-                op("s", [name + "0"], [name + "1"], lambda: S.activation(T.kk[:, a + K1:a + K1 + 20], T.kk[:, a:a + 20], AF.Copy))
-            else:
-                op("v", [t0, t1], ["%s%d" % (name, k)], lambda: V.tensor_tensor(T.kk[:, a + K1 * k:a + K1 * k + 20], in0, in1, o))
+    def small(out, view, in0, in1, o, rd):
+        op("v", rd, [out], lambda: V.tensor_tensor(view, in0, in1, o))
 
     def runs(c):
         return (0, 2) if c == 2 else (c, 1)
@@ -290,10 +251,10 @@ def rank_program(g, core, T, topo):
     def span(c):
         return ((0, cut[0]), (cut[0], C), (0, C))[c]
 
-    def recut(n):
-        cut[0] = n
+    def recut():
+        cut[0] = C - 128
 
-    cut = [HC]
+    cut = [CUT]
 
     def each(name, c):
         a, n = runs(c)
@@ -324,11 +285,10 @@ def rank_program(g, core, T, topo):
         neng = len(topo.engines(core, peer))
         xo, xn = "xi%d" % ((r - 1) % 2), "xi%d" % (r % 2)
         to, tn = "x%d.%%d%%d" % (r - 1), "x%d.%%d%%d" % r
-        ai, ao, hvs = "lhu%d" % (r - 1), "lhu%d" % r, heads(r - 1)[0]
-        mw, mp, fw, fp, qh, sh, lc, ls = ["%s%d" % (w, r) for w in ("mw", "mp", "fw", "fp", "qh", "sh", "lc", "ls")]
-        m1 = lst(mw, K1, K1 + 20)
-        lo_out, hi_out = T.kjs[:, 15:C:16], T.kjs[:, C + 15:2 * C:16]
-        wrote[mp] = {"a%df" % r: neng}
+        hvs = heads(r)[0]
+        m0, m1, fw, fp, qh, sh, lc, ls = ["%s%d" % (w, r) for w in ("ma", "mb", "fw", "fp", "qh", "sh", "lc", "ls")]
+        kd, k1 = T.kk[:, 0:2 * NQ:2], T.kk[:, 1:2 * NQ:2]
+        wrote[fp] = {"a%df" % r: neng}
         cnt["a%df" % r] = neng
         for c in (0, 1):
             wrote["ld%d" % c] = {"a%dc%d" % (r, c): 2 * neng}
@@ -338,44 +298,69 @@ def rank_program(g, core, T, topo):
             op("g", [to % (c, b) for c in (0, 1)], ["xp%d" % b], lambda: g.affine_select(
                 T.xp[:, C * b:C * b + C], T[xo][:, b:1280:4], [[1, C]], A.is_ge, 0.0, 0, 0))
 
-        def lower(i, w):
-            copy(["sk0", "sk1", w], ["ga%d" % i], T.ga[:, HC * i:HC * i + HC], pick("sk", lst(w, 0, 10)))
+        def lower(i):
+            w = edges(r, i, 0)
+            op("s", ["sk0", "sk1", w[0]], ["ga%d" % i], lambda: S.activation(T.ga[:, HC * i:HC * i + HC], pick("sk", lst(*w)), AF.Copy))
 
-        def higher(i, w):
-            op("v", ["sk0", "sk1", w, "ga%d" % i], ["bit%d" % i], lambda: V.tensor_tensor(
-                T.bit[:, i:C:2], pick("sk", lst(w, 10, 20)), T.ga[:, HC * i:HC * i + HC], A.is_gt))
+        def higher(i):
+            w = edges(r, i, 1)
+            op("v", ["sk0", "sk1", w[0], "ga%d" % i], ["bit%d" % i], lambda: V.tensor_tensor(
+                T.bit[:, i:C:2], pick("sk", lst(*w)), T.ga[:, HC * i:HC * i + HC], A.is_gt))
 
         def straight(q, c):
-            a, e = span(c)
-            out, in_ = T.nx[:, 16 + a:16 + e], pick("sum", lst(*heads(r - 1, a // 16, e // 16)))
+            a, e = HC * c, HC * c + HC
+            out, in_ = T.nx[:, 16 + a:16 + e], pick("ro", lst(*heads(r, a // 16, e // 16)), PAD, 2 * C)
             if q == "s":
-                op("s", ["sum", hvs], each("nx%d", c), lambda: S.activation(out, in_, AF.Square, bias=-1.0))
+                op("s", ["ro", hvs, "low", "nlow"], each("nx%d", c), lambda: S.activation(out, in_, AF.Square, bias=T.nlow[:], scale=T.low[:]))
             else:
-                op("v", ["sum", hvs], each("nx%d", c), lambda: V.tensor_scalar(out, in_, 1.0, None, A.not_equal))
+                op("v", ["ro", hvs, "low"], each("nx%d", c), lambda: V.tensor_scalar(out, in_, 1.0, T.low[:], A.not_equal, A.mult))
 
-        def turn():
-            op("v", ["nx0", "nx1"], ["tt0"], lambda: V.transpose(T.tt[:, 0:C], T.nx[:, 16:16 + C]))
-            op("v", ["nx0", "nx1"], ["tt1"], lambda: V.transpose(T.tt[:, C:2 * C + 32], T.nx[:]))
+        def new_out():
+            for h in (0, 1):
+                w = edges(r, 0, h)
+                op("s", ["fi", w[0]], ["pr%d%d" % ((r - 1) % 2, h)], lambda: S.activation(
+                    T.pr[:, (r - 1) % 2 + 2 * h:2 * C:4], pick("fi", lst(*w)), AF.Copy))
 
-        def cand_pick(h, n):
-            copy(["row", heads(n - 1)[0]], ["kjr%d" % h], T.kjr[:, C * h:C * h + C], pick("row", lst(*heads(n - 1)), C * h))
+        def at_heads(n):
+            w = heads(n)
+            op("s", ["ro", w[0]], ["nc"], lambda: S.activation(T.nx[:, C + 32:2 * C + 32], pick("ro", lst(*w), PAD, 2 * C), AF.Copy))
 
-        def cand_scan(h):
-            a, n = runs(h)
-            op("v", each("kjr%d", h) + each("hold%d", h), each("kjs%d", h), lambda: V.tensor_tensor_scan(
-                T.kjs[:, C * a:C * (a + n)], T.hold[:, C * a:C * (a + n)], T.kjr[:, C * a:C * (a + n)], 0.0, A.add, A.max))
+        def cand(n, i):
+            a = ((0, 1, 3) if n % 2 else (3, 2, 0))[i]
+            return T.tc[:, a:a + 16 * NQ:16]
 
         def yadd(b):
-            op("v", ["xp%d" % b, to % (0, b), to % (1, b), mw], ["y%d" % b], lambda: V.tensor_tensor(
-                T.y32[:, C * b:C * b + C], pick("xp", m1, C * b), T[xo][:, b:1280:4], A.add))
+            op("v", ["xp%d" % b, to % (0, b), to % (1, b), m1], ["y%d" % b], lambda: V.tensor_tensor(
+                T.y32[:, C * b:C * b + C], pick("xp", lst(m1), C * b), T[xo][:, b:1280:4], A.add))
 
         def zpick(q, c, b):
             a, e = span(c)
-            out, in_ = T.zt[:, 4 * a + b:4 * e:4], pick("y32", lst(mw, a // 16, e // 16), C * b)
+            out, in_ = T.zt[:, 4 * a + b:4 * e:4], pick("y32", lst(m0, a // 16, e // 16), C * b)
             if q == "s":
-                op("s", ["y%d" % b, mw], each("z%%d%d" % b, c), lambda: S.activation(out, in_, AF.Copy, scale=0.5))
+                op("s", ["y%d" % b, m0], each("z%%d%d" % b, c), lambda: S.activation(out, in_, AF.Copy, scale=0.5))
             else:
-                op("v", ["y%d" % b, mw], each("z%%d%d" % b, c), lambda: V.tensor_scalar(out, in_, 0.5, None, A.mult))
+                op("v", ["y%d" % b, m0], each("z%%d%d" % b, c), lambda: V.tensor_scalar(out, in_, 0.5, None, A.mult))
+
+        def halves(q, name, c, m):
+            a, e = span(c)
+            out, in_ = T[name][:, a:e], pick("xp", lst(m, a // 16, e // 16), 3 * C)
+            if q == "s":
+                op("s", ["xp3", m], each(name + "%d", c), lambda: S.activation(out, in_, AF.Copy, scale=0.5))
+            else:
+                op("v", ["xp3", m], each(name + "%d", c), lambda: V.tensor_scalar(out, in_, 0.5, None, A.mult))
+
+        def zadd(c):
+            a, e = span(c)
+            op("v", ["x1h0", "x1h1", "x0h%d" % c, m0], ["z%d3" % c], lambda: V.tensor_tensor(
+                T.zt[:, 4 * a + 3:4 * e:4], pick("x1h", lst(m0, a // 16, e // 16)), T.x0h[:, a:e], A.add))
+
+        def choose(k):
+            op("v", ["tt0", "tt1", "kd", "k1"], ["ms%d" % k], lambda: V.tensor_tensor_scan(
+                T.ms[:, 112 * k:112 * k + NP], T.tt[:, k:k + 8 * NP:8], T.kk[:, 1:1 + NP], T.kk[:, 0:1], A.mult, A.add))
+
+        def chosen(k):
+            m = (m0, m1)[k]
+            ts(m, "ms", float(HC), None, A.add, to=(lst(m, 0, 32), pick("ms", T.tom[:], 112 * k, 112)), rd=["ms%d" % k, "tom"])
 
         def layer(c):
             quantise("qz", "sz", "zt", c, [t for b in range(4) for t in each("z%%d%d" % b, c)])
@@ -393,20 +378,21 @@ def rank_program(g, core, T, topo):
             send(T[lc][:, a:e].bitcast(dt.uint8), T[qh][:, a:e].bitcast(dt.uint8), "a%dc%d" % (r, c))
             send(T[ls][:, a:e], T[sh][:, a:e], "a%dc%d" % (r, c))
 
-        def send_m():
-            ts(mw, "mf", "sub", None, A.subtract)
-            if str(r) not in OPT.get("fsend", ""):
-                order("g", [mw], [])
-                send(T[mp][:], T[mw][:], "a%df" % r)
-
         def send_f():
             wrapped(fw, "scf")
             order("g", [fw], [])
             send(T[fp][:], T[fw][:], "a%df" % r)
-            wrote[fp] = wrote[mp]
 
-        def unpack(c):
-            for b in range(4):
+        def send_m():
+            order("g", [m0, m1], [])
+            send(T["mp%d" % r][:], T["mw%d" % r][:, 0:52], "a%df" % r)
+            wrote["mp%d" % r] = wrote[fp]
+
+        def behind(name, row, k):
+            spick(name, row, "mp%d" % r, 32 * k, 32 * k + 20)
+
+        def unpack(c, *planes):
+            for b in planes or range(4):
                 product(4 * (c % 2) + b, ("qe", "se"), b, (lc, ls), c, each("ld%d", c) + ["qe%d" % b])
 
         def meet(c, b):
@@ -416,98 +402,93 @@ def rank_program(g, core, T, topo):
                [tn % (k + i, b) for i in range(n)] + ["%s.%d%d" % (xn, k + i, b) for i in range(n)],
                lambda: V.tensor_tensor(T[xn][:, cols], pick("dd", lst("lw", a // 16, e // 16), C * b), T[xo][:, cols], A.add))
 
-        def tails():
-            spick("raw0", "raw2", mp, K1, K1 + 20)
-            spick("tpr", "raw0", mp)
-            dma("y", "ot", T.tp[:], T.tpr[0:128:16, :], rd=["tpr"])
-
         def ones(b):
             op("v", ["et"], ["qe%d" % b], lambda: V.quantize_mx(
                 T.qe[:, 128 * b:128 * b + 128], T.se[:, 128 * b:128 * b + 128], T.et[:, 3 - b:515 - b]))
 
         def store_scales():
             for k in range(4):
-                dma("y", "oq", T.osc[4 * k:4 * k + 4, :], T.so[32 * k:32 * k + 4, :], rd=["qo.0", "qo.1"], total=OPT["oq"])
+                dma("y", "oq", T.osc[4 * k:4 * k + 4, :], T.so[32 * k:32 * k + 4, :], rd=["qo.0", "qo.1"], total=96)
 
         def store_codes(c):
             a, e = span(c)
-            dma("y", "oq", T.oc[:, 4 * a:4 * e], T.qo[:, a:e].bitcast(dt.uint8), rd=each("qo.%d", c), total=OPT["oq"])
+            dma("y", "oq", T.oc[:, 4 * a:4 * e], T.qo[:, a:e].bitcast(dt.uint8), rd=each("qo.%d", c), total=96)
 
+        four = ["pr00", "pr01", "pr10", "pr11"]
+        nxt = [r]
         steps = {
-            "cut": lambda: recut(192), "encf": lambda: places(3), "g2s": lambda: affine("g2", "rr", 2.0, -1.0), "enc": lambda: places(0), "heads": lambda: places(1), "sib": lambda: places(2), "et": units, "turn": turn,
-            "mw": send_m, "tp": tails, "os": store_scales,
-            "gm": lambda: op("v", ["tt0", "tt1", "tof", "kd0", "kd1"], ["mt"], lambda: V.tensor_tensor(
-                T.mt[:], pick("tt", lst("tof", 0, 3), 0, 2 * C + 32), T.kk[:, 0:48], A.mult)),
-            "ad": lambda: op("v", ["mt", "k10", "k11"], ["mf"], lambda: V.tensor_tensor(T.mf[:], T.mt[:], T.kk[:, 48:96], A.add)),
-            "m1p": lambda: spick("m1p", "cio", mp, K1, K1 + 20), "fpr": lambda: spick("fpr", "m1p", mp),
-            "lm": lambda: [spick("m1p", "fr", mp, K1, K1 + 20), spick("lr", "m1p", mp)],
-            "FS": lambda: scan("scf", "fr"), "F": send_f,
-            "TP": lambda: [spick("tpr", "raw2", fp), dma("y", "ot", T.tp[:], T.tpr[0:128:16, :], rd=["tpr"])],
-            "fs": lambda: scan("scf", "fpr"), "f": lambda: wrapped(fp, "scf"),
+            "enc": places, "hv": lambda: ts("hv", "hlt", 1, None, A.arith_shift_right),
+            "heads": lambda: ts("hvs", "hv", 4.0, 3.0, A.mult, A.add),
+            "cut": recut, "os": store_scales, **later,
+            "scat": lambda: op("v", ["enc0", "enc1", "pay0", "pay1"], four, lambda: V.tensor_copy(T.pr[:].indirect(T.enc[:]), T.pay[:])),
+            "fi": lambda: op("v", [fp, "pay0", "pay1"], ["fi"], lambda: V.tensor_copy(T.fi[:].indirect(lst(fp)), T.pay[:, C * (r - 1):C * r])),
+            "pr": new_out,
+            "mn": lambda: op("v", four + ["rst"], ["ro"], lambda: V.tensor_tensor_scan(T.ro[:, PAD:PAD + 2 * C], T.rst[:], T.pr[:], 0.0, A.max, A.min)),
+            "ta": lambda: turn("tv", ["ro"], HC, T.ro[:, PAD + 3:PAD + 2 * C:4], T.ro[:, 3:2 * C + 2 * PAD:4]),
+            "wrap": lambda: wrap_edges(nxt[0]), "cp": lambda: at_heads(nxt[0]),
+            "tc": lambda: turn("tc", ["nc"], C, T.nx[:, C + 32:2 * C + 32], T.nx[:, C + 16:2 * C + 48]),
+            "rho": lambda: small("rho", T.rho[:], cand(nxt[0], 2), T.ciw[:, 0:NQ], A.not_equal, ["tc0", "tc1", "ciw"]),
+            "nd": lambda: small("nd", T.nd[:], cand(nxt[0], 0), cand(nxt[0], 1), A.add, ["tc0", "tc1"]),
+            "g2": lambda: affine("g2", "rho", -2.0, 1.0), "g2v": lambda: ts("g2", "rho", -2.0, 1.0, A.mult, A.add),
+            "kq": lambda: small("kq", T.kq[:], T.rho[:], T.nd[:], A.mult, ["rho", "nd"]),
+            "k1": lambda: small("k1", k1, T.kq[:], cand(nxt[0], 1), A.subtract, ["kq", "tc0", "tc1"]),
+            "kd": lambda: small("kd", kd, T.g2[:], T.nd[:], A.mult, ["g2", "nd"]),
             "qu": lambda: op("v", ["ut"], ["qu"], lambda: V.quantize_mx(T.qu[:], T.su[:], T.ut[:])),
             "qv": lambda: op("v", ["vt"], ["qv"], lambda: V.quantize_mx(T.qv[:], T.sv[:], T.vt[:])),
             "mm": lambda: [product(c, ("qu", "su"), 0, ("qx", "sx"), c, ["qx.%d" % c, "qu"]) for c in (0, 1)],
-            "mm2": lambda: product(0, ("qu", "su"), 0, ("qx", "sx"), 2, ["qx.0", "qx.1", "qu"]),
             "pg": lambda: [plane(b) for b in range(4)],
-            "li": lambda: lower(0, ai), "lo": lambda: lower(1, ao), "hi": lambda: higher(0, ai), "ho": lambda: higher(1, ao),
-            "sum": lambda: op("v", ["bit0", "bit1", "alt"], ["sum"], lambda: V.tensor_tensor_scan(T["sum"][:], T.alt[:], T.bit[:], 0.0, A.mult, A.add)),
-            "nx": lambda: straight(eng[0], 2), "nxs": lambda: straight("s", 0), "nxv": lambda: straight("v", 1),
-            "rs": lambda: scan("scr", "ajr"),
-            "rr": lambda: op("v", ["scr", "ciw"], ["rr"], lambda: V.tensor_tensor(T.rr[:], T.scr[:, 15:C:16], T.ciw[:], A.is_lt)),
-            "g2": lambda: ts("g2", "rr", 2.0, -1.0, A.mult, A.add),
-            "dd": lambda: op("v", ["kjs0", "kjs1"], ["ddc"], lambda: V.tensor_tensor(T.ddc[:], hi_out, lo_out, A.subtract)),
-            "kq": lambda: tt("kq", "ddc", "rr", A.mult),
-            "kd": lambda: both("kd", T.ddc[:], "ddc", T.g2[:], "g2", A.mult),
-            "k1": lambda: both("k1", hi_out, "kjs1", T.kq[:], "kq", A.subtract),
-            "m1r": lambda: spick("m1r", "cio", mw, K1, K1 + 20), "fr": lambda: spick("fr", "m1r", mw),
+            "li": lambda: lower(0), "lo": lambda: lower(1), "hi": lambda: higher(0), "ho": lambda: higher(1),
+            "sum": lambda: op("v", ["bit0", "bit1", "alt"], ["ro"], lambda: V.tensor_tensor_scan(
+                T.ro[:, PAD + 1:PAD + 2 * C:2], T.alt[:], T.bit[:], 0.0, A.mult, A.add)),
+            "nxs": lambda: straight("s", 0), "nxv": lambda: straight("v", 1),
+            "turn": lambda: turn("tt", ["nx0", "nx1"], C, T.nx[:, 16:16 + C], T.nx[:, 0:C + 32]),
+            "g0": lambda: choose(0), "g1": lambda: choose(1), "m0": lambda: chosen(0), "m1": lambda: chosen(1),
+            "m1r": lambda: spick("m1r", "cio", m1), "fr": lambda: spick("fr", "m1r", m0),
+            "FS": lambda: scan("scf", "fr"), "F": send_f,
+            "m1v": lambda: op("v", ["cio", m1], ["m1r"], lambda: V.tensor_copy(T.m1r[:], pick("cio", lst(m1)))),
+            "frv": lambda: op("v", ["m1r", m0], ["fr"], lambda: V.tensor_copy(T.fr[:], pick("m1r", lst(m0)))),
+            "x1": lambda: halves("s", "x1h", 2, m1), "Z0": lambda: zadd(0), "Z1": lambda: zadd(1),
+            "M": send_m, "lm1": lambda: behind("m1r", "fr", 1), "lm0": lambda: behind("lr", "m1r", 0),
+            "tm1": lambda: behind("raw0", "raw2", 1),
+            "tm0": lambda: [behind("tpr", "raw0", 0), dma("y", "ot", T.tp[:], T.tpr[0:128:16, :], rd=["tpr"])],
             "lr": lambda: spick("lr", "fr", fp), "ls": lambda: scan("scl", "lr"), "lw": lambda: wrapped("lw", "scl"),
-            "fi": lambda: op("v", [fp, "cio"], ["fi"], lambda: V.tensor_copy(T.fi[:, 0:C].indirect(lst(fp)), T.cio[:])),
-            "hvr": lambda: spick("hvr", "cio", "hvs"), "tr": lambda: spick("tr", "hvr", "fp1"),
-            "hs": lambda: scan("sch", "tr"), "hw": lambda: wrapped("hvs2", "sch"),
             "hu": lambda: op("v", ["hlt"], ["hu"], lambda: V.tensor_copy(T.hu[:], T.hlt[:, 0:20])),
-            "raw": lambda: [spick("raw0", "cio", "hu"), spick("raw2", "raw0", "fp1")],
-            "ks": lambda: cand_scan(2), "l2": lambda: layer(2), "u2": lambda: unpack(2),
-            "q": lambda: quantise("qx", "sx", xo, 2, [to % (c, b) for c in (0, 1) for b in range(4)]),
+            "hvr": lambda: spick("hvr", "half", "hu"), "tr": lambda: spick("tr", "hvr", "fp1"),
+            "hs": lambda: scan("sch", "tr"),
+            "hw": lambda: ts("hvs2", "sch", "sub4", 4.0, A.subtract, A.mult, to=(T.hvs2[:], T.sch[:, 15:C:16])),
+            "raw": lambda: [spick("raw0", "cio", "hu", bias=float(HC)), spick("raw2", "raw0", "fp1")],
+            "TP": lambda: [spick("tpr", "raw2", fp), dma("y", "ot", T.tp[:], T.tpr[0:128:16, :], rd=["tpr"])],
         }
         for n in range(4):
-            steps.update({
-                "scat%d" % n: lambda n=n: scatter(n), "rp%d" % n: lambda n=n: role_pick(n),
-                "vs%d" % n: lambda n=n: scan("scv%d" % (n % 2), "pr%d" % (n % 2)),
-                "vm%d" % n: lambda n=n: sort2(n), "vc%d" % n: lambda n=n: sorted_list(n),
-                "row%d" % n: lambda n=n: spick("row", "cio", "lhu%d" % n, pairs=True),
-                "pr%d" % n: lambda n=n: spick("pr%d" % (n % 2), "fi", "lhu%d" % (n - 2)),
-                "qe%d" % n: lambda n=n: ones(n), "y%d" % n: lambda n=n: yadd(n), "a%d" % n: lambda n=n: meet(2, n),
-            })
+            steps.update({"qe%d" % n: lambda n=n: ones(n), "y%d" % n: lambda n=n: yadd(n), "a%d" % n: lambda n=n: meet(2, n)})
         for c in (0, 1):
             steps.update({
                 "q%d" % c: lambda c=c: quantise("qx", "sx", xo, c, [to % (c, b) for b in range(4)]),
                 "o%d" % c: lambda c=c: quantise("qo", "so", xn, c, [tn % (c, b) for b in range(4)]),
-                "ks%d" % c: lambda c=c: cand_scan(c), "l%d" % c: lambda c=c: layer(c), "send%d" % c: lambda c=c: send_h(c),
+                "l%d" % c: lambda c=c: layer(c), "send%d" % c: lambda c=c: send_h(c),
                 "u%d" % c: lambda c=c: unpack(c), "oc%d" % c: lambda c=c: store_codes(c),
                 "ym%d" % c: lambda c=c: product(c, ("qv", "sv"), 0, ("qo", "so"), c, ["qo.%d" % c, "qv"]),
                 "oy%d" % c: lambda c=c: dma("s", "oy", T.y[:, slice(*span(c))], T.yo[:, slice(*span(c))], rd=["yo%d" % c], total=32),
             })
             for b in range(4):
                 steps["a%d%d" % (c, b)] = lambda c=c, b=b: meet(c, b)
+                steps["u%d%d" % (c, b)] = lambda c=c, b=b: unpack(c, b)
         for part in "abc":
-            for c in (0, 1):
-                steps["kp%d" % c] = lambda c=c: cand_pick(c, r + (part == "c"))
+            nxt[0] = r + (part == "c")
             for c in (0, 1, 2):
                 a, e = span(c)
                 for q in "sv":
+                    steps["p%s%d" % (q, c)] = lambda q=q, c=c: halves(q, "x0h", c, m0)
                     res = "yo" if part == "c" else "sk"
                     steps["e%s%d" % (q, c)] = lambda q=q, c=c, res=res: evac(
                         q, T[res][:, slice(*span(c))], c % 2, each(res + "%d", c), span(c)[1] - span(c)[0])
                     for b in range(4):
-                        steps["u%d%d" % (c, b)] = lambda c=c, b=b: product(
-                            4 * (c % 2) + b, ("qe", "se"), b, (lc, ls), c, each("ld%d", c) + ["qe%d" % b])
                         steps["z%s%d%d" % (q, c, b)] = lambda q=q, c=c, b=b: zpick(q, c, b)
                         steps["h%s%d%d" % (q, c, b)] = lambda q=q, c=c, a=a, e=e, b=b: evac(
                             q, T.ht[:, 4 * a + b:4 * e:4], 4 * (c % 2) + b, each("h%%d%d" % b, c), e - a, 0.03125)
                         steps["d%s%d%d" % (q, c, b)] = lambda q=q, c=c, a=a, e=e, b=b: evac(
                             q, T.dd[:, C * b + a:C * b + e], 4 * (c % 2) + b, each("d%%d%d" % b, c), e - a)
-            for w in OPT["%s%d" % (part, r)].split():
-                eng[0] = "v" if w.endswith("!") else "s"
-                steps[w.rstrip("!")]()
+            for w in ORDER["%s%d" % (part, r)].split():
+                steps[w]()
     for sem in sorted(cnt):
         need("g", sem, cnt[sem])

from concourse.mybir import dt, AluOpType, ActivationFunctionType

A = AluOpType
AF = ActivationFunctionType
C = 320
HC = 160
CUT = 160
STEP = [1, 2, 4]
CODE = "float8_e4m3fn_x4"
NP, NQ = 81, 41
PAD = 64

SCORES = "pg q0 q1 mm es0 ta wrap ev1 li tc nd hi lo rho ho g2 kq sum k1 nxs nxv kd turn"
LISTS = "g1 g0 m1 m0"
MEET = "a0 a1 a2 a03 a13"
ORDER = {
    "a1": "enc oneg hv own sub altg low sg scat pg qu half q0 et q1 mn mk mm heads cp ta es0 ev1 wrap tc li rho lo nd hi kq ho g2 k1 sum "
          "nxs kd nxv turn hold " + LISTS,
    "b1": "m1r fr y0 y1 y2 y3 zs20 zs21 zs22 FS zv03 F l0 qe0 zs13 hs00 l1 qe3 hs02 qe1 hv01 hv03 send0 hs10 qe2 hv11 hs12 hv13 send1",
    "c1": "sub4 u0 u1 fi lr pr ls lw hu dv01 ds00 dv02 ds03 mn ds11 ds12 ds13 dv10 cp hvr " + MEET,
    "a2": SCORES + " tr " + LISTS,
    "b2": "x1 ps0 y0 zs00 ps1 y1 zs01 y2 Z0 m1v zs02 l0 Z1 zv12 zs10 zs11 l1 fr hs00 hs01 hs02 FS hs10 hv03 F send0 lr hv11 hv12 hv13 send1",
    "c2": "u0 u1 fi hs ls pr hw lw ds00 mn ds02 dv10 ds03 ds11 ds12 ds13 dv01 cp " + MEET,
    "a3": SCORES + " " + LISTS,
    "b3": "y0 x1 ps0 y1 zs00 ps1 y2 zs01 M zs02 zs10 Z0 Z1 l0 zv12 zs11 m1r l1 hv00 hs01 hv02 fr hs10 hv03 send0 hv11 hs12 hv13 send1",
    "c3": "lm1 lm0 ls raw qv lw u0 u1 dv00 ds01 dv02 ds03 dv10 ds11 ds12 ds13 tm1 tm0 " + MEET + " o0 oc0 ym0 o1 ym1 es0 oc1 os ev1 oy0 oy1",
}

SCRATCH = {
    "pmi": ("sbuf", [128, 8], "int32"), "pma": ("sbuf", [128, 8], "int32"), "thr": ("sbuf", [128, 5], "float32"),
    "cio": ("sbuf", [128, 320], "float32"), "j16": ("sbuf", [128, 320], "bfloat16"), "mk": ("sbuf", [128, 320], "float32"),
    "sg": ("sbuf", [128, 320], "bfloat16"), "hold": ("sbuf", [128, 320], "float32"), "alt": ("sbuf", [128, 320], "bfloat16"),
    "pay": ("sbuf", [128, 640], "bfloat16"), "rst": ("sbuf", [128, 640], "bfloat16"), "half": ("sbuf", [128, 320], "float32"),
    "c16": ("sbuf", [128, 42], "float32"), "ciw": ("sbuf", [128, 42], "float32"),
    "tfi": ("sbuf", [128, 6], "float32"), "tov": ("sbuf", [128, 4], "uint16"),
    "one": ("sbuf", [128, 516], "bfloat16"), "et": ("sbuf", [128, 516], "bfloat16"),
    "qe": ("sbuf", [128, 512], CODE), "se": ("sbuf", [128, 512], "uint8"),
    "ut": ("sbuf", [128, 512], "bfloat16"), "vt": ("sbuf", [128, 512], "bfloat16"),
    "qu": ("sbuf", [128, 128], CODE), "su": ("sbuf", [128, 128], "uint8"),
    "qv": ("sbuf", [128, 128], CODE), "sv": ("sbuf", [128, 128], "uint8"),
    "qw": ("sbuf", [128, 512], CODE), "sw": ("sbuf", [128, 512], "uint8"),
    "hlt": ("sbuf", [128, 40], "int32"), "hv": ("sbuf", [128, 40], "int32"),
    "enc": ("sbuf", [128, 40], "uint16"), "hu": ("sbuf", [128, 20], "uint16"),
    "xp": ("sbuf", [128, 1280], "bfloat16"), "y32": ("sbuf", [128, 1280], "float32"), "zt": ("sbuf", [128, 1280], "bfloat16"),
    "ht": ("sbuf", [128, 1280], "bfloat16"), "dd": ("sbuf", [128, 1280], "bfloat16"),
    "qz": ("sbuf", [128, 320], CODE), "sz": ("sbuf", [128, 320], "uint8"),
    "qx": ("sbuf", [128, 320], CODE), "sx": ("sbuf", [128, 320], "uint8"),
    "qo": ("sbuf", [128, 320], CODE), "so": ("sbuf", [128, 320], "uint8"),
    "yo": ("sbuf", [128, 320], "float32"), "tpr": ("sbuf", [128, 320], "float32"),
    "ps": ("psum", [128, 4096], "float32"),
    "sk": ("sbuf", [128, 320], "float32"), "ga": ("sbuf", [128, 320], "float32"), "bit": ("sbuf", [128, 320], "bfloat16"),
    "pr": ("sbuf", [128, 640], "bfloat16"), "ro": ("sbuf", [128, 640 + 2 * PAD], "bfloat16"),
    "nx": ("sbuf", [128, 688], "bfloat16"), "tt": ("sbuf", [128, 672], "bfloat16"), "tv": ("sbuf", [128, 352], "bfloat16"),
    "tc": ("sbuf", [128, 672], "bfloat16"), "kk": ("sbuf", [128, 82], "float32"),
    "hvs": ("sbuf", [128, 40], "uint16"), "hvs2": ("sbuf", [128, 20], "uint16"),
    "ms": ("sbuf", [128, 224], "float32"), "tom": ("sbuf", [128, 2], "uint16"),
    "fi": ("sbuf", [128, 320], "bfloat16"), "x0h": ("sbuf", [128, 320], "bfloat16"), "x1h": ("sbuf", [128, 320], "bfloat16"),
    "m1r": ("sbuf", [128, 320], "float32"), "fr": ("sbuf", [128, 320], "float32"), "lr": ("sbuf", [128, 320], "float32"),
    "lw": ("sbuf", [128, 20], "uint16"),
    "tr": ("sbuf", [128, 320], "float32"), "hvr": ("sbuf", [128, 320], "float32"),
    "raw0": ("sbuf", [128, 320], "float32"), "raw2": ("sbuf", [128, 320], "float32"),
}
for _n in ("p16", "pmf", "sign", "sub", "sub4", "pe", "pv", "low", "nlow"):
    SCRATCH[_n] = ("sbuf", [128, 1], "float32")
for _n in ("rho", "g2", "nd", "kq"):
    SCRATCH[_n] = ("sbuf", [128, NQ], "float32")
for _n in ("h", "f", "l"):
    SCRATCH["sc" + _n] = ("sbuf", [128, 320], "float32")
for _k in (0, 1):
    SCRATCH["xi%d" % _k] = ("sbuf", [128, 1280], "bfloat16")
for _r in (1, 2, 3):
    SCRATCH["qh%d" % _r] = ("sbuf", [128, 320], CODE)
    SCRATCH["sh%d" % _r] = ("sbuf", [128, 320], "uint8")
    SCRATCH["lc%d" % _r] = ("sbuf", [128, 320], CODE)
    SCRATCH["ls%d" % _r] = ("sbuf", [128, 320], "uint8")
    SCRATCH["mw%d" % _r] = ("sbuf", [128, 64], "uint16")
    SCRATCH["mp%d" % _r] = ("sbuf", [128, 52], "uint16")
    SCRATCH["lo%d" % _r] = ("sbuf", [128, 32], "uint16")
    SCRATCH["hi%d" % _r] = ("sbuf", [128, 32], "uint16")
    SCRATCH["fw%d" % _r] = ("sbuf", [128, 20], "uint16")
    SCRATCH["fp%d" % _r] = ("sbuf", [128, 20], "uint16")

SEMAPHORES = ["qv_", "qs_", "qt_", "qg_", "dx", "dl", "du", "dw", "dv", "lsem", "oq", "oy", "ot"] + \
    ["a%df" % r for r in (1, 2, 3)] + ["a%dc%d" % (r, c) for r in (1, 2, 3) for c in (0, 1)]


def rank_program(g, core, T, topo):
    rank = T.rank_of(core)
    if rank is None:
        return
    Q = {"v": g.vector, "s": g.scalar, "t": g.tensor, "g": g, "y": g.sync}
    SEM = {"v": "qv_", "s": "qs_", "t": "qt_", "g": "qg_"}
    cnt = {}
    known = {q: {} for q in Q}
    snap = {}
    wrote, read = {}, {}

    def need(q, sem, val):
        if known[q].get(sem, 0) >= val:
            return
        Q[q].wait_ge(T.sem[sem], val)
        known[q][sem] = val
        for k, w in snap.get((sem, val), {}).items():
            if known[q].get(k, 0) < w:
                known[q][k] = w

    def order(q, rd, wr):
        deps = {}
        for t in rd:
            for k, w in wrote[t].items():
                deps[k] = max(deps.get(k, 0), w)
        for t in wr:
            for d in (wrote.get(t, {}), read.get(t, {})):
                for k, w in d.items():
                    deps[k] = max(deps.get(k, 0), w)
        for k, w in deps.items():
            need(q, k, w)

    def done(sem, val, rd, wr):
        for t in rd:
            d = read.setdefault(t, {})
            d[sem] = max(d.get(sem, 0), val)
        for t in wr:
            wrote[t] = {sem: val}
            read[t] = {}

    def op(q, rd, wr, f):
        order(q, rd, wr)
        sem = SEM[q]
        f().then_inc(T.sem[sem], 1)
        cnt[sem] = cnt.get(sem, 0) + 1
        snap[(sem, cnt[sem])] = dict(known[q])
        done(sem, cnt[sem], rd, wr)

    def dma(q, sem, out, in_, rd=(), wr=(), total=16):
        order(q, rd, wr)
        Q[q].dma_start(out, in_).then_inc(T.sem[sem], 16)
        cnt[sem] = total
        done(sem, total, rd, wr)

    V, S, P = g.vector, g.scalar, g.tensor

    def bank(k, n):
        return T.ps[:, 512 * k:512 * k + n]

    def lst(name, a=0, b=20):
        if name[:2] in ("ma", "mb"):
            return T["mw" + name[2:]][:, a + 32 * (name[1] == "b"):b + 32 * (name[1] == "b")]
        return T[name][:, a:b]

    def pick(name, off, a=0, n=C):
        return T[name][:, a:a + n].indirect(off)

    def ts(out, in_, s1, s2, *ops, to=None, rd=None, wr=None):
        names = [s for s in (s1, s2) if isinstance(s, str)]
        a, b = [T[s][:] if isinstance(s, str) else s for s in (s1, s2)]
        o, i = to or (T[out][:], T[in_][:])
        op("v", (rd or [in_]) + names, wr or [out], lambda: V.tensor_scalar(o, i, a, b, *ops))

    def affine(out, in_, scale, bias, view=None):
        i = T[in_][:] if view is None else view
        if isinstance(bias, str):
            op("s", [in_, bias], [out], lambda: S.activation(T[out][:], i, AF.Identity, bias=T[bias][:], scale=scale))
        else:
            op("s", [in_], [out], lambda: S.activation(T[out][:], i, AF.Copy, bias=bias, scale=scale))

    def count(name, out, pattern, base=0, by=0):
        op("g", [], [name], lambda: g.iota(out, pattern, base, by, allow_small_or_imprecise_dtypes=True))

    dma("s", "dl", T.hlt[:, 0:20], T.hl[:], wr=["hlt"], total=32)
    dma("y", "dl", T.hlt[:, 20:40], T.tl[:], total=32)
    dma("y", "dx", T.xi0[:], T.x[:], wr=["x0.%d%d" % (c, b) for c in (0, 1) for b in range(4)])
    dma("y", "du", T.ut[:], T.u[:], wr=["ut"])
    dma("y", "dw", T.qw[:].bitcast(dt.uint8), T.wc[:], wr=["qw"], total=32)
    dma("y", "dw", T.sw[:], T.ws[:], total=32)
    dma("y", "dv", T.vt[:], T.v[:], wr=["vt"])

    op("g", [], ["pmi0"], lambda: g.iota(T.pmi[:, 0:3], [[64, 3]], 0, 64))
    op("g", [], ["pmi1"], lambda: g.iota(T.pmi[:, 3:4], [[0, 1]], 0, 136))
    op("g", [], ["pmi2"], lambda: g.iota(T.pmi[:, 4:5], [[0, 1]], 0, 16))
    count("cio", T.cio[:], [[1, C]], -HC)
    count("tfi1", T.tfi[:, 2:6], [[2, 2], [3, 2]])
    count("tfi0", T.tfi[:, 0:2], [[256, 2]])
    count("c16", T.c16[:], [[0, 2], [16, 21]], -HC)
    count("rst", T.rst[:], [[0, HC], [-1024, 4]], 512)
    count("j16", T.j16[:], [[0, 20], [16, 16]])
    op("v", [], ["nx0", "nx1", "nc"], lambda: V.memset(T.nx[:], 0.0))
    ts("pma", "pmi", 240, None, A.bitwise_and, to=(T.pma[:, 0:5], T.pmi[:, 0:5]), rd=["pmi0", "pmi1", "pmi2"])
    op("v", [], ["ro"], lambda: V.memset(T.ro[:, 3:2 * C + 2 * PAD:4], 0.0))
    ts("thr", "pma", 128.0, 512.0, A.is_ge, A.mult, to=(T.thr[:], T.pma[:, 0:5]))
    ts("p16", "pma", 1.0, None, A.mult, to=(T.p16[:], T.pma[:, 4:5]))
    op("v", [], ["ms0", "ms1"], lambda: V.memset(T.ms[:], 0.0))
    ts("sign", "thr", -1.0 / 256, 1.0, A.mult, A.add, to=(T.sign[:], T.thr[:, 1:2]))
    for name, n in (("pe", C), ("pv", HC)):
        ts(name, "thr", (n + 16) / 512, "p16", A.mult, A.add, to=(T[name][:], T.thr[:, 3:4]))
    op("s", ["cio", "sign", "thr"], ["pay1"], lambda: S.activation(T.pay[:, C:2 * C], T.cio[:], AF.Identity, bias=T.thr[:, 0:1], scale=T.sign[:]))
    op("v", ["cio", "sign", "thr"], ["pay0"], lambda: V.tensor_scalar(T.pay[:, 0:C], T.cio[:], T.sign[:], T.thr[:, 2:3], A.mult, A.add))
    ts("tov", "tfi", "pv", 2 * HC + 31.0, A.add, A.min, to=(T.tov[:], T.tfi[:, 2:6]), rd=["tfi1"])
    ts("tom", "tfi", "pe", 1.0 / 8, A.add, A.mult, to=(T.tom[:], T.tfi[:, 0:2]), rd=["tfi0"])

    later = {
        "own": lambda: [affine("pmf", "p16", 1.0 / 16, 0.0), affine("ciw", "c16", 1.0, "pmf")],
        "low": lambda: [affine("low", "thr", -1.0 / 512, 1.0, T.thr[:, 4:5]),
                        affine("nlow", "thr", 1.0 / 512, -1.0, T.thr[:, 4:5])],
        "sub": lambda: affine("sub", "p16", -32.0, 7680.0 - HC), "sub4": lambda: affine("sub4", "p16", -32.0, 7680.0 - 0.75),
        "sg": lambda: op("s", ["j16", "p16"], ["sg"], lambda: S.activation(T.sg[:], T.j16[:], AF.Sign, bias=T.p16[:], scale=-1.0)),
        "mk": lambda: op("s", ["sg"], ["mk"], lambda: S.activation(T.mk[:], T.sg[:], AF.Square, scale=128.0)),
        "hold": lambda: affine("hold", "mk", 1.0, 512.0 - 128.0 ** 2),
        "alt": lambda: affine("alt", "rst", -1.0 / 2048, 0.25, T.rst[:, 0:2 * C:2]),
        "altg": lambda: count("alt", T.alt[:], [[0, HC], [1, 2]]),
        "one": lambda: affine("one", "rst", 0.0, 1.0, T.rst[:, 0:516]),
        "oneg": lambda: count("one", T.one[:], [[0, 516]], 1),
        "half": lambda: count("half", T.half[:], [[1, HC], [0, 2]]),
        "et": lambda: op("g", ["one"], ["et"], lambda: g.affine_select(T.et[:], T.one[:], [[-1, 516]], A.is_equal, 0.0, 3, 4)),
    }

    def scan(b, row):
        op("v", [row, "hold"], [b], lambda: V.tensor_tensor_scan(T[b][:], T.hold[:], T[row][:], 0.0, A.add, A.max))

    def wrapped(out, b):
        ts(out, b, "sub", None, A.subtract, to=(T[out][:], T[b][:, 15:C:16]))

    def spick(name, win, off, a=0, b=20, bias=0.0):
        op("s", [win, off], [name], lambda: S.activation(T[name][:], pick(win, lst(off, a, b)), AF.Copy, bias=bias))

    def places():
        for n in (0, 1):
            ts("enc", "hlt", 2.0, float(n), A.mult, A.add, to=(T.enc[:, 20 * n:20 * n + 20], T.hlt[:, 20 * n:20 * n + 20]), wr=["enc%d" % n])

    def heads(r, a=0, b=20):
        return ("hvs", 20 * (r - 1) + a, 20 * (r - 1) + b) if r < 3 else ("hvs2", a, b)

    def edges(r, out, high):
        a = 16 * ((r + out + high) % 2)
        return ("hi%d" if high else "lo%d") % r, a, a + 10

    def turn(out, row, n, view, shifted):
        op("v", row, [out + "0"], lambda: V.transpose(T[out][:, 0:n], view))
        op("v", row, [out + "1"], lambda: V.transpose(T[out][:, n:2 * n + 32], shifted))

    def wrap_edges(r):
        for i, (w, s) in enumerate((("lo%d" % r, 1.0), ("hi%d" % r, -1.0))):
            ts(w, "tv", s, float(HC), A.mult, A.add, to=(T[w][:], pick("tv", lst("tov", 2 * i, 2 * i + 2), 0, 2 * HC + 32)), rd=["tv0", "tv1", "tov"])

    def small(out, view, in0, in1, o, rd):
        op("v", rd, [out], lambda: V.tensor_tensor(view, in0, in1, o))

    def runs(c):
        return (0, 2) if c == 2 else (c, 1)

    def span(c):
        return ((0, cut[0]), (cut[0], C), (0, C))[c]

    def recut():
        cut[0] = C - 128

    cut = [CUT]

    def each(name, c):
        a, n = runs(c)
        return [name % (a + i) for i in range(n)]

    def evac(q, out, k, toks, n, scale=None):
        toks = ["bk%d" % k] + toks
        if q == "s":
            op("s", [], toks, lambda: S.activation(out, bank(k, n), AF.Copy, scale=scale or 1.0))
        elif scale:
            op("v", [], toks, lambda: V.tensor_scalar(out, bank(k, n), scale, None, A.mult))
        else:
            op("v", [], toks, lambda: V.tensor_copy(out, bank(k, n)))

    def product(k, w, b, x, c, toks):
        a, e = span(c)
        op("t", toks, ["bk%d" % k], lambda: P.matmul_mx(
            bank(k, e - a), T[w[0]][:, 128 * b:128 * b + 128], T[w[1]][:, 128 * b:128 * b + 128], T[x[0]][:, a:e], T[x[1]][:, a:e], True, True))

    def quantise(q, s, tile, c, toks):
        a, e = span(c)
        op("v", toks, each(q + ".%d", c), lambda: V.quantize_mx(T[q][:, a:e], T[s][:, a:e], T[tile][:, 4 * a:4 * e]))

    for r in (1, 2, 3):
        peer = T.cores[rank ^ STEP[r - 1]]
        rid, pid = topo.addr(peer)[0], topo.addr(peer)[1]
        mask = topo.mask(core, peer)
        neng = len(topo.engines(core, peer))
        xo, xn = "xi%d" % ((r - 1) % 2), "xi%d" % (r % 2)
        to, tn = "x%d.%%d%%d" % (r - 1), "x%d.%%d%%d" % r
        hvs = heads(r)[0]
        m0, m1, fw, fp, qh, sh, lc, ls = ["%s%d" % (w, r) for w in ("ma", "mb", "fw", "fp", "qh", "sh", "lc", "ls")]
        kd, k1 = T.kk[:, 0:2 * NQ:2], T.kk[:, 1:2 * NQ:2]
        wrote[fp] = {"a%df" % r: neng}
        cnt["a%df" % r] = neng
        for c in (0, 1):
            wrote["ld%d" % c] = {"a%dc%d" % (r, c): 2 * neng}
            cnt["a%dc%d" % (r, c)] = 2 * neng

        def plane(b):
            op("g", [to % (c, b) for c in (0, 1)], ["xp%d" % b], lambda: g.affine_select(
                T.xp[:, C * b:C * b + C], T[xo][:, b:1280:4], [[1, C]], A.is_ge, 0.0, 0, 0))

        def lower(i):
            w = edges(r, i, 0)
            op("s", ["sk0", "sk1", w[0]], ["ga%d" % i], lambda: S.activation(T.ga[:, HC * i:HC * i + HC], pick("sk", lst(*w)), AF.Copy))

        def higher(i):
            w = edges(r, i, 1)
            op("v", ["sk0", "sk1", w[0], "ga%d" % i], ["bit%d" % i], lambda: V.tensor_tensor(
                T.bit[:, i:C:2], pick("sk", lst(*w)), T.ga[:, HC * i:HC * i + HC], A.is_gt))

        def straight(q, c):
            a, e = HC * c, HC * c + HC
            out, in_ = T.nx[:, 16 + a:16 + e], pick("ro", lst(*heads(r, a // 16, e // 16)), PAD, 2 * C)
            if q == "s":
                op("s", ["ro", hvs, "low", "nlow"], each("nx%d", c), lambda: S.activation(out, in_, AF.Square, bias=T.nlow[:], scale=T.low[:]))
            else:
                op("v", ["ro", hvs, "low"], each("nx%d", c), lambda: V.tensor_scalar(out, in_, 1.0, T.low[:], A.not_equal, A.mult))

        def new_out():
            for h in (0, 1):
                w = edges(r, 0, h)
                op("s", ["fi", w[0]], ["pr%d%d" % ((r - 1) % 2, h)], lambda: S.activation(
                    T.pr[:, (r - 1) % 2 + 2 * h:2 * C:4], pick("fi", lst(*w)), AF.Copy))

        def at_heads(n):
            w = heads(n)
            op("s", ["ro", w[0]], ["nc"], lambda: S.activation(T.nx[:, C + 32:2 * C + 32], pick("ro", lst(*w), PAD, 2 * C), AF.Copy))

        def cand(n, i):
            a = ((0, 1, 3) if n % 2 else (3, 2, 0))[i]
            return T.tc[:, a:a + 16 * NQ:16]

        def yadd(b):
            op("v", ["xp%d" % b, to % (0, b), to % (1, b), m1], ["y%d" % b], lambda: V.tensor_tensor(
                T.y32[:, C * b:C * b + C], pick("xp", lst(m1), C * b), T[xo][:, b:1280:4], A.add))

        def zpick(q, c, b):
            a, e = span(c)
            out, in_ = T.zt[:, 4 * a + b:4 * e:4], pick("y32", lst(m0, a // 16, e // 16), C * b)
            if q == "s":
                op("s", ["y%d" % b, m0], each("z%%d%d" % b, c), lambda: S.activation(out, in_, AF.Copy, scale=0.5))
            else:
                op("v", ["y%d" % b, m0], each("z%%d%d" % b, c), lambda: V.tensor_scalar(out, in_, 0.5, None, A.mult))

        def halves(q, name, c, m):
            a, e = span(c)
            out, in_ = T[name][:, a:e], pick("xp", lst(m, a // 16, e // 16), 3 * C)
            if q == "s":
                op("s", ["xp3", m], each(name + "%d", c), lambda: S.activation(out, in_, AF.Copy, scale=0.5))
            else:
                op("v", ["xp3", m], each(name + "%d", c), lambda: V.tensor_scalar(out, in_, 0.5, None, A.mult))

        def zadd(c):
            a, e = span(c)
            op("v", ["x1h0", "x1h1", "x0h%d" % c, m0], ["z%d3" % c], lambda: V.tensor_tensor(
                T.zt[:, 4 * a + 3:4 * e:4], pick("x1h", lst(m0, a // 16, e // 16)), T.x0h[:, a:e], A.add))

        def choose(k):
            op("v", ["tt0", "tt1", "kd", "k1"], ["ms%d" % k], lambda: V.tensor_tensor_scan(
                T.ms[:, 112 * k:112 * k + NP], T.tt[:, k:k + 8 * NP:8], T.kk[:, 1:1 + NP], T.kk[:, 0:1], A.mult, A.add))

        def chosen(k):
            m = (m0, m1)[k]
            ts(m, "ms", float(HC), None, A.add, to=(lst(m, 0, 32), pick("ms", T.tom[:], 112 * k, 112)), rd=["ms%d" % k, "tom"])

        def layer(c):
            quantise("qz", "sz", "zt", c, [t for b in range(4) for t in each("z%%d%d" % b, c)])
            for b in range(4):
                product(4 * (c % 2) + b, ("qw", "sw"), b, ("qz", "sz"), c, each("qz.%d", c) + ["qw"])

        def send(out, in_, sem):
            g.remote_dma(out, in_, T.sem[sem], T.sem.lsem, pid, rid, mask)
            cnt["lsem"] = cnt.get("lsem", 0) + neng

        def send_h(c):
            quantise(qh, sh, "ht", c, ["h%d%d" % (c, b) for b in range(4)])
            order("g", ["%s.%d" % (qh, c)], [])
            a, e = span(c)
            send(T[lc][:, a:e].bitcast(dt.uint8), T[qh][:, a:e].bitcast(dt.uint8), "a%dc%d" % (r, c))
            send(T[ls][:, a:e], T[sh][:, a:e], "a%dc%d" % (r, c))

        def send_f():
            wrapped(fw, "scf")
            order("g", [fw], [])
            send(T[fp][:], T[fw][:], "a%df" % r)

        def send_m():
            order("g", [m0, m1], [])
            send(T["mp%d" % r][:], T["mw%d" % r][:, 0:52], "a%df" % r)
            wrote["mp%d" % r] = wrote[fp]

        def behind(name, row, k):
            spick(name, row, "mp%d" % r, 32 * k, 32 * k + 20)

        def unpack(c, *planes):
            for b in planes or range(4):
                product(4 * (c % 2) + b, ("qe", "se"), b, (lc, ls), c, each("ld%d", c) + ["qe%d" % b])

        def meet(c, b):
            (a, e), (k, n) = span(c), runs(c)
            cols = slice(4 * a + b, 4 * e, 4)
            op("v", ["d0%d" % b, "d1%d" % b, "lw"] + [to % (k + i, b) for i in range(n)],
               [tn % (k + i, b) for i in range(n)] + ["%s.%d%d" % (xn, k + i, b) for i in range(n)],
               lambda: V.tensor_tensor(T[xn][:, cols], pick("dd", lst("lw", a // 16, e // 16), C * b), T[xo][:, cols], A.add))

        def ones(b):
            op("v", ["et"], ["qe%d" % b], lambda: V.quantize_mx(
                T.qe[:, 128 * b:128 * b + 128], T.se[:, 128 * b:128 * b + 128], T.et[:, 3 - b:515 - b]))

        def store_scales():
            for k in range(4):
                dma("y", "oq", T.osc[4 * k:4 * k + 4, :], T.so[32 * k:32 * k + 4, :], rd=["qo.0", "qo.1"], total=96)

        def store_codes(c):
            a, e = span(c)
            dma("y", "oq", T.oc[:, 4 * a:4 * e], T.qo[:, a:e].bitcast(dt.uint8), rd=each("qo.%d", c), total=96)

        four = ["pr00", "pr01", "pr10", "pr11"]
        nxt = [r]
        steps = {
            "enc": places, "hv": lambda: ts("hv", "hlt", 1, None, A.arith_shift_right),
            "heads": lambda: ts("hvs", "hv", 4.0, 3.0, A.mult, A.add),
            "cut": recut, "os": store_scales, **later,
            "scat": lambda: op("v", ["enc0", "enc1", "pay0", "pay1"], four, lambda: V.tensor_copy(T.pr[:].indirect(T.enc[:]), T.pay[:])),
            "fi": lambda: op("v", [fp, "pay0", "pay1"], ["fi"], lambda: V.tensor_copy(T.fi[:].indirect(lst(fp)), T.pay[:, C * (r - 1):C * r])),
            "pr": new_out,
            "mn": lambda: op("v", four + ["rst"], ["ro"], lambda: V.tensor_tensor_scan(T.ro[:, PAD:PAD + 2 * C], T.rst[:], T.pr[:], 0.0, A.max, A.min)),
            "ta": lambda: turn("tv", ["ro"], HC, T.ro[:, PAD + 3:PAD + 2 * C:4], T.ro[:, 3:2 * C + 2 * PAD:4]),
            "wrap": lambda: wrap_edges(nxt[0]), "cp": lambda: at_heads(nxt[0]),
            "tc": lambda: turn("tc", ["nc"], C, T.nx[:, C + 32:2 * C + 32], T.nx[:, C + 16:2 * C + 48]),
            "rho": lambda: small("rho", T.rho[:], cand(nxt[0], 2), T.ciw[:, 0:NQ], A.not_equal, ["tc0", "tc1", "ciw"]),
            "nd": lambda: small("nd", T.nd[:], cand(nxt[0], 0), cand(nxt[0], 1), A.add, ["tc0", "tc1"]),
            "g2": lambda: affine("g2", "rho", -2.0, 1.0), "g2v": lambda: ts("g2", "rho", -2.0, 1.0, A.mult, A.add),
            "kq": lambda: small("kq", T.kq[:], T.rho[:], T.nd[:], A.mult, ["rho", "nd"]),
            "k1": lambda: small("k1", k1, T.kq[:], cand(nxt[0], 1), A.subtract, ["kq", "tc0", "tc1"]),
            "kd": lambda: small("kd", kd, T.g2[:], T.nd[:], A.mult, ["g2", "nd"]),
            "qu": lambda: op("v", ["ut"], ["qu"], lambda: V.quantize_mx(T.qu[:], T.su[:], T.ut[:])),
            "qv": lambda: op("v", ["vt"], ["qv"], lambda: V.quantize_mx(T.qv[:], T.sv[:], T.vt[:])),
            "mm": lambda: [product(c, ("qu", "su"), 0, ("qx", "sx"), c, ["qx.%d" % c, "qu"]) for c in (0, 1)],
            "pg": lambda: [plane(b) for b in range(4)],
            "li": lambda: lower(0), "lo": lambda: lower(1), "hi": lambda: higher(0), "ho": lambda: higher(1),
            "sum": lambda: op("v", ["bit0", "bit1", "alt"], ["ro"], lambda: V.tensor_tensor_scan(
                T.ro[:, PAD + 1:PAD + 2 * C:2], T.alt[:], T.bit[:], 0.0, A.mult, A.add)),
            "nxs": lambda: straight("s", 0), "nxv": lambda: straight("v", 1),
            "turn": lambda: turn("tt", ["nx0", "nx1"], C, T.nx[:, 16:16 + C], T.nx[:, 0:C + 32]),
            "g0": lambda: choose(0), "g1": lambda: choose(1), "m0": lambda: chosen(0), "m1": lambda: chosen(1),
            "m1r": lambda: spick("m1r", "cio", m1), "fr": lambda: spick("fr", "m1r", m0),
            "FS": lambda: scan("scf", "fr"), "F": send_f,
            "m1v": lambda: op("v", ["cio", m1], ["m1r"], lambda: V.tensor_copy(T.m1r[:], pick("cio", lst(m1)))),
            "frv": lambda: op("v", ["m1r", m0], ["fr"], lambda: V.tensor_copy(T.fr[:], pick("m1r", lst(m0)))),
            "x1": lambda: halves("s", "x1h", 2, m1), "Z0": lambda: zadd(0), "Z1": lambda: zadd(1),
            "M": send_m, "lm1": lambda: behind("m1r", "fr", 1), "lm0": lambda: behind("lr", "m1r", 0),
            "tm1": lambda: behind("raw0", "raw2", 1),
            "tm0": lambda: [behind("tpr", "raw0", 0), dma("y", "ot", T.tp[:], T.tpr[0:128:16, :], rd=["tpr"])],
            "lr": lambda: spick("lr", "fr", fp), "ls": lambda: scan("scl", "lr"), "lw": lambda: wrapped("lw", "scl"),
            "hu": lambda: op("v", ["hlt"], ["hu"], lambda: V.tensor_copy(T.hu[:], T.hlt[:, 0:20])),
            "hvr": lambda: spick("hvr", "half", "hu"), "tr": lambda: spick("tr", "hvr", "fp1"),
            "hs": lambda: scan("sch", "tr"),
            "hw": lambda: ts("hvs2", "sch", "sub4", 4.0, A.subtract, A.mult, to=(T.hvs2[:], T.sch[:, 15:C:16])),
            "raw": lambda: [spick("raw0", "cio", "hu", bias=float(HC)), spick("raw2", "raw0", "fp1")],
            "TP": lambda: [spick("tpr", "raw2", fp), dma("y", "ot", T.tp[:], T.tpr[0:128:16, :], rd=["tpr"])],
        }
        for n in range(4):
            steps.update({"qe%d" % n: lambda n=n: ones(n), "y%d" % n: lambda n=n: yadd(n), "a%d" % n: lambda n=n: meet(2, n)})
        for c in (0, 1):
            steps.update({
                "q%d" % c: lambda c=c: quantise("qx", "sx", xo, c, [to % (c, b) for b in range(4)]),
                "o%d" % c: lambda c=c: quantise("qo", "so", xn, c, [tn % (c, b) for b in range(4)]),
                "l%d" % c: lambda c=c: layer(c), "send%d" % c: lambda c=c: send_h(c),
                "u%d" % c: lambda c=c: unpack(c), "oc%d" % c: lambda c=c: store_codes(c),
                "ym%d" % c: lambda c=c: product(c, ("qv", "sv"), 0, ("qo", "so"), c, ["qo.%d" % c, "qv"]),
                "oy%d" % c: lambda c=c: dma("s", "oy", T.y[:, slice(*span(c))], T.yo[:, slice(*span(c))], rd=["yo%d" % c], total=32),
            })
            for b in range(4):
                steps["a%d%d" % (c, b)] = lambda c=c, b=b: meet(c, b)
                steps["u%d%d" % (c, b)] = lambda c=c, b=b: unpack(c, b)
        for part in "abc":
            nxt[0] = r + (part == "c")
            for c in (0, 1, 2):
                a, e = span(c)
                for q in "sv":
                    steps["p%s%d" % (q, c)] = lambda q=q, c=c: halves(q, "x0h", c, m0)
                    res = "yo" if part == "c" else "sk"
                    steps["e%s%d" % (q, c)] = lambda q=q, c=c, res=res: evac(
                        q, T[res][:, slice(*span(c))], c % 2, each(res + "%d", c), span(c)[1] - span(c)[0])
                    for b in range(4):
                        steps["z%s%d%d" % (q, c, b)] = lambda q=q, c=c, b=b: zpick(q, c, b)
                        steps["h%s%d%d" % (q, c, b)] = lambda q=q, c=c, a=a, e=e, b=b: evac(
                            q, T.ht[:, 4 * a + b:4 * e:4], 4 * (c % 2) + b, each("h%%d%d" % b, c), e - a, 0.03125)
                        steps["d%s%d%d" % (q, c, b)] = lambda q=q, c=c, a=a, e=e, b=b: evac(
                            q, T.dd[:, C * b + a:C * b + e], 4 * (c % 2) + b, each("d%%d%d" % b, c), e - a)
            for w in ORDER["%s%d" % (part, r)].split():
                steps[w]()
    for sem in sorted(cnt):
        need("g", sem, cnt[sem])
